import numpy as np
import ml_dtypes


def mxq(x, axis, fmt="e4m3"):
    dtype, down = {"e4m3": (ml_dtypes.float8_e4m3fn, 7), "e5m2": (ml_dtypes.float8_e5m2, 14)}[fmt]
    v = np.moveaxis(np.asarray(x, np.float32).astype(ml_dtypes.bfloat16).astype(np.float64), axis, -1)
    blocks = v.reshape(v.shape[:-1] + (-1, 32))
    amax = np.abs(blocks).max(-1, keepdims=True)
    byte = np.maximum(np.where(amax > 0, np.frexp(amax)[1] - 1 + 127, 0) - down, 1)
    scale = np.exp2(byte - 127.0)
    codes = (blocks / scale).astype(np.float32).astype(dtype).astype(np.float64)
    return np.moveaxis((codes * scale).reshape(v.shape), -1, axis)


WIDE = False


def mx_kscale(k):
    if not WIDE:
        return np.ones(k)
    levels = np.array([10, -10, 5, -5, 0])
    if k % 512:
        return np.exp2(np.random.permutation(np.resize(levels, k // 32))).repeat(32)
    a = np.empty((k // 512, 16))
    for p in range(k // 512):
        a[p, :8] = np.random.permutation(np.resize(levels, 8))
        for g in range(8):
            far = levels[np.abs(levels - a[p, g]) >= 10]
            a[p, g + 8] = far[np.random.randint(len(far))]
    return np.exp2(a.ravel()).repeat(32)


def f64(x):
    return np.asarray(x).astype(np.float64)


def striped(idx):
    return np.tile(idx.reshape(-1, 16).T, (8, 1)).astype(np.uint16)


def unstriped(offs):
    return offs[:16].T.reshape(-1).astype(np.int64)


def striped8(idx):
    return np.concatenate([x.reshape(-1, 16).T for x in idx]).astype(np.uint16)


def runs(offs, k):
    lists = np.stack([offs[16 * r : 16 * r + 16].T.reshape(-1) for r in range(8)]).astype(np.int64)
    return lists[np.arange(k) % 512 // 64]


def pack_weight(w):
    k, n = w.shape
    w = f64(np.asarray(w, np.float32).astype(ml_dtypes.bfloat16)).reshape(k // 32, 32, n)
    amax = np.abs(w).max(1)
    byte = np.clip(np.where(amax > 0, np.frexp(amax)[1] - 1 + 127 - 7, 1), 1, 254)
    scaled = (w * np.exp2(127.0 - byte)[:, None, :]).reshape(k, n).astype(np.float32)
    words = np.ascontiguousarray(scaled.reshape(k // 512, 128, 4, n).transpose(0, 1, 3, 2)).astype(ml_dtypes.float8_e4m3fn).view(np.uint8)
    return words, np.ascontiguousarray(byte.astype(np.uint8).reshape(k // 512, 16, n))


def unpack_weight(words, scales):
    g, p, n, _ = words.shape
    vals = np.ascontiguousarray(words).view(ml_dtypes.float8_e4m3fn).astype(np.float64) * np.repeat(np.exp2(scales.astype(np.float64) - 127.0), 8, axis=1)[..., None]
    return vals.transpose(0, 1, 3, 2).reshape(g * 512, n)


E2M1 = np.array([0.0, 0.5, 1.0, 1.5, 2.0, 3.0, 4.0, 6.0, -0.0, -0.5, -1.0, -1.5, -2.0, -3.0, -4.0, -6.0])


def pack_fp4(w):
    k, n = w.shape
    w = f64(np.asarray(w, np.float32).astype(ml_dtypes.bfloat16)).reshape(k // 32, 32, n)
    amax = np.abs(w).max(1)
    mant, ex = np.frexp(amax / 6.0)
    byte = np.clip(np.where(amax > 0, np.where(mant > 0.5, ex, ex - 1) + 127, 1), 1, 254)
    scaled = (w * np.exp2(127.0 - byte)[:, None, :]).reshape(k, n).astype(np.float32)
    c = np.ascontiguousarray(scaled.reshape(k // 512, 128, 4, n).transpose(0, 1, 3, 2)).astype(ml_dtypes.float4_e2m1fn).view(np.uint8) & 0xF
    words = (c[..., 0::2] | (c[..., 1::2] << 4)).reshape(k // 512, 128, 2 * n)
    return np.ascontiguousarray(words), np.ascontiguousarray(byte.astype(np.uint8).reshape(k // 512, 16, n))


def unpack_fp4(words, scales):
    g, _, n = scales.shape
    words = np.ascontiguousarray(words).reshape(g, 128, n, 2)
    nib = np.empty((g, 128, n, 4), np.uint8)
    nib[..., 0::2] = words & 0xF
    nib[..., 1::2] = words >> 4
    vals = E2M1[nib] * np.repeat(np.exp2(scales.astype(np.float64) - 127.0), 8, axis=1)[..., None]
    return vals.transpose(0, 1, 3, 2).reshape(g * 512, n)


def planes(y):
    n, m = y.shape
    v = y.astype(np.float32).astype(ml_dtypes.bfloat16).astype(np.float64).reshape(n // 32, 32, m)
    top = np.abs(v).max(1)
    byte = np.clip(np.where(top > 0, np.frexp(top)[1] - 1 + 127 - 7, 1), 1, 254)
    codes = (v * np.exp2(127.0 - byte)[:, None, :]).reshape(n, m).astype(np.float32).astype(ml_dtypes.float8_e4m3fn).view(np.uint8)
    words = codes.reshape(n // 512, 128, 4, m).transpose(0, 1, 3, 2)
    return np.ascontiguousarray(words), np.ascontiguousarray(byte.astype(np.uint8).reshape(n // 512, 16, m))


K, T, S, N, H = 512, 2048, 512, 512, 512


def setup_inputs():
    n = np.random.standard_normal
    s = mx_kscale(K)[:, None]
    u = mx_kscale(H)
    packed_xT = pack_weight(n((K, T)) * s)
    packed_w3 = pack_fp4(n((H, N)) / np.sqrt(2 * H) / u[:, None])
    packed_w4 = pack_fp4(n((H, N)) / np.sqrt(2 * H) / u[:, None])
    return {
        "x_words": packed_xT[0],
        "x_scales": packed_xT[1],
        "w1": (n((K, H)) / np.sqrt(K) / s * u).astype(np.float32),
        "w2": (n((K, H)) / np.sqrt(K) / s * u).astype(np.float32),
        "wr1": np.random.uniform(-1.0, 1.0, (H, 1)).astype(np.float32),
        "wi1": np.random.uniform(-1.0, 1.0, (H, 1)).astype(np.float32),
        "wr2": np.random.uniform(-1.0, 1.0, (H, 1)).astype(np.float32),
        "wi2": np.random.uniform(-1.0, 1.0, (H, 1)).astype(np.float32),
        "w3_words": packed_w3[0],
        "w3_scales": packed_w3[1],
        "w4_words": packed_w4[0],
        "w4_scales": packed_w4[1],
        "offs": striped(np.random.permutation(T)[:S]),
        "m1": striped8(np.stack([np.random.permutation(S) for _ in range(8)])),
        "m2": striped8(np.stack([np.random.permutation(S) for _ in range(8)])),
    }


def reference(x_words, x_scales, w1, w2, wr1, wi1, wr2, wi2, w3_words, w3_scales, w4_words, w4_scales, offs, m1, m2):
    xq = unpack_weight(x_words, x_scales)[:, unstriped(offs)]
    re = mxq(f64(w1), 0, "e4m3").T @ xq
    a1 = re[np.arange(H)[:, None], runs(m1, H)]
    im = mxq(f64(w2), 0, "e4m3").T @ xq
    b1 = im[np.arange(H)[:, None], runs(m1, H)]
    a2 = re[np.arange(H)[:, None], runs(m2, H)]
    b2 = im[np.arange(H)[:, None], runs(m2, H)]
    z = f64(wr1) * a1 - (f64(wi1) * b1) + f64(wr2) * a2 - (f64(wi2) * b2)
    z2 = f64(wr1) * b1 + f64(wi1) * a1 + f64(wr2) * b2 + f64(wi2) * a2
    out_0 = unpack_fp4(w3_words, w3_scales).T @ mxq(z, 0, "e4m3") + unpack_fp4(w4_words, w4_scales).T @ mxq(z2, 0, "e4m3")
    return (out_0,) + planes(out_0)

@@ -1,0 +1,252 @@
+from contextlib import ExitStack
+
+import concourse.mybir as mybir
+from concourse.masks import make_identity
+
+K, T, S, N, H = 512, 2048, 512, 512, 512
+FLOPS = 4 * 2 * 512 * 512 * 512
+
+F32 = mybir.dt.float32
+BF16 = mybir.dt.bfloat16
+I32 = mybir.dt.int32
+U32 = mybir.dt.uint32
+U16 = mybir.dt.uint16
+U8 = mybir.dt.uint8
+FP8X4 = mybir.dt.float8_e4m3fn_x4
+FP4X4 = mybir.dt.float4_e2m1fn_x4
+MULT = mybir.AluOpType.mult
+COPY = mybir.ActivationFunctionType.Copy
+
+P = 128
+PACK = 4
+CH = 128
+PHASES = (
+    (0, 256, ("a1", "a2"), ("vv", "vv")),
+    (0, 256, ("b1", "b2"), ("ss", "ss")),
+    (256, 256, ("a1", "a2"), ("vv", "vs")),
+    (256, 128, ("b1", "b2"), ("vs", "vs")),
+    (384, 128, ("b1", "b2"), ("vv", "vv")),
+)
+RING = 6
+TERMS = 16
+
+
+def tile_picked_beamf_none_po_kernel(
+    tc, x_words, x_scales, w1, w2, wr1, wi1, wr2, wi2, w3_words, w3_scales, w4_words, w4_scales,
+    offs, m1, m2, out_0, out_1, out_2,
+):
+    nc = tc.nc
+    with ExitStack() as ctx:
+        keep = ctx.enter_context(tc.tile_pool(name="keep", bufs=1))
+        ring = ctx.enter_context(tc.tile_pool(name="ring", bufs=RING))
+        terms = ctx.enter_context(tc.tile_pool(name="terms", bufs=TERMS))
+        acc = ctx.enter_context(tc.psum_pool(name="acc", bufs=4))
+        work = ctx.enter_context(tc.psum_pool(name="work", bufs=4))
+
+        def held(shape, dtype, name):
+            return keep.tile(shape, dtype, name=name, align_bytes=64)
+
+        offs_t = keep.tile([P, S // 16], U16, name="offs_t")
+        m1_t = keep.tile([P, S // 16], U16, name="m1_t")
+        m2_t = keep.tile([P, S // 16], U16, name="m2_t")
+        xw = held([P, T], I32, "xw")
+        xs = held([P, T], U8, "xs")
+        w34w = [held([P, 2 * N], U8, "w3w"), held([P, 2 * N], U8, "w4w")]
+        w34s = held([P, 2 * N], U8, "w34s")
+        raw = [[held([P, PACK, H // 2], F32, "raw%d%d" % (i, h)) for h in range(2)] for i in range(2)]
+        wt = {}
+        for name in ("wr1", "wi1", "wr2", "wi2", "nwi1", "nwi2"):
+            wt[name] = held([P, PACK], F32, name)
+
+        nc.vector.memset(xs[:].bitcast(I32), 0)
+        nc.vector.memset(w34s[:].bitcast(I32), 0)
+        ident = held([P, P], F32, "ident")
+
+        nc.sync.dma_start(offs_t[:], offs)
+        for q in range(4):
+            nc.scalar.dma_start(xs[32 * q : 32 * q + 4, :].bitcast(I32), x_scales[0, 4 * q : 4 * q + 4, :].bitcast(I32))
+        nc.sync.dma_start(w34w[0][:].bitcast(I32), w3_words[0].bitcast(I32))
+        nc.sync.dma_start(w34w[1][:].bitcast(I32), w4_words[0].bitcast(I32))
+        nc.sync.dma_start(xw[:], x_words[0].rearrange("p c r -> p (c r)").bitcast(I32))
+        w_rows = [w.rearrange("(p j) c -> p j c", j=PACK) for w in (w1, w2)]
+        for h in range(2):
+            nc.sync.dma_start(raw[0][h][:], w_rows[0][:, :, 256 * h : 256 * h + 256])
+        nc.sync.dma_start(m1_t[:], m1)
+        nc.sync.dma_start(m2_t[:], m2)
+        for h in range(2):
+            nc.sync.dma_start(raw[1][h][:], w_rows[1][:, :, 256 * h : 256 * h + 256])
+        for name, src in (("wr1", wr1), ("wi1", wi1), ("wr2", wr2), ("wi2", wi2)):
+            nc.gpsimd.dma_start(wt[name][:], src.rearrange("(p t) o -> p (t o)", t=PACK))
+        make_identity(nc, ident[:])
+        for i, src in enumerate((w3_scales, w4_scales)):
+            for q in range(4):
+                nc.sync.dma_start(
+                    w34s[32 * q : 32 * q + 4, i * N : (i + 1) * N].bitcast(I32), src[0, 4 * q : 4 * q + 4, :].bitcast(I32)
+                )
+        nc.scalar.activation(wt["nwi1"][:], wt["wi1"][:], COPY, scale=-1.0)
+        nc.scalar.activation(wt["nwi2"][:], wt["wi2"][:], COPY, scale=-1.0)
+
+        w34d = [held([P, 2 * N], U8, "w3d"), held([P, 2 * N], U8, "w4d")]
+        for i in range(2):
+            nc.vector.tensor_copy(
+                w34d[i][:].rearrange("p (t m e) -> p m t e", t=PACK, e=2),
+                w34w[i][:].rearrange("p (m t e) -> p m t e", t=PACK, e=2),
+            )
+
+        xgw = held([P, S], U32, "xgw")
+        xgs = held([P, S], U8, "xgs")
+        nc.vector.tensor_copy(xgs[:], xs[:].indirect(offs_t[:]))
+        nc.vector.tensor_copy(xgw[:], xw[:].bitcast(U32).indirect(offs_t[:]))
+
+        grouped = [held([P, PACK * H], BF16, "grouped%d" % i) for i in range(2)]
+        wc = [held([P, H], U32, "wc%d" % i) for i in range(2)]
+        wsc = [held([P, H], U8, "wsc%d" % i) for i in range(2)]
+        win = [[held([P, S], F32, "win%d%d" % (i, t)) for t in range(PACK)] for i in range(2)]
+
+        def regroup(i, h, eng):
+            dst = grouped[i][:].rearrange("p (t m j) -> p m j t", t=PACK, j=PACK)[:, 64 * h : 64 * h + 64]
+            src = raw[i][h][:].rearrange("p j (m t) -> p m j t", t=PACK)
+            if eng == "v":
+                nc.vector.tensor_copy(dst, src)
+            else:
+                nc.scalar.copy(dst, src)
+
+        def project(i, t):
+            cols = slice(t * P, (t + 1) * P)
+            nc.vector.quantize_mx(out=wc[i][:, cols].bitcast(FP8X4), scales=wsc[i][:, cols], in_=grouped[i][:, t * 512 : (t + 1) * 512])
+            bank = work.tile([P, S], F32, name="bank")
+            nc.tensor.matmul_mx(
+                out=bank[:], lhsT=wc[i][:, cols].bitcast(FP8X4), lhsT_scale=wsc[i][:, cols],
+                rhs=xgw[:].bitcast(FP8X4), rhs_scale=xgs[:], start=True, stop=True,
+            )
+            nc.scalar.copy(win[i][t][:], bank[:])
+
+        regroup(0, 0, "v")
+        regroup(0, 1, "v")
+        for t in range(PACK):
+            project(0, t)
+        regroup(1, 0, "s")
+        regroup(1, 1, "s")
+
+        w34sd = held([P, 2 * N], U8, "w34sd")
+        oc = held([P, S], U32, "oc")
+        osc = held([P, S], U8, "osc")
+        out_rows = out_0.rearrange("(p t) j -> p t j", t=PACK)
+        out_words = out_1[0].rearrange("p c r -> p (c r)").bitcast(I32)
+
+        def deal_scales():
+            nc.vector.tensor_copy(
+                w34sd[:].rearrange("p (w t m) -> p w m t", w=2, t=PACK),
+                w34s[:].rearrange("p (w m t) -> p w m t", w=2, t=PACK),
+            )
+
+        SRC = {
+            "a1": (0, m1_t, "wr1", "wi1"), "a2": (0, m2_t, "wr2", "wi2"),
+            "b1": (1, m1_t, "nwi1", "wr1"), "b2": (1, m2_t, "nwi2", "wr2"),
+        }
+        banks = {}
+        count = {}
+        picked = {}
+
+        def gather(g, t, s):
+            j0, n = PHASES[g][0], PHASES[g][1]
+            i, lst = SRC[s][0], SRC[s][1]
+            tile = ring.tile([P, 256], F32, name="picked")
+            nc.vector.tensor_copy(tile[:, 0:n], win[i][t][:].indirect(lst[:, j0 // 16 : (j0 + n) // 16]))
+            picked[(g, t, s)] = tile
+
+        def weigh(g, t, s):
+            j0, n = PHASES[g][0], PHASES[g][1]
+            engines = PHASES[g][3][PHASES[g][2].index(s)]
+            tile = picked[(g, t, s)]
+            for z in range(2):
+                w = wt[SRC[s][2 + z]][:, t : t + 1]
+                term = terms.tile([P, 256], F32, name="term")
+                if engines[z] == "v":
+                    nc.vector.tensor_scalar(term[:, 0:n], tile[:, 0:n], w, None, MULT)
+                else:
+                    nc.scalar.activation(term[:, 0:n], tile[:, 0:n], COPY, scale=w)
+                for c in range(j0 // CH, (j0 + n) // CH):
+                    if (c, z) not in banks:
+                        banks[(c, z)] = acc.tile([P, H], F32, name="acc")
+                        count[(c, z)] = 0
+                    k = count[(c, z)]
+                    nc.tensor.matmul(
+                        banks[(c, z)][:, t * P : (t + 1) * P], lhsT=term[:, c * CH - j0 : (c + 1) * CH - j0], rhs=ident[:],
+                        is_transpose=True, start=(k == 0), stop=(k == 15),
+                    )
+                    count[(c, z)] = k + 1
+
+        st = {}
+
+        def stage(c, k):
+            if k == 0:
+                zb = held([P, 2 * H], BF16, "zb%d" % c)
+                for z in range(2):
+                    move = nc.vector.tensor_copy if (c == 3 and z == 0) else nc.scalar.copy
+                    move(
+                        zb[:, z * H : (z + 1) * H].rearrange("j (u p e) -> j u p e", u=2, e=2),
+                        banks[(c, z)][:].rearrange("j (u e p) -> j u p e", u=2, e=2),
+                    )
+                st[(c, "zb")] = zb
+            elif k == 1:
+                words = st[(c, "zb")][:].bitcast(F32)
+                bank = work.tile([P, 512], F32, name="bank")
+                for b in range(4):
+                    nc.tensor.transpose(bank[:, b * P : (b + 1) * P], words[:, b * P : (b + 1) * P], ident[:])
+                zq = held([P, 2 * H], BF16, "zq%d" % c)
+                nc.scalar.copy(
+                    zq[:].bitcast(F32).rearrange("p (z j u) -> p z j u", z=2, u=2),
+                    bank[:].rearrange("p (z u j) -> p z j u", z=2, u=2),
+                )
+                st[(c, "zq")] = zq
+            elif k == 2:
+                zc = held([P, 2 * CH], U32, "zc%d" % c)
+                zs = held([P, 2 * CH], U8, "zs%d" % c)
+                nc.vector.quantize_mx(out=zc[:].bitcast(FP8X4), scales=zs[:], in_=st[(c, "zq")][:])
+                bank = work.tile([P, 512], F32, name="bank")
+                for t in range(PACK):
+                    for z in range(2):
+                        nc.tensor.matmul_mx(
+                            out=bank[:, t * CH : (t + 1) * CH],
+                            lhsT=w34d[z][:, 2 * P * t : 2 * P * (t + 1)].bitcast(FP4X4),
+                            lhsT_scale=w34sd[:, z * N + t * P : z * N + (t + 1) * P],
+                            rhs=zc[:, z * CH : (z + 1) * CH].bitcast(FP8X4), rhs_scale=zs[:, z * CH : (z + 1) * CH],
+                            start=(z == 0), stop=(z == 1),
+                        )
+                ob = held([P, PACK * CH], BF16, "ob%d" % c)
+                move = nc.vector.tensor_copy if c == 3 else nc.scalar.copy
+                move(ob[:].rearrange("p (j t) -> p j t", t=PACK), bank[:].rearrange("p (t j) -> p j t", t=PACK))
+                of = held([P, PACK * CH], F32, "of%d" % c)
+                nc.scalar.copy(of[:], bank[:])
+                nc.sync.dma_start(out_rows[:, :, c * CH : (c + 1) * CH], of[:].rearrange("p (t j) -> p t j", t=PACK))
+                st[(c, "ob")] = ob
+            else:
+                cols = slice(c * CH, (c + 1) * CH)
+                nc.vector.quantize_mx(out=oc[:, cols].bitcast(FP8X4), scales=osc[:, cols], in_=st[(c, "ob")][:])
+                nc.sync.dma_start(out_words[:, cols], oc[:, cols].bitcast(I32))
+
+        steps = [(g, t, s) for g in range(len(PHASES)) for t in range(PACK) for s in PHASES[g][2]]
+        later = {}
+        for n, step in enumerate(steps):
+            g = step[0]
+            if PHASES[g][2][0] == "b1" and (n + 1 == len(steps) or steps[n + 1][0] != g):
+                j0, w = PHASES[g][0], PHASES[g][1]
+                for r, c in enumerate(range(j0 // CH, (j0 + w) // CH)):
+                    for k in range(4):
+                        later.setdefault(n + 2 + r + 2 * k, []).append((c, k))
+        for n in range(len(steps) + 16):
+            if n < len(steps):
+                gather(*steps[n])
+            if 1 <= n <= len(steps):
+                weigh(*steps[n - 1])
+            if 3 <= n < 3 + PACK:
+                project(1, n - 3)
+            if n == 10:
+                deal_scales()
+            for c, k in later.get(n, []):
+                stage(c, k)
+
+        for q in range(4):
+            eng = nc.sync if q % 2 == 0 else nc.scalar
+            eng.dma_start(out_2[0, 4 * q : 4 * q + 4, :].bitcast(I32), osc[32 * q : 32 * q + 4, :].bitcast(I32))

@@ -15,20 +15,22 @@ U8 = mybir.dt.uint8
 FP8X4 = mybir.dt.float8_e4m3fn_x4
 FP4X4 = mybir.dt.float4_e2m1fn_x4
 MULT = mybir.AluOpType.mult
+ADD = mybir.AluOpType.add
 COPY = mybir.ActivationFunctionType.Copy
 
 P = 128
 PACK = 4
 CH = 128
-PHASES = (
-    (0, 256, ("a1", "a2"), ("vv", "vv")),
-    (0, 256, ("b1", "b2"), ("ss", "ss")),
-    (256, 256, ("a1", "a2"), ("vv", "vs")),
-    (256, 128, ("b1", "b2"), ("vs", "vs")),
-    (384, 128, ("b1", "b2"), ("vv", "vv")),
-)
-RING = 6
-TERMS = 16
+GSHARE = ((6, 0), (6, 1), (7, 0), (7, 1))
+C2 = 3
+C3 = 4
+ORDER = (6, 7, 4, 5)
+T0 = "pick4"
+T1 = "zb00"
+T2 = "term1111"
+S2 = 0
+T3 = "zb11"
+S3 = 0
 
 
 def tile_picked_beamf_none_po_kernel(
@@ -38,10 +40,7 @@ def tile_picked_beamf_none_po_kernel(
     nc = tc.nc
     with ExitStack() as ctx:
         keep = ctx.enter_context(tc.tile_pool(name="keep", bufs=1))
-        ring = ctx.enter_context(tc.tile_pool(name="ring", bufs=RING))
-        terms = ctx.enter_context(tc.tile_pool(name="terms", bufs=TERMS))
-        acc = ctx.enter_context(tc.psum_pool(name="acc", bufs=4))
-        work = ctx.enter_context(tc.psum_pool(name="work", bufs=4))
+        psum = ctx.enter_context(tc.psum_pool(name="psum", bufs=1))
 
         def held(shape, dtype, name):
             return keep.tile(shape, dtype, name=name, align_bytes=64)
@@ -58,15 +57,20 @@ def tile_picked_beamf_none_po_kernel(
         for name in ("wr1", "wi1", "wr2", "wi2", "nwi1", "nwi2"):
             wt[name] = held([P, PACK], F32, name)
 
-        nc.vector.memset(xs[:].bitcast(I32), 0)
+        nc.gpsimd.memset(xs[:].bitcast(I32), 0)
         nc.vector.memset(w34s[:].bitcast(I32), 0)
+        wide = {}
+        for i in range(2):
+            for t in range(2):
+                wide[(i, t)] = held([P, 2 * S], F32, "wide%d%d" % (i, t))
+                nc.vector.memset(wide[(i, t)][:, S : 2 * S], 0.0)
         ident = held([P, P], F32, "ident")
 
         nc.sync.dma_start(offs_t[:], offs)
-        for q in range(4):
-            nc.scalar.dma_start(xs[32 * q : 32 * q + 4, :].bitcast(I32), x_scales[0, 4 * q : 4 * q + 4, :].bitcast(I32))
         nc.sync.dma_start(w34w[0][:].bitcast(I32), w3_words[0].bitcast(I32))
         nc.sync.dma_start(w34w[1][:].bitcast(I32), w4_words[0].bitcast(I32))
+        for q in range(4):
+            nc.sync.dma_start(xs[32 * q : 32 * q + 4, :].bitcast(I32), x_scales[0, 4 * q : 4 * q + 4, :].bitcast(I32))
         nc.sync.dma_start(xw[:], x_words[0].rearrange("p c r -> p (c r)").bitcast(I32))
         w_rows = [w.rearrange("(p j) c -> p j c", j=PACK) for w in (w1, w2)]
         for h in range(2):
@@ -101,7 +105,6 @@ def tile_picked_beamf_none_po_kernel(
         grouped = [held([P, PACK * H], BF16, "grouped%d" % i) for i in range(2)]
         wc = [held([P, H], U32, "wc%d" % i) for i in range(2)]
         wsc = [held([P, H], U8, "wsc%d" % i) for i in range(2)]
-        win = [[held([P, S], F32, "win%d%d" % (i, t)) for t in range(PACK)] for i in range(2)]
 
         def regroup(i, h, eng):
             dst = grouped[i][:].rearrange("p (t m j) -> p m j t", t=PACK, j=PACK)[:, 64 * h : 64 * h + 64]
@@ -111,22 +114,19 @@ def tile_picked_beamf_none_po_kernel(
             else:
                 nc.scalar.copy(dst, src)
 
+        def bank(b):
+            return psum.tile([P, 512], F32, name="bank%d" % b)
+
+        proj = {}
+
         def project(i, t):
             cols = slice(t * P, (t + 1) * P)
             nc.vector.quantize_mx(out=wc[i][:, cols].bitcast(FP8X4), scales=wsc[i][:, cols], in_=grouped[i][:, t * 512 : (t + 1) * 512])
-            bank = work.tile([P, S], F32, name="bank")
+            proj[(i, t)] = bank(4 * i + t)
             nc.tensor.matmul_mx(
-                out=bank[:], lhsT=wc[i][:, cols].bitcast(FP8X4), lhsT_scale=wsc[i][:, cols],
+                out=proj[(i, t)][:], lhsT=wc[i][:, cols].bitcast(FP8X4), lhsT_scale=wsc[i][:, cols],
                 rhs=xgw[:].bitcast(FP8X4), rhs_scale=xgs[:], start=True, stop=True,
             )
-            nc.scalar.copy(win[i][t][:], bank[:])
-
-        regroup(0, 0, "v")
-        regroup(0, 1, "v")
-        for t in range(PACK):
-            project(0, t)
-        regroup(1, 0, "s")
-        regroup(1, 1, "s")
 
         w34sd = held([P, 2 * N], U8, "w34sd")
         oc = held([P, S], U32, "oc")
@@ -135,90 +135,134 @@ def tile_picked_beamf_none_po_kernel(
         out_words = out_1[0].rearrange("p c r -> p (c r)").bitcast(I32)
 
         def deal_scales():
-            nc.vector.tensor_copy(
+            nc.gpsimd.tensor_copy(
                 w34sd[:].rearrange("p (w t m) -> p w m t", w=2, t=PACK),
                 w34s[:].rearrange("p (w m t) -> p w m t", w=2, t=PACK),
             )
 
-        SRC = {
-            "a1": (0, m1_t, "wr1", "wi1"), "a2": (0, m2_t, "wr2", "wi2"),
-            "b1": (1, m1_t, "nwi1", "wr1"), "b2": (1, m2_t, "nwi2", "wr2"),
-        }
+        lists = (m1_t, m2_t)
+        wr = (wt["wr1"], wt["wr2"])
+        wi = (wt["wi1"], wt["wi2"])
+        nwi = (wt["nwi1"], wt["nwi2"])
+        win = {}
+        cross = {}
         banks = {}
         count = {}
+        ACC = {(0, 0): 0, (1, 0): 1, (2, 0): 4, (3, 0): 5, (0, 1): 2, (1, 1): 6, (2, 1): 3, (3, 1): 7}
+
+        def raw_out(i, t):
+            nc.scalar.copy(wide[(i, t)][:, 0:S], proj[(i, t)][:])
+
+        def cross_terms(i, t):
+            for mic in range(2):
+                tile = held([P, S], F32, "cross%d%d%d" % (i, t, mic))
+                w = (wi, nwi)[i][mic][:, t : t + 1]
+                nc.scalar.activation(tile[:], proj[(i, t)][:], COPY, scale=w)
+                cross[(i, t, mic)] = tile
+
+        def combine(t):
+            for z in range(2):
+                for mic in range(2):
+                    tile = held([P, S], F32, "win%d%d%d" % (z, t, mic))
+                    nc.vector.scalar_tensor_tensor(tile[:], proj[(z, t)][:], wr[mic][:, t : t + 1], cross[(1 - z, t, mic)][:], MULT, ADD)
+                    win[(z, t, mic)] = tile
+
+        def add_term(term, t, z, j0, n):
+            u, e = divmod(t, 2)
+            for c in range(j0 // CH, (j0 + n) // CH):
+                if (c, u) not in banks:
+                    banks[(c, u)] = bank(ACC[(c, u)])
+                    count[(c, u)] = 0
+                k = count[(c, u)]
+                nc.tensor.matmul(
+                    banks[(c, u)][:, (2 * z + e) * P : (2 * z + e + 1) * P], lhsT=term[:, c * CH - j0 : (c + 1) * CH - j0], rhs=ident[:],
+                    is_transpose=True, start=(k == 0), stop=(k == (15 if u == 0 else 7)),
+                )
+                count[(c, u)] = k + 1
+
         picked = {}
 
-        def gather(g, t, s):
-            j0, n = PHASES[g][0], PHASES[g][1]
-            i, lst = SRC[s][0], SRC[s][1]
-            tile = ring.tile([P, 256], F32, name="picked")
-            nc.vector.tensor_copy(tile[:, 0:n], win[i][t][:].indirect(lst[:, j0 // 16 : (j0 + n) // 16]))
-            picked[(g, t, s)] = tile
+        def gather_raw(i, t, mic, tile):
+            nc.vector.tensor_copy(tile, wide[(i, t)][:].indirect(lists[mic][:]))
 
-        def weigh(g, t, s):
-            j0, n = PHASES[g][0], PHASES[g][1]
-            engines = PHASES[g][3][PHASES[g][2].index(s)]
-            tile = picked[(g, t, s)]
+        def weigh(k, i, t, mic):
             for z in range(2):
-                w = wt[SRC[s][2 + z]][:, t : t + 1]
-                term = terms.tile([P, 256], F32, name="term")
-                if engines[z] == "v":
-                    nc.vector.tensor_scalar(term[:, 0:n], tile[:, 0:n], w, None, MULT)
+                w = wr[mic] if z == i else (wi, nwi)[i][mic]
+                term = held([P, S], F32, "term%d%d%d%d" % (i, t, mic, z))
+                if (k, z) in GSHARE:
+                    nc.gpsimd.tensor_scalar(term[:], picked[k], w[:, t : t + 1], 0.0, MULT, ADD)
                 else:
-                    nc.scalar.activation(term[:, 0:n], tile[:, 0:n], COPY, scale=w)
-                for c in range(j0 // CH, (j0 + n) // CH):
-                    if (c, z) not in banks:
-                        banks[(c, z)] = acc.tile([P, H], F32, name="acc")
-                        count[(c, z)] = 0
-                    k = count[(c, z)]
-                    nc.tensor.matmul(
-                        banks[(c, z)][:, t * P : (t + 1) * P], lhsT=term[:, c * CH - j0 : (c + 1) * CH - j0], rhs=ident[:],
-                        is_transpose=True, start=(k == 0), stop=(k == 15),
-                    )
-                    count[(c, z)] = k + 1
+                    nc.scalar.activation(term[:], picked[k], COPY, scale=w[:, t : t + 1])
+                add_term(term, t, z, 0, S)
+
+        def gather_chunk(c, tag, tag2=None, split=8):
+            tile = held([P, 8 * CH], F32, tag)
+            k = 0
+            for t in (2, 3):
+                for z in range(2):
+                    for mic in range(2):
+                        if k == split:
+                            tile = held([P, 8 * CH], F32, tag2)
+                        piece = tile[:, k * CH : (k + 1) * CH]
+                        nc.vector.tensor_copy(piece, win[(z, t, mic)][:].indirect(lists[mic][:, 8 * c : 8 * c + 8]))
+                        add_term(piece, t, z, c * CH, CH)
+                        k = k + 1
 
         st = {}
+        both = held([P, 3 * H], BF16, "both")
+
+        def turn_back(c, u):
+            zb = held([P, H], BF16, "zb%d%d" % (c, u))
+            move = nc.vector.tensor_copy if (c == 3 and u == 1) else nc.scalar.copy
+            move(zb[:].rearrange("j (z p e) -> j z p e", z=2, e=2), banks[(c, u)][:].rearrange("j (z e p) -> j z p e", z=2, e=2))
+            words = zb[:].bitcast(F32)
+            if u == 0:
+                first = bank((0, 1, 4, 5)[c])
+                if c == 3:
+                    second = bank(0)
+                    st[(c, "back")] = [first[:, 0:256], second[:, 0:256]]
+                else:
+                    st[(c, "back")] = [first[:, 0:256], first[:, 256:512]]
+                st[(c, "first")] = first
+            for z in range(2):
+                nc.tensor.transpose(st[(c, "back")][z][:, u * P : (u + 1) * P], words[:, z * P : (z + 1) * P], ident[:])
 
         def stage(c, k):
-            if k == 0:
-                zb = held([P, 2 * H], BF16, "zb%d" % c)
-                for z in range(2):
-                    move = nc.vector.tensor_copy if (c == 3 and z == 0) else nc.scalar.copy
-                    move(
-                        zb[:, z * H : (z + 1) * H].rearrange("j (u p e) -> j u p e", u=2, e=2),
-                        banks[(c, z)][:].rearrange("j (u e p) -> j u p e", u=2, e=2),
-                    )
-                st[(c, "zb")] = zb
+            if k == 0 or k == 4:
+                turn_back(c, k // 4)
             elif k == 1:
-                words = st[(c, "zb")][:].bitcast(F32)
-                bank = work.tile([P, 512], F32, name="bank")
-                for b in range(4):
-                    nc.tensor.transpose(bank[:, b * P : (b + 1) * P], words[:, b * P : (b + 1) * P], ident[:])
-                zq = held([P, 2 * H], BF16, "zq%d" % c)
-                nc.scalar.copy(
-                    zq[:].bitcast(F32).rearrange("p (z j u) -> p z j u", z=2, u=2),
-                    bank[:].rearrange("p (z u j) -> p z j u", z=2, u=2),
-                )
+                zq = both[:, 0 : 2 * H] if c == 1 else held([P, 2 * H], BF16, "zq%d" % c)
+                if c == 3:
+                    for z, move in enumerate((nc.vector.tensor_copy, nc.scalar.copy)):
+                        move(
+                            zq[:].bitcast(F32)[:, z * 256 : (z + 1) * 256].rearrange("p (j u) -> p j u", u=2),
+                            st[(c, "back")][z].rearrange("p (u j) -> p j u", u=2),
+                        )
+                else:
+                    nc.scalar.copy(
+                        zq[:].bitcast(F32).rearrange("p (z j u) -> p z j u", z=2, u=2),
+                        st[(c, "first")][:].rearrange("p (z u j) -> p z j u", z=2, u=2),
+                    )
                 st[(c, "zq")] = zq
             elif k == 2:
                 zc = held([P, 2 * CH], U32, "zc%d" % c)
                 zs = held([P, 2 * CH], U8, "zs%d" % c)
                 nc.vector.quantize_mx(out=zc[:].bitcast(FP8X4), scales=zs[:], in_=st[(c, "zq")][:])
-                bank = work.tile([P, 512], F32, name="bank")
+                res = bank((2, 6, 3, 1)[c])
                 for t in range(PACK):
                     for z in range(2):
                         nc.tensor.matmul_mx(
-                            out=bank[:, t * CH : (t + 1) * CH],
+                            out=res[:, t * CH : (t + 1) * CH],
                             lhsT=w34d[z][:, 2 * P * t : 2 * P * (t + 1)].bitcast(FP4X4),
                             lhsT_scale=w34sd[:, z * N + t * P : z * N + (t + 1) * P],
                             rhs=zc[:, z * CH : (z + 1) * CH].bitcast(FP8X4), rhs_scale=zs[:, z * CH : (z + 1) * CH],
                             start=(z == 0), stop=(z == 1),
                         )
-                ob = held([P, PACK * CH], BF16, "ob%d" % c)
+                ob = both[:, 2 * H : 3 * H] if c == 0 else held([P, PACK * CH], BF16, "ob%d" % c)
                 move = nc.vector.tensor_copy if c == 3 else nc.scalar.copy
-                move(ob[:].rearrange("p (j t) -> p j t", t=PACK), bank[:].rearrange("p (t j) -> p j t", t=PACK))
+                move(ob[:].rearrange("p (j t) -> p j t", t=PACK), res[:].rearrange("p (t j) -> p j t", t=PACK))
                 of = held([P, PACK * CH], F32, "of%d" % c)
-                nc.scalar.copy(of[:], bank[:])
+                nc.scalar.copy(of[:], res[:])
                 nc.sync.dma_start(out_rows[:, :, c * CH : (c + 1) * CH], of[:].rearrange("p (t j) -> p t j", t=PACK))
                 st[(c, "ob")] = ob
             else:
@@ -226,26 +270,68 @@ def tile_picked_beamf_none_po_kernel(
                 nc.vector.quantize_mx(out=oc[:, cols].bitcast(FP8X4), scales=osc[:, cols], in_=st[(c, "ob")][:])
                 nc.sync.dma_start(out_words[:, cols], oc[:, cols].bitcast(I32))
 
-        steps = [(g, t, s) for g in range(len(PHASES)) for t in range(PACK) for s in PHASES[g][2]]
-        later = {}
-        for n, step in enumerate(steps):
-            g = step[0]
-            if PHASES[g][2][0] == "b1" and (n + 1 == len(steps) or steps[n + 1][0] != g):
-                j0, w = PHASES[g][0], PHASES[g][1]
-                for r, c in enumerate(range(j0 // CH, (j0 + w) // CH)):
-                    for k in range(4):
-                        later.setdefault(n + 2 + r + 2 * k, []).append((c, k))
-        for n in range(len(steps) + 16):
-            if n < len(steps):
-                gather(*steps[n])
-            if 1 <= n <= len(steps):
-                weigh(*steps[n - 1])
-            if 3 <= n < 3 + PACK:
-                project(1, n - 3)
-            if n == 10:
-                deal_scales()
-            for c, k in later.get(n, []):
-                stage(c, k)
+        regroup(0, 0, "s")
+        regroup(0, 1, "v")
+        regroup(1, 0, "s")
+        for t in range(PACK):
+            project(0, t)
+        raw_out(0, 0)
+        raw_out(0, 1)
+        sources = [(i, t, mic) for i in range(2) for t in range(2) for mic in range(2)]
+        first_pick = held([P, S], F32, "pick0")
+        picked[0] = first_pick[:]
+        gather_raw(0, 0, 0, picked[0])
+        regroup(1, 1, "v")
+        for t in range(PACK):
+            project(1, t)
+        pin = held([P, 2 * S], F32, "grouped1")
+        picked[1] = pin[:, 0:S]
+        picked[2] = pin[:, S : 2 * S]
+        for k in range(3, 8):
+            other = held([P, S], F32, "pick%d" % k)
+            picked[k] = other[:]
+        raw_out(1, 0)
+        raw_out(1, 1)
+        for k, (i, t, mic) in enumerate(sources):
+            if k > 0:
+                gather_raw(i, t, mic, picked[k])
+        deal_scales()
+        cross_terms(0, 2)
+        for k in range(0, C2):
+            weigh(k, *sources[k])
+        cross_terms(1, 2)
+        combine(2)
+        for k in range(C2, C3):
+            weigh(k, *sources[k])
+        cross_terms(0, 3)
+        cross_terms(1, 3)
+        combine(3)
+        for k in ORDER:
+            weigh(k, *sources[k])
+        turn_back(0, 0)
+        gather_chunk(0, T0)
+        turn_back(1, 0)
+        stage(0, 4)
+        gather_chunk(1, T1)
+        stage(0, 1)
+        turn_back(2, 0)
+        stage(1, 4)
+        stage(0, 2)
+        gather_chunk(2, T2, "zq0", S2)
+        stage(1, 1)
+        turn_back(3, 0)
+        stage(2, 4)
+        stage(0, 3)
+        stage(1, 2)
+        gather_chunk(3, T3, "both", S3)
+        stage(2, 1)
+        stage(1, 3)
+        stage(2, 2)
+        stage(3, 4)
+        stage(3, 1)
+        stage(2, 3)
+        stage(3, 2)
+        stage(3, 3)
 
         for q in range(4):
             eng = nc.sync if q % 2 == 0 else nc.scalar

@@ -25,6 +25,7 @@ GSHARE = ((6, 0), (6, 1), (7, 0), (7, 1))
 C2 = 3
 C3 = 4
 ORDER = (6, 7, 4, 5)
+TD = "wide11"
 T0 = "pick4"
 T1 = "zb00"
 T2 = "term1111"
@@ -79,16 +80,16 @@ def tile_picked_beamf_none_po_kernel(
         nc.sync.dma_start(m2_t[:], m2)
         for h in range(2):
             nc.sync.dma_start(raw[1][h][:], w_rows[1][:, :, 256 * h : 256 * h + 256])
-        for name, src in (("wr1", wr1), ("wi1", wi1), ("wr2", wr2), ("wi2", wi2)):
-            nc.gpsimd.dma_start(wt[name][:], src.rearrange("(p t) o -> p (t o)", t=PACK))
+        for name, src in (("wi1", wi1), ("wi2", wi2), ("wr1", wr1), ("wr2", wr2)):
+            nc.sync.dma_start(wt[name][:], src.rearrange("(p t) o -> p (t o)", t=PACK))
         make_identity(nc, ident[:])
         for i, src in enumerate((w3_scales, w4_scales)):
             for q in range(4):
                 nc.sync.dma_start(
                     w34s[32 * q : 32 * q + 4, i * N : (i + 1) * N].bitcast(I32), src[0, 4 * q : 4 * q + 4, :].bitcast(I32)
                 )
-        nc.scalar.activation(wt["nwi1"][:], wt["wi1"][:], COPY, scale=-1.0)
-        nc.scalar.activation(wt["nwi2"][:], wt["wi2"][:], COPY, scale=-1.0)
+        nc.gpsimd.tensor_scalar(wt["nwi1"][:], wt["wi1"][:], -1.0, 0.0, MULT, ADD)
+        nc.gpsimd.tensor_scalar(wt["nwi2"][:], wt["wi2"][:], -1.0, 0.0, MULT, ADD)
 
         w34d = [held([P, 2 * N], U8, "w3d"), held([P, 2 * N], U8, "w4d")]
         for i in range(2):
@@ -106,9 +107,9 @@ def tile_picked_beamf_none_po_kernel(
         wc = [held([P, H], U32, "wc%d" % i) for i in range(2)]
         wsc = [held([P, H], U8, "wsc%d" % i) for i in range(2)]
 
-        def regroup(i, h, eng):
-            dst = grouped[i][:].rearrange("p (t m j) -> p m j t", t=PACK, j=PACK)[:, 64 * h : 64 * h + 64]
-            src = raw[i][h][:].rearrange("p j (m t) -> p m j t", t=PACK)
+        def regroup(i, h, eng, t0=0, t1=PACK):
+            dst = grouped[i][:].rearrange("p (t m j) -> p m j t", t=PACK, j=PACK)[:, 64 * h : 64 * h + 64, :, t0:t1]
+            src = raw[i][h][:].rearrange("p j (m t) -> p m j t", t=PACK)[:, :, :, t0:t1]
             if eng == "v":
                 nc.vector.tensor_copy(dst, src)
             else:
@@ -128,16 +129,19 @@ def tile_picked_beamf_none_po_kernel(
                 rhs=xgw[:].bitcast(FP8X4), rhs_scale=xgs[:], start=True, stop=True,
             )
 
-        w34sd = held([P, 2 * N], U8, "w34sd")
         oc = held([P, S], U32, "oc")
         osc = held([P, S], U8, "osc")
         out_rows = out_0.rearrange("(p t) j -> p t j", t=PACK)
         out_words = out_1[0].rearrange("p c r -> p (c r)").bitcast(I32)
 
+        dealt = {}
+
         def deal_scales():
+            w34sd = held([P, 2 * N], U8, TD)
+            dealt[0] = w34sd
             nc.gpsimd.tensor_copy(
-                w34sd[:].rearrange("p (w t m) -> p w m t", w=2, t=PACK),
-                w34s[:].rearrange("p (w m t) -> p w m t", w=2, t=PACK),
+                w34sd[:].rearrange("p (w t m) -> p w t m", w=2, t=PACK),
+                w34s[:].rearrange("p (w m t) -> p w t m", w=2, t=PACK),
             )
 
         lists = (m1_t, m2_t)
@@ -151,7 +155,8 @@ def tile_picked_beamf_none_po_kernel(
         ACC = {(0, 0): 0, (1, 0): 1, (2, 0): 4, (3, 0): 5, (0, 1): 2, (1, 1): 6, (2, 1): 3, (3, 1): 7}
 
         def raw_out(i, t):
-            nc.scalar.copy(wide[(i, t)][:, 0:S], proj[(i, t)][:])
+            move = nc.vector.tensor_copy if (i, t) == (0, 0) else nc.scalar.copy
+            move(wide[(i, t)][:, 0:S], proj[(i, t)][:])
 
         def cross_terms(i, t):
             for mic in range(2):
@@ -254,15 +259,17 @@ def tile_picked_beamf_none_po_kernel(
                         nc.tensor.matmul_mx(
                             out=res[:, t * CH : (t + 1) * CH],
                             lhsT=w34d[z][:, 2 * P * t : 2 * P * (t + 1)].bitcast(FP4X4),
-                            lhsT_scale=w34sd[:, z * N + t * P : z * N + (t + 1) * P],
+                            lhsT_scale=dealt[0][:, z * N + t * P : z * N + (t + 1) * P],
                             rhs=zc[:, z * CH : (z + 1) * CH].bitcast(FP8X4), rhs_scale=zs[:, z * CH : (z + 1) * CH],
                             start=(z == 0), stop=(z == 1),
                         )
                 ob = both[:, 2 * H : 3 * H] if c == 0 else held([P, PACK * CH], BF16, "ob%d" % c)
-                move = nc.vector.tensor_copy if c == 3 else nc.scalar.copy
-                move(ob[:].rearrange("p (j t) -> p j t", t=PACK), res[:].rearrange("p (t j) -> p j t", t=PACK))
                 of = held([P, PACK * CH], F32, "of%d" % c)
+                if c < 3:
+                    nc.scalar.copy(ob[:].rearrange("p (j t) -> p j t", t=PACK), res[:].rearrange("p (t j) -> p j t", t=PACK))
                 nc.scalar.copy(of[:], res[:])
+                if c == 3:
+                    nc.vector.tensor_copy(ob[:].rearrange("p (j t) -> p j t", t=PACK), of[:].rearrange("p (t j) -> p j t", t=PACK))
                 nc.sync.dma_start(out_rows[:, :, c * CH : (c + 1) * CH], of[:].rearrange("p (t j) -> p t j", t=PACK))
                 st[(c, "ob")] = ob
             else:
@@ -271,7 +278,8 @@ def tile_picked_beamf_none_po_kernel(
                 nc.sync.dma_start(out_words[:, cols], oc[:, cols].bitcast(I32))
 
         regroup(0, 0, "s")
-        regroup(0, 1, "v")
+        regroup(0, 1, "v", 0, 1)
+        regroup(0, 1, "v", 1, PACK)
         regroup(1, 0, "s")
         for t in range(PACK):
             project(0, t)
@@ -281,7 +289,7 @@ def tile_picked_beamf_none_po_kernel(
         first_pick = held([P, S], F32, "pick0")
         picked[0] = first_pick[:]
         gather_raw(0, 0, 0, picked[0])
-        regroup(1, 1, "v")
+        regroup(1, 1, "s")
         for t in range(PACK):
             project(1, t)
         pin = held([P, 2 * S], F32, "grouped1")

@@ -3,7 +3,7 @@ from contextlib import ExitStack
 import concourse.mybir as mybir
 from concourse.masks import make_identity
 
-K, T, S, N, H = 512, 2048, 512, 512, 512
+T, S, N, H = 2048, 512, 512, 512
 FLOPS = 4 * 2 * 512 * 512 * 512
 
 F32 = mybir.dt.float32
@@ -19,19 +19,19 @@ ADD = mybir.AluOpType.add
 COPY = mybir.ActivationFunctionType.Copy
 
 P = 128
-PACK = 4
+LANES = 4
 CH = 128
-GSHARE = ((6, 0), (6, 1), (7, 0), (7, 1))
-C2 = 3
-C3 = 4
-ORDER = (6, 7, 4, 5)
-TD = "wide11"
-T0 = "pick4"
-T1 = "zb00"
-T2 = "term1111"
-S2 = 0
-T3 = "zb11"
-S3 = 0
+LAST = 3
+HALF = H // 2
+BANK = 512
+FIRST_ON_GPSIMD = 6
+WEIGHED_BEFORE_LANE_2 = 3
+
+SUM_BANK = {(0, 0): 0, (1, 0): 1, (2, 0): 4, (3, 0): 5, (0, 1): 2, (1, 1): 6, (2, 1): 3}
+BACK_BANK = (0, 1, 4, 5)
+OUT_BANK = (2, 6, 3)
+LAST_OUT_BANK = (7, 1)
+TERMS_IN_BANK = (16, 8)
 
 
 def tile_picked_beamf_none_po_kernel(
@@ -46,20 +46,23 @@ def tile_picked_beamf_none_po_kernel(
         def held(shape, dtype, name):
             return keep.tile(shape, dtype, name=name, align_bytes=64)
 
+        def bank(b):
+            return psum.tile([P, BANK], F32, name="bank%d" % b)
+
         offs_t = keep.tile([P, S // 16], U16, name="offs_t")
         m1_t = keep.tile([P, S // 16], U16, name="m1_t")
         m2_t = keep.tile([P, S // 16], U16, name="m2_t")
         xw = held([P, T], I32, "xw")
         xs = held([P, T], U8, "xs")
-        w34w = [held([P, 2 * N], U8, "w3w"), held([P, 2 * N], U8, "w4w")]
-        w34s = held([P, 2 * N], U8, "w34s")
-        raw = [[held([P, PACK, H // 2], F32, "raw%d%d" % (i, h)) for h in range(2)] for i in range(2)]
+        w34_words = [held([P, 2 * N], U8, "w3w"), held([P, 2 * N], U8, "w4w")]
+        w34_scales = held([P, 2 * N], U8, "w34s")
+        raw = [[held([P, LANES, HALF], F32, "raw%d%d" % (i, h)) for h in range(2)] for i in range(2)]
         wt = {}
         for name in ("wr1", "wi1", "wr2", "wi2", "nwi1", "nwi2"):
-            wt[name] = held([P, PACK], F32, name)
+            wt[name] = held([P, LANES], F32, name)
 
         nc.gpsimd.memset(xs[:].bitcast(I32), 0)
-        nc.vector.memset(w34s[:].bitcast(I32), 0)
+        nc.vector.memset(w34_scales[:].bitcast(I32), 0)
         wide = {}
         for i in range(2):
             for t in range(2):
@@ -68,279 +71,302 @@ def tile_picked_beamf_none_po_kernel(
         ident = held([P, P], F32, "ident")
 
         nc.sync.dma_start(offs_t[:], offs)
-        nc.sync.dma_start(w34w[0][:].bitcast(I32), w3_words[0].bitcast(I32))
-        nc.sync.dma_start(w34w[1][:].bitcast(I32), w4_words[0].bitcast(I32))
+        nc.sync.dma_start(w34_words[0][:].bitcast(I32), w3_words[0].bitcast(I32))
+        nc.sync.dma_start(w34_words[1][:].bitcast(I32), w4_words[0].bitcast(I32))
         for q in range(4):
             nc.sync.dma_start(xs[32 * q : 32 * q + 4, :].bitcast(I32), x_scales[0, 4 * q : 4 * q + 4, :].bitcast(I32))
         nc.sync.dma_start(xw[:], x_words[0].rearrange("p c r -> p (c r)").bitcast(I32))
-        w_rows = [w.rearrange("(p j) c -> p j c", j=PACK) for w in (w1, w2)]
+        w_rows = [w.rearrange("(p j) c -> p j c", j=LANES) for w in (w1, w2)]
         for h in range(2):
-            nc.sync.dma_start(raw[0][h][:], w_rows[0][:, :, 256 * h : 256 * h + 256])
+            nc.sync.dma_start(raw[0][h][:], w_rows[0][:, :, HALF * h : HALF * (h + 1)])
         nc.sync.dma_start(m1_t[:], m1)
         nc.sync.dma_start(m2_t[:], m2)
         for h in range(2):
-            nc.sync.dma_start(raw[1][h][:], w_rows[1][:, :, 256 * h : 256 * h + 256])
+            nc.sync.dma_start(raw[1][h][:], w_rows[1][:, :, HALF * h : HALF * (h + 1)])
         for name, src in (("wi1", wi1), ("wi2", wi2), ("wr1", wr1), ("wr2", wr2)):
-            nc.sync.dma_start(wt[name][:], src.rearrange("(p t) o -> p (t o)", t=PACK))
+            nc.sync.dma_start(wt[name][:], src.rearrange("(p t) o -> p (t o)", t=LANES))
         make_identity(nc, ident[:])
         for i, src in enumerate((w3_scales, w4_scales)):
             for q in range(4):
                 nc.sync.dma_start(
-                    w34s[32 * q : 32 * q + 4, i * N : (i + 1) * N].bitcast(I32), src[0, 4 * q : 4 * q + 4, :].bitcast(I32)
+                    w34_scales[32 * q : 32 * q + 4, i * N : (i + 1) * N].bitcast(I32),
+                    src[0, 4 * q : 4 * q + 4, :].bitcast(I32),
                 )
         nc.gpsimd.tensor_scalar(wt["nwi1"][:], wt["wi1"][:], -1.0, 0.0, MULT, ADD)
         nc.gpsimd.tensor_scalar(wt["nwi2"][:], wt["wi2"][:], -1.0, 0.0, MULT, ADD)
+        lists = (m1_t, m2_t)
+        wr = (wt["wr1"], wt["wr2"])
+        w_cross = ((wt["wi1"], wt["wi2"]), (wt["nwi1"], wt["nwi2"]))
 
-        w34d = [held([P, 2 * N], U8, "w3d"), held([P, 2 * N], U8, "w4d")]
+        w34_dealt = [held([P, 2 * N], U8, "w3d"), held([P, 2 * N], U8, "w4d")]
         for i in range(2):
             nc.vector.tensor_copy(
-                w34d[i][:].rearrange("p (t m e) -> p m t e", t=PACK, e=2),
-                w34w[i][:].rearrange("p (m t e) -> p m t e", t=PACK, e=2),
+                w34_dealt[i][:].rearrange("p (t m e) -> p m t e", t=LANES, e=2),
+                w34_words[i][:].rearrange("p (m t e) -> p m t e", t=LANES, e=2),
             )
 
-        xgw = held([P, S], U32, "xgw")
-        xgs = held([P, S], U8, "xgs")
-        nc.vector.tensor_copy(xgs[:], xs[:].indirect(offs_t[:]))
-        nc.vector.tensor_copy(xgw[:], xw[:].bitcast(U32).indirect(offs_t[:]))
+        xg_words = held([P, S], U32, "xgw")
+        xg_scales = held([P, S], U8, "xgs")
+        nc.vector.tensor_copy(xg_scales[:], xs[:].indirect(offs_t[:]))
+        nc.vector.tensor_copy(xg_words[:], xw[:].bitcast(U32).indirect(offs_t[:]))
 
-        grouped = [held([P, PACK * H], BF16, "grouped%d" % i) for i in range(2)]
-        wc = [held([P, H], U32, "wc%d" % i) for i in range(2)]
-        wsc = [held([P, H], U8, "wsc%d" % i) for i in range(2)]
-
-        def regroup(i, h, eng, t0=0, t1=PACK):
-            dst = grouped[i][:].rearrange("p (t m j) -> p m j t", t=PACK, j=PACK)[:, 64 * h : 64 * h + 64, :, t0:t1]
-            src = raw[i][h][:].rearrange("p j (m t) -> p m j t", t=PACK)[:, :, :, t0:t1]
-            if eng == "v":
-                nc.vector.tensor_copy(dst, src)
-            else:
-                nc.scalar.copy(dst, src)
-
-        def bank(b):
-            return psum.tile([P, 512], F32, name="bank%d" % b)
-
+        grouped = [held([P, LANES * H], BF16, "grouped%d" % i) for i in range(2)]
+        w_codes = [held([P, H], U32, "wc%d" % i) for i in range(2)]
+        w_scales = [held([P, H], U8, "wsc%d" % i) for i in range(2)]
         proj = {}
+
+        def regroup(i, h, move, t0, t1):
+            m_half = slice(HALF // LANES * h, HALF // LANES * (h + 1))
+            move(
+                grouped[i][:].rearrange("p (t m j) -> p m j t", t=LANES, j=LANES)[:, m_half, :, t0:t1],
+                raw[i][h][:].rearrange("p j (m t) -> p m j t", t=LANES)[:, :, :, t0:t1],
+            )
 
         def project(i, t):
             cols = slice(t * P, (t + 1) * P)
-            nc.vector.quantize_mx(out=wc[i][:, cols].bitcast(FP8X4), scales=wsc[i][:, cols], in_=grouped[i][:, t * 512 : (t + 1) * 512])
-            proj[(i, t)] = bank(4 * i + t)
+            nc.vector.quantize_mx(
+                out=w_codes[i][:, cols].bitcast(FP8X4), scales=w_scales[i][:, cols],
+                in_=grouped[i][:, t * LANES * P : (t + 1) * LANES * P],
+            )
+            proj[(i, t)] = bank(LANES * i + t)
             nc.tensor.matmul_mx(
-                out=proj[(i, t)][:], lhsT=wc[i][:, cols].bitcast(FP8X4), lhsT_scale=wsc[i][:, cols],
-                rhs=xgw[:].bitcast(FP8X4), rhs_scale=xgs[:], start=True, stop=True,
+                out=proj[(i, t)][:], lhsT=w_codes[i][:, cols].bitcast(FP8X4), lhsT_scale=w_scales[i][:, cols],
+                rhs=xg_words[:].bitcast(FP8X4), rhs_scale=xg_scales[:], start=True, stop=True,
             )
 
-        oc = held([P, S], U32, "oc")
-        osc = held([P, S], U8, "osc")
-        out_rows = out_0.rearrange("(p t) j -> p t j", t=PACK)
+        out_codes = held([P, S], U32, "oc")
+        out_scales = held([P, S], U8, "osc")
+        out_rows = out_0.rearrange("(p t) j -> p t j", t=LANES)
         out_words = out_1[0].rearrange("p c r -> p (c r)").bitcast(I32)
 
-        dealt = {}
-
-        def deal_scales():
-            w34sd = held([P, 2 * N], U8, TD)
-            dealt[0] = w34sd
-            nc.gpsimd.tensor_copy(
-                w34sd[:].rearrange("p (w t m) -> p w t m", w=2, t=PACK),
-                w34s[:].rearrange("p (w m t) -> p w t m", w=2, t=PACK),
-            )
-
-        lists = (m1_t, m2_t)
-        wr = (wt["wr1"], wt["wr2"])
-        wi = (wt["wi1"], wt["wi2"])
-        nwi = (wt["nwi1"], wt["nwi2"])
-        win = {}
-        cross = {}
-        banks = {}
-        count = {}
-        ACC = {(0, 0): 0, (1, 0): 1, (2, 0): 4, (3, 0): 5, (0, 1): 2, (1, 1): 6, (2, 1): 3, (3, 1): 7}
-
-        def raw_out(i, t):
-            move = nc.vector.tensor_copy if (i, t) == (0, 0) else nc.scalar.copy
-            move(wide[(i, t)][:, 0:S], proj[(i, t)][:])
+        cross, mixed, sums, count, picked = {}, {}, {}, {}, {}
 
         def cross_terms(i, t):
             for mic in range(2):
-                tile = held([P, S], F32, "cross%d%d%d" % (i, t, mic))
-                w = (wi, nwi)[i][mic][:, t : t + 1]
-                nc.scalar.activation(tile[:], proj[(i, t)][:], COPY, scale=w)
-                cross[(i, t, mic)] = tile
+                cross[(i, t, mic)] = held([P, S], F32, "cross%d%d%d" % (i, t, mic))
+                nc.scalar.activation(cross[(i, t, mic)][:], proj[(i, t)][:], COPY, scale=w_cross[i][mic][:, t : t + 1])
 
         def combine(t):
             for z in range(2):
                 for mic in range(2):
-                    tile = held([P, S], F32, "win%d%d%d" % (z, t, mic))
-                    nc.vector.scalar_tensor_tensor(tile[:], proj[(z, t)][:], wr[mic][:, t : t + 1], cross[(1 - z, t, mic)][:], MULT, ADD)
-                    win[(z, t, mic)] = tile
+                    mixed[(z, t, mic)] = held([P, S], F32, "win%d%d%d" % (z, t, mic))
+                    nc.vector.scalar_tensor_tensor(
+                        mixed[(z, t, mic)][:], proj[(z, t)][:], wr[mic][:, t : t + 1], cross[(1 - z, t, mic)][:], MULT, ADD
+                    )
 
         def add_term(term, t, z, j0, n):
             u, e = divmod(t, 2)
             for c in range(j0 // CH, (j0 + n) // CH):
-                if (c, u) not in banks:
-                    banks[(c, u)] = bank(ACC[(c, u)])
+                if (c, u) not in sums:
+                    sums[(c, u)] = bank(SUM_BANK[(c, u)])
                     count[(c, u)] = 0
-                k = count[(c, u)]
                 nc.tensor.matmul(
-                    banks[(c, u)][:, (2 * z + e) * P : (2 * z + e + 1) * P], lhsT=term[:, c * CH - j0 : (c + 1) * CH - j0], rhs=ident[:],
-                    is_transpose=True, start=(k == 0), stop=(k == (15 if u == 0 else 7)),
+                    sums[(c, u)][:, (2 * z + e) * P : (2 * z + e + 1) * P],
+                    lhsT=term[:, c * CH - j0 : (c + 1) * CH - j0], rhs=ident[:], is_transpose=True,
+                    start=(count[(c, u)] == 0), stop=(count[(c, u)] == TERMS_IN_BANK[u] - 1),
                 )
-                count[(c, u)] = k + 1
+                count[(c, u)] = count[(c, u)] + 1
 
-        picked = {}
+        lookups = [(i, t, mic) for i in range(2) for t in range(2) for mic in range(2)]
 
-        def gather_raw(i, t, mic, tile):
-            nc.vector.tensor_copy(tile, wide[(i, t)][:].indirect(lists[mic][:]))
+        def gather_plain(k):
+            i, t, mic = lookups[k]
+            nc.vector.tensor_copy(picked[k], wide[(i, t)][:].indirect(lists[mic][:]))
 
-        def weigh(k, i, t, mic):
+        def weigh(k):
+            i, t, mic = lookups[k]
+            terms = held([P, 2 * S], F32, "wide11" if k == FIRST_ON_GPSIMD else "terms%d" % k)
             for z in range(2):
-                w = wr[mic] if z == i else (wi, nwi)[i][mic]
-                term = held([P, S], F32, "term%d%d%d%d" % (i, t, mic, z))
-                if (k, z) in GSHARE:
-                    nc.gpsimd.tensor_scalar(term[:], picked[k], w[:, t : t + 1], 0.0, MULT, ADD)
+                w = wr[mic] if z == i else w_cross[i][mic]
+                term = terms[:, z * S : (z + 1) * S]
+                if k >= FIRST_ON_GPSIMD:
+                    nc.gpsimd.tensor_scalar(term, picked[k], w[:, t : t + 1], 0.0, MULT, ADD)
                 else:
-                    nc.scalar.activation(term[:], picked[k], COPY, scale=w[:, t : t + 1])
+                    nc.scalar.activation(term, picked[k], COPY, scale=w[:, t : t + 1])
                 add_term(term, t, z, 0, S)
 
-        def gather_chunk(c, tag, tag2=None, split=8):
-            tile = held([P, 8 * CH], F32, tag)
-            k = 0
-            for t in (2, 3):
-                for z in range(2):
-                    for mic in range(2):
-                        if k == split:
-                            tile = held([P, 8 * CH], F32, tag2)
-                        piece = tile[:, k * CH : (k + 1) * CH]
-                        nc.vector.tensor_copy(piece, win[(z, t, mic)][:].indirect(lists[mic][:, 8 * c : 8 * c + 8]))
-                        add_term(piece, t, z, c * CH, CH)
-                        k = k + 1
+        def gather_mixed(t, j0, n, name):
+            tile = held([P, 4 * n], F32, name)
+            for z in range(2):
+                for mic in range(2):
+                    piece = tile[:, (2 * z + mic) * n : (2 * z + mic + 1) * n]
+                    offsets = lists[mic][:, j0 // 16 : (j0 + n) // 16]
+                    nc.vector.tensor_copy(piece, mixed[(z, t, mic)][:].indirect(offsets))
+                    add_term(piece, t, z, j0, n)
 
-        st = {}
-        both = held([P, 3 * H], BF16, "both")
+        z_last = held([P, 2 * LANES * CH], F32, "zlast")
+        back, z_in, out_bf, w34_scales_dealt = {}, {}, {}, {}
 
         def turn_back(c, u):
-            zb = held([P, H], BF16, "zb%d%d" % (c, u))
-            move = nc.vector.tensor_copy if (c == 3 and u == 1) else nc.scalar.copy
-            move(zb[:].rearrange("j (z p e) -> j z p e", z=2, e=2), banks[(c, u)][:].rearrange("j (z e p) -> j z p e", z=2, e=2))
-            words = zb[:].bitcast(F32)
+            pairs = held([P, H], BF16, "zb%d%d" % (c, u))
+            nc.scalar.copy(
+                pairs[:].rearrange("j (z p e) -> j z p e", z=2, e=2),
+                sums[(c, u)][:].rearrange("j (z e p) -> j z p e", z=2, e=2),
+            )
+            words = pairs[:].bitcast(F32)
             if u == 0:
-                first = bank((0, 1, 4, 5)[c])
-                if c == 3:
-                    second = bank(0)
-                    st[(c, "back")] = [first[:, 0:256], second[:, 0:256]]
-                else:
-                    st[(c, "back")] = [first[:, 0:256], first[:, 256:512]]
-                st[(c, "first")] = first
+                back[c] = bank(BACK_BANK[c])
             for z in range(2):
-                nc.tensor.transpose(st[(c, "back")][z][:, u * P : (u + 1) * P], words[:, z * P : (z + 1) * P], ident[:])
+                nc.tensor.transpose(back[c][:, (2 * z + u) * P : (2 * z + u + 1) * P], words[:, z * P : (z + 1) * P], ident[:])
 
-        def stage(c, k):
-            if k == 0 or k == 4:
-                turn_back(c, k // 4)
-            elif k == 1:
-                zq = both[:, 0 : 2 * H] if c == 1 else held([P, 2 * H], BF16, "zq%d" % c)
-                if c == 3:
-                    for z, move in enumerate((nc.vector.tensor_copy, nc.scalar.copy)):
-                        move(
-                            zq[:].bitcast(F32)[:, z * 256 : (z + 1) * 256].rearrange("p (j u) -> p j u", u=2),
-                            st[(c, "back")][z].rearrange("p (u j) -> p j u", u=2),
-                        )
-                else:
-                    nc.scalar.copy(
-                        zq[:].bitcast(F32).rearrange("p (z j u) -> p z j u", z=2, u=2),
-                        st[(c, "first")][:].rearrange("p (z u j) -> p z j u", z=2, u=2),
-                    )
-                st[(c, "zq")] = zq
-            elif k == 2:
-                zc = held([P, 2 * CH], U32, "zc%d" % c)
-                zs = held([P, 2 * CH], U8, "zs%d" % c)
-                nc.vector.quantize_mx(out=zc[:].bitcast(FP8X4), scales=zs[:], in_=st[(c, "zq")][:])
-                res = bank((2, 6, 3, 1)[c])
-                for t in range(PACK):
-                    for z in range(2):
-                        nc.tensor.matmul_mx(
-                            out=res[:, t * CH : (t + 1) * CH],
-                            lhsT=w34d[z][:, 2 * P * t : 2 * P * (t + 1)].bitcast(FP4X4),
-                            lhsT_scale=dealt[0][:, z * N + t * P : z * N + (t + 1) * P],
-                            rhs=zc[:, z * CH : (z + 1) * CH].bitcast(FP8X4), rhs_scale=zs[:, z * CH : (z + 1) * CH],
-                            start=(z == 0), stop=(z == 1),
-                        )
-                ob = both[:, 2 * H : 3 * H] if c == 0 else held([P, PACK * CH], BF16, "ob%d" % c)
-                of = held([P, PACK * CH], F32, "of%d" % c)
-                if c < 3:
-                    nc.scalar.copy(ob[:].rearrange("p (j t) -> p j t", t=PACK), res[:].rearrange("p (t j) -> p j t", t=PACK))
-                nc.scalar.copy(of[:], res[:])
-                if c == 3:
-                    nc.vector.tensor_copy(ob[:].rearrange("p (j t) -> p j t", t=PACK), of[:].rearrange("p (t j) -> p j t", t=PACK))
-                nc.sync.dma_start(out_rows[:, :, c * CH : (c + 1) * CH], of[:].rearrange("p (t j) -> p t j", t=PACK))
-                st[(c, "ob")] = ob
-            else:
-                cols = slice(c * CH, (c + 1) * CH)
-                nc.vector.quantize_mx(out=oc[:, cols].bitcast(FP8X4), scales=osc[:, cols], in_=st[(c, "ob")][:])
-                nc.sync.dma_start(out_words[:, cols], oc[:, cols].bitcast(I32))
+        def close_sums(c):
+            turn_back(c, 1)
 
-        regroup(0, 0, "s")
-        regroup(0, 1, "v", 0, 1)
-        regroup(0, 1, "v", 1, PACK)
-        regroup(1, 0, "s")
-        for t in range(PACK):
+        def interleave(c):
+            z_in[c] = held([P, 2 * H], BF16, "zq%d" % c)
+            nc.scalar.copy(
+                z_in[c][:].bitcast(F32).rearrange("p (z j u) -> p z j u", z=2, u=2),
+                back[c][:].rearrange("p (z u j) -> p z j u", z=2, u=2),
+            )
+
+        def out_lane(res, t, z_codes, z_scales):
+            for z in range(2):
+                nc.tensor.matmul_mx(
+                    out=res,
+                    lhsT=w34_dealt[z][:, 2 * P * t : 2 * P * (t + 1)].bitcast(FP4X4),
+                    lhsT_scale=w34_scales_dealt[0][:, z * N + t * P : z * N + (t + 1) * P],
+                    rhs=z_codes[:, z * CH : (z + 1) * CH].bitcast(FP8X4), rhs_scale=z_scales[:, z * CH : (z + 1) * CH],
+                    start=(z == 0), stop=(z == 1),
+                )
+
+        def multiply(c):
+            z_codes = held([P, 2 * CH], U32, "zc%d" % c)
+            z_scales = held([P, 2 * CH], U8, "zs%d" % c)
+            nc.vector.quantize_mx(out=z_codes[:].bitcast(FP8X4), scales=z_scales[:], in_=z_in[c][:])
+            res = bank(OUT_BANK[c])
+            for t in range(LANES):
+                out_lane(res[:, t * CH : (t + 1) * CH], t, z_codes, z_scales)
+            out_bf[c] = held([P, LANES * CH], BF16, "ob%d" % c)
+            out_f32 = held([P, LANES * CH], F32, "of%d" % c)
+            nc.scalar.copy(out_bf[c][:].rearrange("p (j t) -> p j t", t=LANES), res[:].rearrange("p (t j) -> p j t", t=LANES))
+            nc.scalar.copy(out_f32[:], res[:])
+            nc.sync.dma_start(out_rows[:, :, c * CH : (c + 1) * CH], out_f32[:].rearrange("p (t j) -> p t j", t=LANES))
+
+        def hand_on(c):
+            cols = slice(c * CH, (c + 1) * CH)
+            nc.vector.quantize_mx(out=out_codes[:, cols].bitcast(FP8X4), scales=out_scales[:, cols], in_=out_bf[c][:])
+            if c % 2 == 1:
+                done = slice((c - 1) * CH, (c + 1) * CH)
+                nc.sync.dma_start(out_words[:, done], out_codes[:, done].bitcast(I32))
+
+        def last_low_lanes():
+            turned = held([P, H], F32, "zt3")
+            nc.scalar.copy(turned[:], sums[(LAST, 0)][:])
+            res = bank(BACK_BANK[LAST])
+            for b in range(4):
+                nc.tensor.transpose(res[:, b * P : (b + 1) * P], turned[:, b * P : (b + 1) * P], ident[:])
+            nc.scalar.copy(
+                z_last[:].rearrange("p (z t j) -> p z t j", z=2, t=LANES)[:, :, 0:2, :],
+                res[:].rearrange("p (z e j) -> p z e j", z=2, e=2),
+            )
+
+        def last_high_lanes(z, name, move):
+            cols = slice(LAST * CH // 16, (LAST + 1) * CH // 16)
+            first = held([P, 2 * CH], F32, name)
+            for e in range(2):
+                nc.vector.tensor_copy(first[:, e * CH : (e + 1) * CH], mixed[(z, 2 + e, 0)][:].indirect(lists[0][:, cols]))
+            for e in range(2):
+                at = (z * LANES + 2 + e) * CH
+                nc.vector.tensor_tensor(
+                    z_last[:, at : at + CH], mixed[(z, 2 + e, 1)][:].indirect(lists[1][:, cols]),
+                    first[:, e * CH : (e + 1) * CH], ADD,
+                )
+            z_in[(LAST, z)] = held([P, H], BF16, "zq3%d" % z)
+            move(
+                z_in[(LAST, z)][:].rearrange("p (j t) -> p j t", t=LANES),
+                z_last[:, z * H : (z + 1) * H].rearrange("p (t j) -> p j t", t=LANES),
+            )
+
+        def last_multiply():
+            z_codes = held([P, 2 * CH], U32, "zc3")
+            z_scales = held([P, 2 * CH], U8, "zs3")
+            for z in range(2):
+                cols = slice(z * CH, (z + 1) * CH)
+                nc.vector.quantize_mx(out=z_codes[:, cols].bitcast(FP8X4), scales=z_scales[:, cols], in_=z_in[(LAST, z)][:])
+            out_bf[LAST] = held([P, LANES * CH], BF16, "ob3")
+            for u in range(2):
+                res = bank(LAST_OUT_BANK[u])
+                for e in range(2):
+                    out_lane(res[:, e * CH : (e + 1) * CH], 2 * u + e, z_codes, z_scales)
+                nc.vector.tensor_copy(
+                    out_bf[LAST][:].rearrange("p (j t) -> p j t", t=LANES)[:, :, 2 * u : 2 * u + 2],
+                    res[:, 0 : 2 * CH].rearrange("p (e j) -> p j e", e=2),
+                )
+                out_f32 = held([P, 2 * CH], F32, "of3%d" % u)
+                nc.scalar.copy(out_f32[:], res[:, 0 : 2 * CH])
+                nc.sync.dma_start(
+                    out_rows[:, 2 * u : 2 * u + 2, LAST * CH : (LAST + 1) * CH], out_f32[:].rearrange("p (e j) -> p e j", e=2)
+                )
+
+        regroup(0, 0, nc.scalar.copy, 0, LANES)
+        regroup(0, 1, nc.vector.tensor_copy, 0, 1)
+        regroup(0, 1, nc.vector.tensor_copy, 1, LANES)
+        regroup(1, 0, nc.scalar.copy, 0, LANES)
+        for t in range(LANES):
             project(0, t)
-        raw_out(0, 0)
-        raw_out(0, 1)
-        sources = [(i, t, mic) for i in range(2) for t in range(2) for mic in range(2)]
-        first_pick = held([P, S], F32, "pick0")
-        picked[0] = first_pick[:]
-        gather_raw(0, 0, 0, picked[0])
-        regroup(1, 1, "s")
-        for t in range(PACK):
+        for t in range(2):
+            nc.scalar.copy(wide[(0, t)][:, 0:S], proj[(0, t)][:])
+        picked[0] = held([P, S], F32, "pick0")[:]
+        gather_plain(0)
+        regroup(1, 1, nc.vector.tensor_copy, 0, LANES)
+        for t in range(LANES):
             project(1, t)
-        pin = held([P, 2 * S], F32, "grouped1")
-        picked[1] = pin[:, 0:S]
-        picked[2] = pin[:, S : 2 * S]
-        for k in range(3, 8):
-            other = held([P, S], F32, "pick%d" % k)
-            picked[k] = other[:]
-        raw_out(1, 0)
-        raw_out(1, 1)
-        for k, (i, t, mic) in enumerate(sources):
-            if k > 0:
-                gather_raw(i, t, mic, picked[k])
-        deal_scales()
+        after_w2 = held([P, 2 * S], F32, "grouped1")
+        picked[1] = after_w2[:, 0:S]
+        picked[2] = after_w2[:, S : 2 * S]
+        for k in range(3, len(lookups)):
+            picked[k] = held([P, S], F32, "pick%d" % k)[:]
+        for t in range(2):
+            nc.scalar.copy(wide[(1, t)][:, 0:S], proj[(1, t)][:])
+        for k in range(1, len(lookups)):
+            gather_plain(k)
+
         cross_terms(0, 2)
-        for k in range(0, C2):
-            weigh(k, *sources[k])
+        for k in range(WEIGHED_BEFORE_LANE_2):
+            weigh(k)
         cross_terms(1, 2)
         combine(2)
-        for k in range(C2, C3):
-            weigh(k, *sources[k])
-        cross_terms(0, 3)
+        for k in range(WEIGHED_BEFORE_LANE_2, len(lookups)):
+            weigh(k)
+        gather_mixed(2, 0, 2 * CH, "pick5")
+        w34_scales_dealt[0] = held([P, 2 * N], U8, "pick5")
+        nc.gpsimd.tensor_copy(
+            w34_scales_dealt[0][:].rearrange("p (w t m) -> p w t m", w=2, t=LANES),
+            w34_scales[:].rearrange("p (w m t) -> p w t m", w=2, t=LANES),
+        )
         cross_terms(1, 3)
+        cross_terms(0, 3)
         combine(3)
-        for k in ORDER:
-            weigh(k, *sources[k])
-        turn_back(0, 0)
-        gather_chunk(0, T0)
-        turn_back(1, 0)
-        stage(0, 4)
-        gather_chunk(1, T1)
-        stage(0, 1)
-        turn_back(2, 0)
-        stage(1, 4)
-        stage(0, 2)
-        gather_chunk(2, T2, "zq0", S2)
-        stage(1, 1)
-        turn_back(3, 0)
-        stage(2, 4)
-        stage(0, 3)
-        stage(1, 2)
-        gather_chunk(3, T3, "both", S3)
-        stage(2, 1)
-        stage(1, 3)
-        stage(2, 2)
-        stage(3, 4)
-        stage(3, 1)
-        stage(2, 3)
-        stage(3, 2)
-        stage(3, 3)
+        for c in range(LAST):
+            turn_back(c, 0)
+        gather_mixed(3, 0, CH, "run10")
+        gather_mixed(3, CH, CH, "run11")
+
+        close_sums(0)
+
+        close_sums(1)
+        gather_mixed(2, 2 * CH, CH, "run10")
+        gather_mixed(3, 2 * CH, CH, "run11")
+        interleave(0)
+        last_low_lanes()
+
+        close_sums(2)
+        interleave(1)
+        multiply(0)
+
+        interleave(2)
+        last_high_lanes(0, "zq0", nc.scalar.copy)
+        multiply(1)
+        hand_on(0)
+
+        multiply(2)
+        last_high_lanes(1, "ob0", nc.vector.tensor_copy)
+        hand_on(1)
+        last_multiply()
+
+        hand_on(2)
+        hand_on(LAST)
 
         for q in range(4):
-            eng = nc.sync if q % 2 == 0 else nc.scalar
-            eng.dma_start(out_2[0, 4 * q : 4 * q + 4, :].bitcast(I32), osc[32 * q : 32 * q + 4, :].bitcast(I32))
+            queue = nc.sync if q % 2 == 0 else nc.scalar
+            queue.dma_start(out_2[0, 4 * q : 4 * q + 4, :].bitcast(I32), out_scales[32 * q : 32 * q + 4, :].bitcast(I32))

@@ -24,14 +24,11 @@ CH = 128
 LAST = 3
 HALF = H // 2
 BANK = 512
-FIRST_ON_GPSIMD = 6
-WEIGHED_BEFORE_LANE_2 = 3
-
-SUM_BANK = {(0, 0): 0, (1, 0): 1, (2, 0): 4, (3, 0): 5, (0, 1): 2, (1, 1): 6, (2, 1): 3}
-BACK_BANK = (0, 1, 4, 5)
-OUT_BANK = (2, 6, 3)
-LAST_OUT_BANK = (7, 1)
-TERMS_IN_BANK = (16, 8)
+PROJ_BANK = ((0, 1, 4, 5), (6, 7, 6, 7))
+SUM_BANK = (2, 3, 0, 1)
+OUT_BANK = (4, 5, 6)
+LAST_OUT_BANK = (2, 3, 0, 7)
+TERMS_IN_BANK = 16
 
 
 def tile_picked_beamf_none_po_kernel(
@@ -56,34 +53,34 @@ def tile_picked_beamf_none_po_kernel(
         xs = held([P, T], U8, "xs")
         w34_words = [held([P, 2 * N], U8, "w3w"), held([P, 2 * N], U8, "w4w")]
         w34_scales = held([P, 2 * N], U8, "w34s")
-        raw = [[held([P, LANES, HALF], F32, "raw%d%d" % (i, h)) for h in range(2)] for i in range(2)]
+        raw = [held([P, LANES, H], F32, "raw%d" % i) for i in range(2)]
         wt = {}
         for name in ("wr1", "wi1", "wr2", "wi2", "nwi1", "nwi2"):
             wt[name] = held([P, LANES], F32, name)
 
         nc.gpsimd.memset(xs[:].bitcast(I32), 0)
         nc.vector.memset(w34_scales[:].bitcast(I32), 0)
-        wide = {}
+        window = {}
         for i in range(2):
             for t in range(2):
-                wide[(i, t)] = held([P, 2 * S], F32, "wide%d%d" % (i, t))
-                nc.vector.memset(wide[(i, t)][:, S : 2 * S], 0.0)
+                window[(i, t)] = held([P, 2 * S], F32, "window%d%d" % (i, t))
+                nc.vector.memset(window[(i, t)][:, S : 2 * S], 0.0)
         ident = held([P, P], F32, "ident")
 
+        w_rows = [w.rearrange("(p j) c -> p j c", j=LANES) for w in (w1, w2)]
         nc.sync.dma_start(offs_t[:], offs)
-        nc.sync.dma_start(w34_words[0][:].bitcast(I32), w3_words[0].bitcast(I32))
-        nc.sync.dma_start(w34_words[1][:].bitcast(I32), w4_words[0].bitcast(I32))
         for q in range(4):
             nc.sync.dma_start(xs[32 * q : 32 * q + 4, :].bitcast(I32), x_scales[0, 4 * q : 4 * q + 4, :].bitcast(I32))
+        nc.sync.dma_start(raw[0][:], w_rows[0])
         nc.sync.dma_start(xw[:], x_words[0].rearrange("p c r -> p (c r)").bitcast(I32))
-        w_rows = [w.rearrange("(p j) c -> p j c", j=LANES) for w in (w1, w2)]
-        for h in range(2):
-            nc.sync.dma_start(raw[0][h][:], w_rows[0][:, :, HALF * h : HALF * (h + 1)])
+        nc.sync.dma_start(w34_words[0][:].bitcast(I32), w3_words[0].bitcast(I32))
+        nc.sync.dma_start(w34_words[1][:].bitcast(I32), w4_words[0].bitcast(I32))
         nc.sync.dma_start(m1_t[:], m1)
         nc.sync.dma_start(m2_t[:], m2)
-        for h in range(2):
-            nc.sync.dma_start(raw[1][h][:], w_rows[1][:, :, HALF * h : HALF * (h + 1)])
-        for name, src in (("wi1", wi1), ("wi2", wi2), ("wr1", wr1), ("wr2", wr2)):
+        for name, src in (("wr1", wr1), ("wi1", wi1)):
+            nc.sync.dma_start(wt[name][:], src.rearrange("(p t) o -> p (t o)", t=LANES))
+        nc.sync.dma_start(raw[1][:], w_rows[1])
+        for name, src in (("wr2", wr2), ("wi2", wi2)):
             nc.sync.dma_start(wt[name][:], src.rearrange("(p t) o -> p (t o)", t=LANES))
         make_identity(nc, ident[:])
         for i, src in enumerate((w3_scales, w4_scales)):
@@ -99,7 +96,8 @@ def tile_picked_beamf_none_po_kernel(
         w_cross = ((wt["wi1"], wt["wi2"]), (wt["nwi1"], wt["nwi2"]))
 
         w34_dealt = [held([P, 2 * N], U8, "w3d"), held([P, 2 * N], U8, "w4d")]
-        for i in range(2):
+
+        def deal_words(i):
             nc.vector.tensor_copy(
                 w34_dealt[i][:].rearrange("p (t m e) -> p m t e", t=LANES, e=2),
                 w34_words[i][:].rearrange("p (m t e) -> p m t e", t=LANES, e=2),
@@ -108,126 +106,125 @@ def tile_picked_beamf_none_po_kernel(
         xg_words = held([P, S], U32, "xgw")
         xg_scales = held([P, S], U8, "xgs")
         nc.vector.tensor_copy(xg_scales[:], xs[:].indirect(offs_t[:]))
-        nc.vector.tensor_copy(xg_words[:], xw[:].bitcast(U32).indirect(offs_t[:]))
 
-        grouped = [held([P, LANES * H], BF16, "grouped%d" % i) for i in range(2)]
+        grouped = {}
         w_codes = [held([P, H], U32, "wc%d" % i) for i in range(2)]
         w_scales = [held([P, H], U8, "wsc%d" % i) for i in range(2)]
         proj = {}
 
-        def regroup(i, h, move, t0, t1):
-            m_half = slice(HALF // LANES * h, HALF // LANES * (h + 1))
+        def regroup(i, u, move):
             move(
-                grouped[i][:].rearrange("p (t m j) -> p m j t", t=LANES, j=LANES)[:, m_half, :, t0:t1],
-                raw[i][h][:].rearrange("p j (m t) -> p m j t", t=LANES)[:, :, :, t0:t1],
+                grouped[(i, u)][:].rearrange("p (t m j) -> p m j t", t=2, j=LANES),
+                raw[i][:].rearrange("p j (m t) -> p m j t", t=LANES)[:, :, :, 2 * u : 2 * u + 2],
             )
 
-        def project(i, t):
-            cols = slice(t * P, (t + 1) * P)
+        def quantise_w(i, t0, t1):
+            cols = slice(t0 * P, t1 * P)
             nc.vector.quantize_mx(
                 out=w_codes[i][:, cols].bitcast(FP8X4), scales=w_scales[i][:, cols],
-                in_=grouped[i][:, t * LANES * P : (t + 1) * LANES * P],
+                in_=grouped[(i, t0 // 2)][:, t0 % 2 * H : (t0 % 2 + t1 - t0) * H],
             )
-            proj[(i, t)] = bank(LANES * i + t)
+
+        def project(i, t, j0=0, n=S):
+            cols = slice(t * P, (t + 1) * P)
+            proj[(i, t)] = bank(PROJ_BANK[i][t] if j0 == 0 else SUM_BANK[0])
             nc.tensor.matmul_mx(
-                out=proj[(i, t)][:], lhsT=w_codes[i][:, cols].bitcast(FP8X4), lhsT_scale=w_scales[i][:, cols],
-                rhs=xg_words[:].bitcast(FP8X4), rhs_scale=xg_scales[:], start=True, stop=True,
+                out=proj[(i, t)][:, j0 : j0 + n], lhsT=w_codes[i][:, cols].bitcast(FP8X4), lhsT_scale=w_scales[i][:, cols],
+                rhs=xg_words[:, j0 : j0 + n].bitcast(FP8X4), rhs_scale=xg_scales[:, j0 : j0 + n], start=True, stop=True,
             )
+
+        def fill(i, t, j0=0, n=S):
+            nc.scalar.copy(window[(i, t)][:, j0 : j0 + n], proj[(i, t)][:, j0 : j0 + n])
 
         out_codes = held([P, S], U32, "oc")
         out_scales = held([P, S], U8, "osc")
         out_rows = out_0.rearrange("(p t) j -> p t j", t=LANES)
         out_words = out_1[0].rearrange("p c r -> p (c r)").bitcast(I32)
 
-        cross, mixed, sums, count, picked = {}, {}, {}, {}, {}
+        cross, mixed, sums, count = {}, {}, {}, {}
 
-        def cross_terms(i, t):
-            for mic in range(2):
-                cross[(i, t, mic)] = held([P, S], F32, "cross%d%d%d" % (i, t, mic))
-                nc.scalar.activation(cross[(i, t, mic)][:], proj[(i, t)][:], COPY, scale=w_cross[i][mic][:, t : t + 1])
-
-        def combine(t):
-            for z in range(2):
+        def cross_terms(i, name):
+            tile = held([P, 4 * S], F32, name)
+            for t in (2, 3):
                 for mic in range(2):
-                    mixed[(z, t, mic)] = held([P, S], F32, "win%d%d%d" % (z, t, mic))
-                    nc.vector.scalar_tensor_tensor(
-                        mixed[(z, t, mic)][:], proj[(z, t)][:], wr[mic][:, t : t + 1], cross[(1 - z, t, mic)][:], MULT, ADD
-                    )
+                    at = (2 * (t - 2) + mic) * S
+                    cross[(i, t, mic)] = tile[:, at : at + S]
+                    nc.scalar.activation(cross[(i, t, mic)], proj[(i, t)][:], COPY, scale=w_cross[i][mic][:, t : t + 1])
 
-        def add_term(term, t, z, j0, n):
-            u, e = divmod(t, 2)
-            for c in range(j0 // CH, (j0 + n) // CH):
-                if (c, u) not in sums:
-                    sums[(c, u)] = bank(SUM_BANK[(c, u)])
-                    count[(c, u)] = 0
-                nc.tensor.matmul(
-                    sums[(c, u)][:, (2 * z + e) * P : (2 * z + e + 1) * P],
-                    lhsT=term[:, c * CH - j0 : (c + 1) * CH - j0], rhs=ident[:], is_transpose=True,
-                    start=(count[(c, u)] == 0), stop=(count[(c, u)] == TERMS_IN_BANK[u] - 1),
+        def combine(z, t, names):
+            for mic in range(2):
+                mixed[(z, t, mic)] = held([P, S], F32, names[mic])
+                nc.vector.scalar_tensor_tensor(
+                    mixed[(z, t, mic)][:], proj[(z, t)][:], wr[mic][:, t : t + 1], cross[(1 - z, t, mic)], MULT, ADD
                 )
-                count[(c, u)] = count[(c, u)] + 1
 
-        lookups = [(i, t, mic) for i in range(2) for t in range(2) for mic in range(2)]
+        def add_term(term, t, z, chunks):
+            for c in chunks:
+                if c not in sums:
+                    sums[c] = bank(SUM_BANK[c])
+                    count[c] = 0
+                nc.tensor.matmul(
+                    sums[c][:, (2 * z + t) * P : (2 * z + t + 1) * P],
+                    lhsT=term[:, c * CH : (c + 1) * CH], rhs=ident[:], is_transpose=True,
+                    start=(count[c] == 0), stop=(count[c] == TERMS_IN_BANK - 1),
+                )
+                count[c] = count[c] + 1
 
-        def gather_plain(k):
-            i, t, mic = lookups[k]
-            nc.vector.tensor_copy(picked[k], wide[(i, t)][:].indirect(lists[mic][:]))
+        def look_up(dst, i, t, mic):
+            nc.vector.tensor_copy(dst, window[(i, t)][:].indirect(lists[mic][:]))
 
-        def weigh(k):
-            i, t, mic = lookups[k]
-            terms = held([P, 2 * S], F32, "wide11" if k == FIRST_ON_GPSIMD else "terms%d" % k)
+        def weigh(src, i, t, mic, on_gpsimd):
+            terms = held([P, 2 * S], F32, "terms%d%d%d" % (i, t, mic))
             for z in range(2):
                 w = wr[mic] if z == i else w_cross[i][mic]
                 term = terms[:, z * S : (z + 1) * S]
-                if k >= FIRST_ON_GPSIMD:
-                    nc.gpsimd.tensor_scalar(term, picked[k], w[:, t : t + 1], 0.0, MULT, ADD)
+                if on_gpsimd[z]:
+                    nc.gpsimd.tensor_scalar(term, src, w[:, t : t + 1], 0.0, MULT, ADD)
                 else:
-                    nc.scalar.activation(term, picked[k], COPY, scale=w[:, t : t + 1])
-                add_term(term, t, z, 0, S)
+                    nc.scalar.activation(term, src, COPY, scale=w[:, t : t + 1])
+                add_term(term, t, z, range(4))
 
-        def gather_mixed(t, j0, n, name):
-            tile = held([P, 4 * n], F32, name)
-            for z in range(2):
-                for mic in range(2):
-                    piece = tile[:, (2 * z + mic) * n : (2 * z + mic + 1) * n]
-                    offsets = lists[mic][:, j0 // 16 : (j0 + n) // 16]
-                    nc.vector.tensor_copy(piece, mixed[(z, t, mic)][:].indirect(offsets))
-                    add_term(piece, t, z, j0, n)
+        z_in, z_high, out_bf, dealt_scales = {}, {}, {}, {}
 
-        z_last = held([P, 2 * LANES * CH], F32, "zlast")
-        back, z_in, out_bf, w34_scales_dealt = {}, {}, {}, {}
-
-        def turn_back(c, u):
-            pairs = held([P, H], BF16, "zb%d%d" % (c, u))
+        def low_lanes(c):
+            pairs = held([P, H], BF16, "zb%d" % c)
             nc.scalar.copy(
                 pairs[:].rearrange("j (z p e) -> j z p e", z=2, e=2),
-                sums[(c, u)][:].rearrange("j (z e p) -> j z p e", z=2, e=2),
+                sums[c][:].rearrange("j (z e p) -> j z p e", z=2, e=2),
             )
             words = pairs[:].bitcast(F32)
-            if u == 0:
-                back[c] = bank(BACK_BANK[c])
+            back = bank(SUM_BANK[c])
             for z in range(2):
-                nc.tensor.transpose(back[c][:, (2 * z + u) * P : (2 * z + u + 1) * P], words[:, z * P : (z + 1) * P], ident[:])
-
-        def close_sums(c):
-            turn_back(c, 1)
-
-        def interleave(c):
+                nc.tensor.transpose(back[:, z * P : (z + 1) * P], words[:, z * P : (z + 1) * P], ident[:])
             z_in[c] = held([P, 2 * H], BF16, "zq%d" % c)
-            nc.scalar.copy(
-                z_in[c][:].bitcast(F32).rearrange("p (z j u) -> p z j u", z=2, u=2),
-                back[c][:].rearrange("p (z u j) -> p z j u", z=2, u=2),
+            nc.scalar.copy(z_in[c][:].bitcast(F32).rearrange("p (n u) -> p n u", u=2)[:, :, 0], back[:, 0 : 2 * P])
+
+        def high_lanes(c, z, first_name, sum_name):
+            cols = slice(c * CH // 16, (c + 1) * CH // 16)
+            first = held([P, 2 * CH], F32, first_name)
+            for e in range(2):
+                nc.vector.tensor_copy(first[:, e * CH : (e + 1) * CH], mixed[(z, 2 + e, 0)][:].indirect(lists[0][:, cols]))
+            z_high[(c, z)] = held([P, 2 * CH], F32, sum_name)
+            for e in range(2):
+                nc.vector.tensor_tensor(
+                    z_high[(c, z)][:, e * CH : (e + 1) * CH], mixed[(z, 2 + e, 1)][:].indirect(lists[1][:, cols]),
+                    first[:, e * CH : (e + 1) * CH], ADD,
+                )
+
+        def round_high(c, z, move):
+            move(
+                z_in[c][:, z * H : (z + 1) * H].rearrange("p (j t) -> p j t", t=LANES)[:, :, 2:4],
+                z_high[(c, z)][:].rearrange("p (e j) -> p j e", e=2),
             )
 
-        def out_lane(res, t, z_codes, z_scales):
-            for z in range(2):
-                nc.tensor.matmul_mx(
-                    out=res,
-                    lhsT=w34_dealt[z][:, 2 * P * t : 2 * P * (t + 1)].bitcast(FP4X4),
-                    lhsT_scale=w34_scales_dealt[0][:, z * N + t * P : z * N + (t + 1) * P],
-                    rhs=z_codes[:, z * CH : (z + 1) * CH].bitcast(FP8X4), rhs_scale=z_scales[:, z * CH : (z + 1) * CH],
-                    start=(z == 0), stop=(z == 1),
-                )
+        def out_pass(res, t, z, z_codes, z_scales):
+            nc.tensor.matmul_mx(
+                out=res,
+                lhsT=w34_dealt[z][:, 2 * P * t : 2 * P * (t + 1)].bitcast(FP4X4),
+                lhsT_scale=dealt_scales[0][:, z * N + t * P : z * N + (t + 1) * P],
+                rhs=z_codes[:, z * CH : (z + 1) * CH].bitcast(FP8X4), rhs_scale=z_scales[:, z * CH : (z + 1) * CH],
+                start=(z == 0), stop=(z == 1),
+            )
 
         def multiply(c):
             z_codes = held([P, 2 * CH], U32, "zc%d" % c)
@@ -235,12 +232,13 @@ def tile_picked_beamf_none_po_kernel(
             nc.vector.quantize_mx(out=z_codes[:].bitcast(FP8X4), scales=z_scales[:], in_=z_in[c][:])
             res = bank(OUT_BANK[c])
             for t in range(LANES):
-                out_lane(res[:, t * CH : (t + 1) * CH], t, z_codes, z_scales)
+                for z in range(2):
+                    out_pass(res[:, t * CH : (t + 1) * CH], t, z, z_codes, z_scales)
             out_bf[c] = held([P, LANES * CH], BF16, "ob%d" % c)
             out_f32 = held([P, LANES * CH], F32, "of%d" % c)
-            nc.scalar.copy(out_bf[c][:].rearrange("p (j t) -> p j t", t=LANES), res[:].rearrange("p (t j) -> p j t", t=LANES))
             nc.scalar.copy(out_f32[:], res[:])
             nc.sync.dma_start(out_rows[:, :, c * CH : (c + 1) * CH], out_f32[:].rearrange("p (t j) -> p t j", t=LANES))
+            nc.scalar.copy(out_bf[c][:].rearrange("p (j t) -> p j t", t=LANES), res[:].rearrange("p (t j) -> p j t", t=LANES))
 
         def hand_on(c):
             cols = slice(c * CH, (c + 1) * CH)
@@ -249,122 +247,108 @@ def tile_picked_beamf_none_po_kernel(
                 done = slice((c - 1) * CH, (c + 1) * CH)
                 nc.sync.dma_start(out_words[:, done], out_codes[:, done].bitcast(I32))
 
-        def last_low_lanes():
-            turned = held([P, H], F32, "zt3")
-            nc.scalar.copy(turned[:], sums[(LAST, 0)][:])
-            res = bank(BACK_BANK[LAST])
-            for b in range(4):
-                nc.tensor.transpose(res[:, b * P : (b + 1) * P], turned[:, b * P : (b + 1) * P], ident[:])
-            nc.scalar.copy(
-                z_last[:].rearrange("p (z t j) -> p z t j", z=2, t=LANES)[:, :, 0:2, :],
-                res[:].rearrange("p (z e j) -> p z e j", z=2, e=2),
-            )
+        last = {}
 
-        def last_high_lanes(z, name, move):
-            cols = slice(LAST * CH // 16, (LAST + 1) * CH // 16)
-            first = held([P, 2 * CH], F32, name)
-            for e in range(2):
-                nc.vector.tensor_copy(first[:, e * CH : (e + 1) * CH], mixed[(z, 2 + e, 0)][:].indirect(lists[0][:, cols]))
-            for e in range(2):
-                at = (z * LANES + 2 + e) * CH
-                nc.vector.tensor_tensor(
-                    z_last[:, at : at + CH], mixed[(z, 2 + e, 1)][:].indirect(lists[1][:, cols]),
-                    first[:, e * CH : (e + 1) * CH], ADD,
-                )
-            z_in[(LAST, z)] = held([P, H], BF16, "zq3%d" % z)
-            move(
-                z_in[(LAST, z)][:].rearrange("p (j t) -> p j t", t=LANES),
-                z_last[:, z * H : (z + 1) * H].rearrange("p (t j) -> p j t", t=LANES),
+        def last_passes(z):
+            if z == 0:
+                last["codes"] = held([P, 2 * CH], U32, "zc3")
+                last["scales"] = held([P, 2 * CH], U8, "zs3")
+            cols = slice(z * CH, (z + 1) * CH)
+            nc.vector.quantize_mx(
+                out=last["codes"][:, cols].bitcast(FP8X4), scales=last["scales"][:, cols], in_=z_in[LAST][:, z * H : (z + 1) * H]
             )
+            for t in range(LANES):
+                if z == 0:
+                    last[t] = bank(LAST_OUT_BANK[t])
+                out_pass(last[t][:, 0:CH], t, z, last["codes"], last["scales"])
 
-        def last_multiply():
-            z_codes = held([P, 2 * CH], U32, "zc3")
-            z_scales = held([P, 2 * CH], U8, "zs3")
-            for z in range(2):
-                cols = slice(z * CH, (z + 1) * CH)
-                nc.vector.quantize_mx(out=z_codes[:, cols].bitcast(FP8X4), scales=z_scales[:, cols], in_=z_in[(LAST, z)][:])
+        def last_out():
+            out_f32 = held([P, LANES * CH], F32, "of3")
+            for t in range(LANES):
+                move = nc.scalar.copy if t % 2 == 0 else nc.vector.tensor_copy
+                move(out_f32[:, t * CH : (t + 1) * CH], last[t][:, 0:CH])
+            nc.sync.dma_start(out_rows[:, :, LAST * CH : (LAST + 1) * CH], out_f32[:].rearrange("p (t j) -> p t j", t=LANES))
             out_bf[LAST] = held([P, LANES * CH], BF16, "ob3")
-            for u in range(2):
-                res = bank(LAST_OUT_BANK[u])
-                for e in range(2):
-                    out_lane(res[:, e * CH : (e + 1) * CH], 2 * u + e, z_codes, z_scales)
-                nc.vector.tensor_copy(
-                    out_bf[LAST][:].rearrange("p (j t) -> p j t", t=LANES)[:, :, 2 * u : 2 * u + 2],
-                    res[:, 0 : 2 * CH].rearrange("p (e j) -> p j e", e=2),
-                )
-                out_f32 = held([P, 2 * CH], F32, "of3%d" % u)
-                nc.scalar.copy(out_f32[:], res[:, 0 : 2 * CH])
-                nc.sync.dma_start(
-                    out_rows[:, 2 * u : 2 * u + 2, LAST * CH : (LAST + 1) * CH], out_f32[:].rearrange("p (e j) -> p e j", e=2)
-                )
+            nc.vector.tensor_copy(out_bf[LAST][:].rearrange("p (j t) -> p j t", t=LANES), out_f32[:].rearrange("p (t j) -> p j t", t=LANES))
 
-        regroup(0, 0, nc.scalar.copy, 0, LANES)
-        regroup(0, 1, nc.vector.tensor_copy, 0, 1)
-        regroup(0, 1, nc.vector.tensor_copy, 1, LANES)
-        regroup(1, 0, nc.scalar.copy, 0, LANES)
-        for t in range(LANES):
+        def slot(name):
+            return held([P, S], F32, name)[:]
+
+        for u in range(2):
+            grouped[(0, u)] = held([P, 2 * H], BF16, "grouped%d" % u)
+        regroup(0, 0, nc.vector.tensor_copy)
+        regroup(0, 1, nc.scalar.copy)
+        quantise_w(0, 0, 2)
+        quantise_w(0, 2, LANES)
+        for h in range(2):
+            nc.vector.tensor_copy(
+                xg_words[:, h * HALF : (h + 1) * HALF], xw[:].bitcast(U32).indirect(offs_t[:, h * HALF // 16 : (h + 1) * HALF // 16])
+            )
+            project(0, 0, h * HALF, HALF)
+            fill(0, 0, h * HALF, HALF)
+        for t in range(1, LANES):
             project(0, t)
-        for t in range(2):
-            nc.scalar.copy(wide[(0, t)][:, 0:S], proj[(0, t)][:])
-        picked[0] = held([P, S], F32, "pick0")[:]
-        gather_plain(0)
-        regroup(1, 1, nc.vector.tensor_copy, 0, LANES)
-        for t in range(LANES):
-            project(1, t)
-        after_w2 = held([P, 2 * S], F32, "grouped1")
-        picked[1] = after_w2[:, 0:S]
-        picked[2] = after_w2[:, S : 2 * S]
-        for k in range(3, len(lookups)):
-            picked[k] = held([P, S], F32, "pick%d" % k)[:]
-        for t in range(2):
-            nc.scalar.copy(wide[(1, t)][:, 0:S], proj[(1, t)][:])
-        for k in range(1, len(lookups)):
-            gather_plain(k)
-
-        cross_terms(0, 2)
-        for k in range(WEIGHED_BEFORE_LANE_2):
-            weigh(k)
-        cross_terms(1, 2)
-        combine(2)
-        for k in range(WEIGHED_BEFORE_LANE_2, len(lookups)):
-            weigh(k)
-        gather_mixed(2, 0, 2 * CH, "pick5")
-        w34_scales_dealt[0] = held([P, 2 * N], U8, "pick5")
+        fill(0, 1)
+        for i in range(2):
+            deal_words(i)
+        picked = {}
+        for k in range(2):
+            picked[k] = slot("ring%d" % k)
+            look_up(picked[k], 0, 0, k)
+        for u in range(2):
+            grouped[(1, u)] = held([P, 2 * H], BF16, "grouped%d" % u)
+            regroup(1, u, nc.scalar.copy)
+        for u in range(2):
+            quantise_w(1, 2 * u, 2 * u + 2)
+            if u == 0:
+                for t in range(2):
+                    project(1, t)
+                    fill(1, t)
+            else:
+                for t in (2, 3):
+                    project(1, t)
+            picked[2 + u] = slot("grouped%d" % u)
+            look_up(picked[2 + u], 0, 1, u)
+        for k in range(4):
+            weigh(picked[k], 0, k // 2, k % 2, (True, True))
+        cross_terms(1, "cross1")
+        cross_terms(0, "raw1")
+        for k in range(4, 8):
+            picked[k] = slot(("ring2", "ring0", "ring1", "grouped0")[k - 4])
+            look_up(picked[k], 1, k // 2 % 2, k % 2)
+        for k in range(4, 8):
+            weigh(picked[k], 1, k // 2 % 2, k % 2, (True, k < 6))
+        combine(0, 2, ("ring0", "mixed021"))
+        combine(0, 3, ("ring1", "mixed031"))
+        combine(1, 2, ("grouped0", "mixed121"))
+        combine(1, 3, ("mixed130", "mixed131"))
+        dealt_scales[0] = held([P, 2 * N], U8, "cross1")
         nc.gpsimd.tensor_copy(
-            w34_scales_dealt[0][:].rearrange("p (w t m) -> p w t m", w=2, t=LANES),
+            dealt_scales[0][:].rearrange("p (w t m) -> p w t m", w=2, t=LANES),
             w34_scales[:].rearrange("p (w m t) -> p w t m", w=2, t=LANES),
         )
-        cross_terms(1, 3)
-        cross_terms(0, 3)
-        combine(3)
-        for c in range(LAST):
-            turn_back(c, 0)
-        gather_mixed(3, 0, CH, "run10")
-        gather_mixed(3, CH, CH, "run11")
-
-        close_sums(0)
-
-        close_sums(1)
-        gather_mixed(2, 2 * CH, CH, "run10")
-        gather_mixed(3, 2 * CH, CH, "run11")
-        interleave(0)
-        last_low_lanes()
-
-        close_sums(2)
-        interleave(1)
-        multiply(0)
-
-        interleave(2)
-        last_high_lanes(0, "zq0", nc.scalar.copy)
-        multiply(1)
-        hand_on(0)
-
-        multiply(2)
-        last_high_lanes(1, "ob0", nc.vector.tensor_copy)
-        hand_on(1)
-        last_multiply()
-
+        low_lanes(0)
+        low_lanes(1)
+        names = {}
+        for c in range(4):
+            for z in range(2):
+                names[(c, z)] = "zc%d" % (c - 2) if c >= 2 and z == 1 else "high%d%d" % (c, z)
+        for c in range(4):
+            high_lanes(c, 0, "zb0" if c == 0 else names[(c - 1, 0)], names[(c, 0)])
+            if c > 0:
+                round_high(c - 1, 1, nc.scalar.copy)
+                multiply(c - 1)
+            round_high(c, 0, nc.scalar.copy)
+            high_lanes(c, 1, "zb1" if c == 0 else names[(c - 1, 1)], names[(c, 1)])
+            if c < 2:
+                low_lanes(c + 2)
+            if c > 1:
+                hand_on(c - 2)
+        last_passes(0)
+        round_high(LAST, 1, nc.vector.tensor_copy)
+        last_passes(1)
         hand_on(2)
+        last_out()
         hand_on(LAST)
 
         for q in range(4):

@@ -69,19 +69,17 @@ def tile_picked_beamf_none_po_kernel(
 
         w_rows = [w.rearrange("(p j) c -> p j c", j=LANES) for w in (w1, w2)]
         nc.sync.dma_start(offs_t[:], offs)
+        nc.sync.dma_start(raw[0][:], w_rows[0])
         for q in range(4):
             nc.sync.dma_start(xs[32 * q : 32 * q + 4, :].bitcast(I32), x_scales[0, 4 * q : 4 * q + 4, :].bitcast(I32))
-        nc.sync.dma_start(raw[0][:], w_rows[0])
         nc.sync.dma_start(xw[:], x_words[0].rearrange("p c r -> p (c r)").bitcast(I32))
+        nc.sync.dma_start(m1_t[:], m1)
+        nc.sync.dma_start(raw[1][:], w_rows[1])
+        nc.sync.dma_start(m2_t[:], m2)
+        for name, src in (("wr1", wr1), ("wi1", wi1), ("wr2", wr2), ("wi2", wi2)):
+            nc.sync.dma_start(wt[name][:], src.rearrange("(p t) o -> p (t o)", t=LANES))
         nc.sync.dma_start(w34_words[0][:].bitcast(I32), w3_words[0].bitcast(I32))
         nc.sync.dma_start(w34_words[1][:].bitcast(I32), w4_words[0].bitcast(I32))
-        nc.sync.dma_start(m1_t[:], m1)
-        nc.sync.dma_start(m2_t[:], m2)
-        for name, src in (("wr1", wr1), ("wi1", wi1)):
-            nc.sync.dma_start(wt[name][:], src.rearrange("(p t) o -> p (t o)", t=LANES))
-        nc.sync.dma_start(raw[1][:], w_rows[1])
-        for name, src in (("wr2", wr2), ("wi2", wi2)):
-            nc.sync.dma_start(wt[name][:], src.rearrange("(p t) o -> p (t o)", t=LANES))
         make_identity(nc, ident[:])
         for i, src in enumerate((w3_scales, w4_scales)):
             for q in range(4):
@@ -95,12 +93,13 @@ def tile_picked_beamf_none_po_kernel(
         wr = (wt["wr1"], wt["wr2"])
         w_cross = ((wt["wi1"], wt["wi2"]), (wt["nwi1"], wt["nwi2"]))
 
-        w34_dealt = [held([P, 2 * N], U8, "w3d"), held([P, 2 * N], U8, "w4d")]
+        w34_dealt = {}
 
-        def deal_words(i):
-            nc.vector.tensor_copy(
-                w34_dealt[i][:].rearrange("p (t m e) -> p m t e", t=LANES, e=2),
-                w34_words[i][:].rearrange("p (m t e) -> p m t e", t=LANES, e=2),
+        def deal_words(i, name):
+            w34_dealt[i] = held([P, 2 * N], U8, name)
+            nc.gpsimd.tensor_copy(
+                w34_dealt[i][:].rearrange("p (t m e) -> p t m e", t=LANES, e=2),
+                w34_words[i][:].rearrange("p (m t e) -> p t m e", t=LANES, e=2),
             )
 
         xg_words = held([P, S], U32, "xgw")
@@ -143,13 +142,9 @@ def tile_picked_beamf_none_po_kernel(
 
         cross, mixed, sums, count = {}, {}, {}, {}
 
-        def cross_terms(i, name):
-            tile = held([P, 4 * S], F32, name)
-            for t in (2, 3):
-                for mic in range(2):
-                    at = (2 * (t - 2) + mic) * S
-                    cross[(i, t, mic)] = tile[:, at : at + S]
-                    nc.scalar.activation(cross[(i, t, mic)], proj[(i, t)][:], COPY, scale=w_cross[i][mic][:, t : t + 1])
+        def cross_term(i, t, mic, dst):
+            cross[(i, t, mic)] = dst
+            nc.scalar.activation(cross[(i, t, mic)], proj[(i, t)][:], COPY, scale=w_cross[i][mic][:, t : t + 1])
 
         def combine(z, t, names):
             for mic in range(2):
@@ -173,18 +168,17 @@ def tile_picked_beamf_none_po_kernel(
         def look_up(dst, i, t, mic):
             nc.vector.tensor_copy(dst, window[(i, t)][:].indirect(lists[mic][:]))
 
-        def weigh(src, i, t, mic, on_gpsimd):
-            terms = held([P, 2 * S], F32, "terms%d%d%d" % (i, t, mic))
+        def weigh(src, i, t, mic, on_gpsimd, names):
             for z in range(2):
                 w = wr[mic] if z == i else w_cross[i][mic]
-                term = terms[:, z * S : (z + 1) * S]
+                term = names[z]
                 if on_gpsimd[z]:
                     nc.gpsimd.tensor_scalar(term, src, w[:, t : t + 1], 0.0, MULT, ADD)
                 else:
                     nc.scalar.activation(term, src, COPY, scale=w[:, t : t + 1])
                 add_term(term, t, z, range(4))
 
-        z_in, z_high, out_bf, dealt_scales = {}, {}, {}, {}
+        z_in, z_high, out_bf, dealt_scales, back, result = {}, {}, {}, {}, {}, {}
 
         def low_lanes(c):
             pairs = held([P, H], BF16, "zb%d" % c)
@@ -193,28 +187,33 @@ def tile_picked_beamf_none_po_kernel(
                 sums[c][:].rearrange("j (z e p) -> j z p e", z=2, e=2),
             )
             words = pairs[:].bitcast(F32)
-            back = bank(SUM_BANK[c])
+            back[c] = bank(SUM_BANK[c])
             for z in range(2):
-                nc.tensor.transpose(back[:, z * P : (z + 1) * P], words[:, z * P : (z + 1) * P], ident[:])
-            z_in[c] = held([P, 2 * H], BF16, "zq%d" % c)
-            nc.scalar.copy(z_in[c][:].bitcast(F32).rearrange("p (n u) -> p n u", u=2)[:, :, 0], back[:, 0 : 2 * P])
+                nc.tensor.transpose(back[c][:, z * P : (z + 1) * P], words[:, z * P : (z + 1) * P], ident[:])
 
-        def high_lanes(c, z, first_name, sum_name):
-            cols = slice(c * CH // 16, (c + 1) * CH // 16)
-            first = held([P, 2 * CH], F32, first_name)
+        def place_low(c):
+            z_in[c] = held([P, 2 * H], BF16, "zb%d" % c)
+            nc.scalar.copy(z_in[c][:].bitcast(F32).rearrange("p (n u) -> p n u", u=2)[:, :, 0], back[c][:, 0 : 2 * P])
+
+        def high_lanes(c, chunks, z, first_name, sum_name):
+            n = chunks * CH
+            cols = slice(c * CH // 16, (c * CH + n) // 16)
+            first = held([P, 2 * n], F32, first_name)
             for e in range(2):
-                nc.vector.tensor_copy(first[:, e * CH : (e + 1) * CH], mixed[(z, 2 + e, 0)][:].indirect(lists[0][:, cols]))
-            z_high[(c, z)] = held([P, 2 * CH], F32, sum_name)
+                nc.vector.tensor_copy(first[:, e * n : (e + 1) * n], mixed[(z, 2 + e, 0)][:].indirect(lists[0][:, cols]))
+            total = held([P, 2 * n], F32, sum_name)
             for e in range(2):
                 nc.vector.tensor_tensor(
-                    z_high[(c, z)][:, e * CH : (e + 1) * CH], mixed[(z, 2 + e, 1)][:].indirect(lists[1][:, cols]),
-                    first[:, e * CH : (e + 1) * CH], ADD,
+                    total[:, e * n : (e + 1) * n], mixed[(z, 2 + e, 1)][:].indirect(lists[1][:, cols]),
+                    first[:, e * n : (e + 1) * n], ADD,
                 )
+            for d in range(chunks):
+                z_high[(c + d, z)] = total[:].rearrange("p (e j) -> p j e", e=2)[:, d * CH : (d + 1) * CH, :]
 
         def round_high(c, z, move):
             move(
                 z_in[c][:, z * H : (z + 1) * H].rearrange("p (j t) -> p j t", t=LANES)[:, :, 2:4],
-                z_high[(c, z)][:].rearrange("p (e j) -> p j e", e=2),
+                z_high[(c, z)],
             )
 
         def out_pass(res, t, z, z_codes, z_scales):
@@ -238,13 +237,16 @@ def tile_picked_beamf_none_po_kernel(
             out_f32 = held([P, LANES * CH], F32, "of%d" % c)
             nc.scalar.copy(out_f32[:], res[:])
             nc.sync.dma_start(out_rows[:, :, c * CH : (c + 1) * CH], out_f32[:].rearrange("p (t j) -> p t j", t=LANES))
-            nc.scalar.copy(out_bf[c][:].rearrange("p (j t) -> p j t", t=LANES), res[:].rearrange("p (t j) -> p j t", t=LANES))
+            result[c] = res
+
+        def round_out(c):
+            nc.scalar.copy(out_bf[c][:].rearrange("p (j t) -> p j t", t=LANES), result[c][:].rearrange("p (t j) -> p j t", t=LANES))
 
         def hand_on(c):
             cols = slice(c * CH, (c + 1) * CH)
             nc.vector.quantize_mx(out=out_codes[:, cols].bitcast(FP8X4), scales=out_scales[:, cols], in_=out_bf[c][:])
-            if c % 2 == 1:
-                done = slice((c - 1) * CH, (c + 1) * CH)
+            if c > 0:
+                done = slice((c - 1) * CH, (c + 1) * CH) if c == 1 else cols
                 nc.sync.dma_start(out_words[:, done], out_codes[:, done].bitcast(I32))
 
         last = {}
@@ -289,8 +291,6 @@ def tile_picked_beamf_none_po_kernel(
         for t in range(1, LANES):
             project(0, t)
         fill(0, 1)
-        for i in range(2):
-            deal_words(i)
         picked = {}
         for k in range(2):
             picked[k] = slot("ring%d" % k)
@@ -298,55 +298,69 @@ def tile_picked_beamf_none_po_kernel(
         for u in range(2):
             grouped[(1, u)] = held([P, 2 * H], BF16, "grouped%d" % u)
             regroup(1, u, nc.scalar.copy)
-        for u in range(2):
-            quantise_w(1, 2 * u, 2 * u + 2)
-            if u == 0:
-                for t in range(2):
-                    project(1, t)
-                    fill(1, t)
-            else:
-                for t in (2, 3):
-                    project(1, t)
-            picked[2 + u] = slot("grouped%d" % u)
-            look_up(picked[2 + u], 0, 1, u)
-        for k in range(4):
-            weigh(picked[k], 0, k // 2, k % 2, (True, True))
-        cross_terms(1, "cross1")
-        cross_terms(0, "raw1")
+        picked = [picked[0], picked[1]]
+        quantise_w(1, 0, 2)
+        for t in range(2):
+            project(1, t)
+            fill(1, t)
+        after = [held([P, 2 * S], F32, "grouped0")]
+        picked.append(after[0][:, 0:S])
+        look_up(picked[2], 0, 1, 0)
+        quantise_w(1, 2, LANES)
+        for t in (2, 3):
+            project(1, t)
+        after.append(held([P, 2 * S], F32, "grouped1"))
+        picked.append(after[1][:, 0:S])
+        look_up(picked[3], 0, 1, 1)
         for k in range(4, 8):
-            picked[k] = slot(("ring2", "ring0", "ring1", "grouped0")[k - 4])
+            picked.append(slot("pick%d" % k))
             look_up(picked[k], 1, k // 2 % 2, k % 2)
-        for k in range(4, 8):
-            weigh(picked[k], 1, k // 2 % 2, k % 2, (True, k < 6))
-        combine(0, 2, ("ring0", "mixed021"))
-        combine(0, 3, ("ring1", "mixed031"))
-        combine(1, 2, ("grouped0", "mixed121"))
-        combine(1, 3, ("mixed130", "mixed131"))
-        dealt_scales[0] = held([P, 2 * N], U8, "cross1")
+        for i, name in ((1, "cross1"), (0, "raw1")):
+            four = held([P, 4 * S], F32, name)
+            for n in range(4):
+                cross_term(i, 2 + n // 2, n % 2, four[:, n * S : (n + 1) * S])
+        for k in range(8):
+            names = [slot("term%d%d" % (k, z)) for z in range(2)]
+            if k < 2:
+                names[1 - k] = after[k][:, S : 2 * S]
+            weigh(picked[k], k // 4, k // 2 % 2, k % 2, (k < 7, k < 4), names)
+        for z in range(2):
+            for t in (2, 3):
+                combine(z, t, ("mixed%d%d0" % (z, t), "mixed%d%d1" % (z, t)))
+        deal_words(0, "pick6")
+        deal_words(1, "term50")
+        dealt_scales[0] = held([P, 2 * N], U8, "term60")
         nc.gpsimd.tensor_copy(
             dealt_scales[0][:].rearrange("p (w t m) -> p w t m", w=2, t=LANES),
             w34_scales[:].rearrange("p (w m t) -> p w t m", w=2, t=LANES),
         )
-        low_lanes(0)
-        low_lanes(1)
-        names = {}
         for c in range(4):
-            for z in range(2):
-                names[(c, z)] = "zc%d" % (c - 2) if c >= 2 and z == 1 else "high%d%d" % (c, z)
-        for c in range(4):
-            high_lanes(c, 0, "zb0" if c == 0 else names[(c - 1, 0)], names[(c, 0)])
-            if c > 0:
-                round_high(c - 1, 1, nc.scalar.copy)
-                multiply(c - 1)
-            round_high(c, 0, nc.scalar.copy)
-            high_lanes(c, 1, "zb1" if c == 0 else names[(c - 1, 1)], names[(c, 1)])
-            if c < 2:
-                low_lanes(c + 2)
-            if c > 1:
-                hand_on(c - 2)
+            low_lanes(c)
+        place_low(0)
+        place_low(1)
+        for z in range(2):
+            high_lanes(0, 2, z, "first%d" % z, "high%d" % z)
+            for c in range(2):
+                round_high(c, z, nc.scalar.copy)
+            place_low(2 + z)
+        high_lanes(2, 1, 0, "first20", "high20")
+        multiply(0)
+        multiply(1)
+        round_high(2, 0, nc.scalar.copy)
+        high_lanes(2, 1, 1, "high1", "high21")
+        round_high(2, 1, nc.scalar.copy)
+        high_lanes(LAST, 1, 0, "zc0", "high30")
+        multiply(2)
+        round_high(LAST, 0, nc.scalar.copy)
+        round_out(0)
+        round_out(1)
+        hand_on(0)
+        high_lanes(LAST, 1, 1, "high21", "high31")
         last_passes(0)
         round_high(LAST, 1, nc.vector.tensor_copy)
         last_passes(1)
+        hand_on(1)
+        round_out(2)
         hand_on(2)
         last_out()
         hand_on(LAST)

@@ -71,7 +71,7 @@ def tile_picked_beamf_none_po_kernel(
         nc.sync.dma_start(offs_t[:], offs)
         nc.sync.dma_start(raw[0][:], w_rows[0])
         for q in range(4):
-            nc.sync.dma_start(xs[32 * q : 32 * q + 4, :].bitcast(I32), x_scales[0, 4 * q : 4 * q + 4, :].bitcast(I32))
+            nc.sync.dma_start(xs[q:P:32, :].bitcast(I32), x_scales[0, q:16:4, :].bitcast(I32))
         nc.sync.dma_start(xw[:], x_words[0].rearrange("p c r -> p (c r)").bitcast(I32))
         nc.sync.dma_start(m1_t[:], m1)
         nc.sync.dma_start(raw[1][:], w_rows[1])
@@ -84,8 +84,8 @@ def tile_picked_beamf_none_po_kernel(
         for i, src in enumerate((w3_scales, w4_scales)):
             for q in range(4):
                 nc.sync.dma_start(
-                    w34_scales[32 * q : 32 * q + 4, i * N : (i + 1) * N].bitcast(I32),
-                    src[0, 4 * q : 4 * q + 4, :].bitcast(I32),
+                    w34_scales[q:P:32, i * N : (i + 1) * N].bitcast(I32),
+                    src[0, q:16:4, :].bitcast(I32),
                 )
         nc.gpsimd.tensor_scalar(wt["nwi1"][:], wt["wi1"][:], -1.0, 0.0, MULT, ADD)
         nc.gpsimd.tensor_scalar(wt["nwi2"][:], wt["wi2"][:], -1.0, 0.0, MULT, ADD)
@@ -195,20 +195,30 @@ def tile_picked_beamf_none_po_kernel(
             z_in[c] = held([P, 2 * H], BF16, "zb%d" % c)
             nc.scalar.copy(z_in[c][:].bitcast(F32).rearrange("p (n u) -> p n u", u=2)[:, :, 0], back[c][:, 0 : 2 * P])
 
-        def high_lanes(c, chunks, z, first_name, sum_name):
+        first = {}
+
+        def fetch_first(c, chunks, z, name):
             n = chunks * CH
-            cols = slice(c * CH // 16, (c * CH + n) // 16)
-            first = held([P, 2 * n], F32, first_name)
+            first[(c, z)] = held([P, 2 * n], F32, name)
             for e in range(2):
-                nc.vector.tensor_copy(first[:, e * n : (e + 1) * n], mixed[(z, 2 + e, 0)][:].indirect(lists[0][:, cols]))
-            total = held([P, 2 * n], F32, sum_name)
+                offsets = lists[0][:, c * CH // 16 : (c * CH + n) // 16]
+                nc.vector.tensor_copy(first[(c, z)][:, e * n : (e + 1) * n], mixed[(z, 2 + e, 0)][:].indirect(offsets))
+
+        def add_second(c, chunks, z, name):
+            n = chunks * CH
+            total = held([P, 2 * n], F32, name)
             for e in range(2):
+                offsets = lists[1][:, c * CH // 16 : (c * CH + n) // 16]
                 nc.vector.tensor_tensor(
-                    total[:, e * n : (e + 1) * n], mixed[(z, 2 + e, 1)][:].indirect(lists[1][:, cols]),
-                    first[:, e * n : (e + 1) * n], ADD,
+                    total[:, e * n : (e + 1) * n], mixed[(z, 2 + e, 1)][:].indirect(offsets),
+                    first[(c, z)][:, e * n : (e + 1) * n], ADD,
                 )
             for d in range(chunks):
                 z_high[(c + d, z)] = total[:].rearrange("p (e j) -> p j e", e=2)[:, d * CH : (d + 1) * CH, :]
+
+        def high_lanes(c, chunks, z, first_name, sum_name):
+            fetch_first(c, chunks, z, first_name)
+            add_second(c, chunks, z, sum_name)
 
         def round_high(c, z, move):
             move(
@@ -339,10 +349,13 @@ def tile_picked_beamf_none_po_kernel(
         place_low(0)
         place_low(1)
         for z in range(2):
-            high_lanes(0, 2, z, "first%d" % z, "high%d" % z)
+            fetch_first(0, 2, z, "first%d" % z)
+        for z in range(2):
+            add_second(0, 2, z, "high%d" % z)
             for c in range(2):
                 round_high(c, z, nc.scalar.copy)
-            place_low(2 + z)
+        place_low(2)
+        place_low(LAST)
         high_lanes(2, 1, 0, "first20", "high20")
         multiply(0)
         multiply(1)

@@ -29,6 +29,7 @@ SUM_BANK = (2, 3, 0, 1)
 OUT_BANK = (4, 5, 6)
 LAST_OUT_BANK = (2, 3, 0, 7)
 TERMS_IN_BANK = 16
+ASIDE = 2
 
 
 def tile_picked_beamf_none_po_kernel(
@@ -74,12 +75,12 @@ def tile_picked_beamf_none_po_kernel(
             nc.sync.dma_start(xs[q:P:32, :].bitcast(I32), x_scales[0, q:16:4, :].bitcast(I32))
         nc.sync.dma_start(xw[:], x_words[0].rearrange("p c r -> p (c r)").bitcast(I32))
         nc.sync.dma_start(m1_t[:], m1)
+        nc.sync.dma_start(w34_words[0][:].bitcast(I32), w3_words[0].bitcast(I32))
+        nc.sync.dma_start(w34_words[1][:].bitcast(I32), w4_words[0].bitcast(I32))
         nc.sync.dma_start(raw[1][:], w_rows[1])
         nc.sync.dma_start(m2_t[:], m2)
         for name, src in (("wr1", wr1), ("wi1", wi1), ("wr2", wr2), ("wi2", wi2)):
             nc.sync.dma_start(wt[name][:], src.rearrange("(p t) o -> p (t o)", t=LANES))
-        nc.sync.dma_start(w34_words[0][:].bitcast(I32), w3_words[0].bitcast(I32))
-        nc.sync.dma_start(w34_words[1][:].bitcast(I32), w4_words[0].bitcast(I32))
         make_identity(nc, ident[:])
         for i, src in enumerate((w3_scales, w4_scales)):
             for q in range(4):
@@ -146,12 +147,17 @@ def tile_picked_beamf_none_po_kernel(
             cross[(i, t, mic)] = dst
             nc.scalar.activation(cross[(i, t, mic)], proj[(i, t)][:], COPY, scale=w_cross[i][mic][:, t : t + 1])
 
-        def combine(z, t, names):
-            for mic in range(2):
-                mixed[(z, t, mic)] = held([P, S], F32, names[mic])
-                nc.vector.scalar_tensor_tensor(
-                    mixed[(z, t, mic)][:], proj[(z, t)][:], wr[mic][:, t : t + 1], cross[(1 - z, t, mic)], MULT, ADD
-                )
+        def combine(z, t, mic):
+            mixed[(z, t, mic)] = held([P, S], F32, "mixed%d%d%d" % (z, t, mic))
+            nc.vector.scalar_tensor_tensor(
+                mixed[(z, t, mic)][:], proj[(z, t)][:], wr[mic][:, t : t + 1], cross[(1 - z, t, mic)], MULT, ADD
+            )
+
+        def combine_aside(z, t, mic):
+            direct = slot("direct%d%d%d" % (z, t, mic))
+            nc.scalar.activation(direct, proj[(z, t)][:], COPY, scale=wr[mic][:, t : t + 1])
+            mixed[(z, t, mic)] = held([P, S], F32, "mixed%d%d%d" % (z, t, mic))
+            nc.gpsimd.tensor_tensor(mixed[(z, t, mic)][:], direct, cross[(1 - z, t, mic)], ADD)
 
         def add_term(term, t, z, chunks):
             for c in chunks:
@@ -301,6 +307,8 @@ def tile_picked_beamf_none_po_kernel(
         for t in range(1, LANES):
             project(0, t)
         fill(0, 1)
+        for i in range(2):
+            deal_words(i, "w%dd" % (3 + i))
         picked = {}
         for k in range(2):
             picked[k] = slot("ring%d" % k)
@@ -319,31 +327,31 @@ def tile_picked_beamf_none_po_kernel(
         quantise_w(1, 2, LANES)
         for t in (2, 3):
             project(1, t)
-        after.append(held([P, 2 * S], F32, "grouped1"))
-        picked.append(after[1][:, 0:S])
+        after.append(held([P, 5 * S], F32, "grouped1"))
+        picked.append(slot("raw1"))
         look_up(picked[3], 0, 1, 1)
         for k in range(4, 8):
             picked.append(slot("pick%d" % k))
             look_up(picked[k], 1, k // 2 % 2, k % 2)
-        for i, name in ((1, "cross1"), (0, "raw1")):
-            four = held([P, 4 * S], F32, name)
+        for i in (1, 0):
             for n in range(4):
-                cross_term(i, 2 + n // 2, n % 2, four[:, n * S : (n + 1) * S])
+                dst = slot("cross%d" % n) if i == 1 else after[1][:, (n + (n > 0)) * S : (n + (n > 0) + 1) * S]
+                cross_term(i, 2 + n % 2, n // 2, dst)
         for k in range(8):
             names = [slot("term%d%d" % (k, z)) for z in range(2)]
             if k < 2:
                 names[1 - k] = after[k][:, S : 2 * S]
             weigh(picked[k], k // 4, k // 2 % 2, k % 2, (k < 7, k < 4), names)
-        for z in range(2):
-            for t in (2, 3):
-                combine(z, t, ("mixed%d%d0" % (z, t), "mixed%d%d1" % (z, t)))
-        deal_words(0, "pick6")
-        deal_words(1, "term50")
-        dealt_scales[0] = held([P, 2 * N], U8, "term60")
+        dealt_scales[0] = held([P, 2 * N], U8, "pick5")
         nc.gpsimd.tensor_copy(
             dealt_scales[0][:].rearrange("p (w t m) -> p w t m", w=2, t=LANES),
             w34_scales[:].rearrange("p (w m t) -> p w t m", w=2, t=LANES),
         )
+        windows = [(z, t, mic) for mic in range(2) for z in range(2) for t in (2, 3)]
+        for key in windows[:-ASIDE]:
+            combine(*key)
+        for key in windows[-ASIDE:]:
+            combine_aside(*key)
         for c in range(4):
             low_lanes(c)
         place_low(0)
@@ -356,7 +364,7 @@ def tile_picked_beamf_none_po_kernel(
                 round_high(c, z, nc.scalar.copy)
         place_low(2)
         place_low(LAST)
-        high_lanes(2, 1, 0, "first20", "high20")
+        high_lanes(2, 1, 0, "direct131", "high20")
         multiply(0)
         multiply(1)
         round_high(2, 0, nc.scalar.copy)

@@ -16,6 +16,7 @@ FP8X4 = mybir.dt.float8_e4m3fn_x4
 FP4X4 = mybir.dt.float4_e2m1fn_x4
 MULT = mybir.AluOpType.mult
 ADD = mybir.AluOpType.add
+SUBTRACT = mybir.AluOpType.subtract
 COPY = mybir.ActivationFunctionType.Copy
 
 P = 128
@@ -29,7 +30,6 @@ SUM_BANK = (2, 3, 0, 1)
 OUT_BANK = (4, 5, 6)
 LAST_OUT_BANK = (2, 3, 0, 7)
 TERMS_IN_BANK = 16
-ASIDE = 2
 
 
 def tile_picked_beamf_none_po_kernel(
@@ -56,7 +56,7 @@ def tile_picked_beamf_none_po_kernel(
         w34_scales = held([P, 2 * N], U8, "w34s")
         raw = [held([P, LANES, H], F32, "raw%d" % i) for i in range(2)]
         wt = {}
-        for name in ("wr1", "wi1", "wr2", "wi2", "nwi1", "nwi2"):
+        for name in ("wr1", "wi1", "wr2", "wi2"):
             wt[name] = held([P, LANES], F32, name)
 
         nc.gpsimd.memset(xs[:].bitcast(I32), 0)
@@ -69,8 +69,8 @@ def tile_picked_beamf_none_po_kernel(
         ident = held([P, P], F32, "ident")
 
         w_rows = [w.rearrange("(p j) c -> p j c", j=LANES) for w in (w1, w2)]
-        nc.sync.dma_start(offs_t[:], offs)
         nc.sync.dma_start(raw[0][:], w_rows[0])
+        nc.sync.dma_start(offs_t[:], offs)
         for q in range(4):
             nc.sync.dma_start(xs[q:P:32, :].bitcast(I32), x_scales[0, q:16:4, :].bitcast(I32))
         nc.sync.dma_start(xw[:], x_words[0].rearrange("p c r -> p (c r)").bitcast(I32))
@@ -88,11 +88,16 @@ def tile_picked_beamf_none_po_kernel(
                     w34_scales[q:P:32, i * N : (i + 1) * N].bitcast(I32),
                     src[0, q:16:4, :].bitcast(I32),
                 )
-        nc.gpsimd.tensor_scalar(wt["nwi1"][:], wt["wi1"][:], -1.0, 0.0, MULT, ADD)
-        nc.gpsimd.tensor_scalar(wt["nwi2"][:], wt["wi2"][:], -1.0, 0.0, MULT, ADD)
         lists = (m1_t, m2_t)
         wr = (wt["wr1"], wt["wr2"])
-        w_cross = ((wt["wi1"], wt["wi2"]), (wt["nwi1"], wt["nwi2"]))
+        wi = (wt["wi1"], wt["wi2"])
+        w_cross = (wi, {})
+
+        def negate(name):
+            negated = held([P, 2 * LANES], F32, name)
+            for mic in range(2):
+                w_cross[1][mic] = negated[:, LANES * mic : LANES * (mic + 1)]
+                nc.scalar.activation(w_cross[1][mic], wi[mic][:], COPY, scale=-1.0)
 
         w34_dealt = {}
 
@@ -108,28 +113,26 @@ def tile_picked_beamf_none_po_kernel(
         nc.vector.tensor_copy(xg_scales[:], xs[:].indirect(offs_t[:]))
 
         grouped = {}
-        w_codes = [held([P, H], U32, "wc%d" % i) for i in range(2)]
-        w_scales = [held([P, H], U8, "wsc%d" % i) for i in range(2)]
+        w_codes, w_scales = {}, {}
         proj = {}
 
-        def regroup(i, u, move):
+        def regroup(i, u, move, rows=slice(0, P)):
             move(
-                grouped[(i, u)][:].rearrange("p (t m j) -> p m j t", t=2, j=LANES),
-                raw[i][:].rearrange("p j (m t) -> p m j t", t=LANES)[:, :, :, 2 * u : 2 * u + 2],
+                grouped[(i, u)][:].rearrange("p (t m j) -> p m j t", t=2, j=LANES)[:, rows],
+                raw[i][:].rearrange("p j (m t) -> p m j t", t=LANES)[:, rows, :, 2 * u : 2 * u + 2],
             )
 
-        def quantise_w(i, t0, t1):
-            cols = slice(t0 * P, t1 * P)
-            nc.vector.quantize_mx(
-                out=w_codes[i][:, cols].bitcast(FP8X4), scales=w_scales[i][:, cols],
-                in_=grouped[(i, t0 // 2)][:, t0 % 2 * H : (t0 % 2 + t1 - t0) * H],
-            )
+        def quantise_w(i, u, name):
+            w_codes[(i, u)] = held([P, 2 * P], U32, name)
+            w_scales[(i, u)] = held([P, 2 * P], U8, "wsc%d%d" % (i, u))
+            nc.vector.quantize_mx(out=w_codes[(i, u)][:].bitcast(FP8X4), scales=w_scales[(i, u)][:], in_=grouped[(i, u)][:])
 
         def project(i, t, j0=0, n=S):
-            cols = slice(t * P, (t + 1) * P)
+            u, e = divmod(t, 2)
+            cols = slice(e * P, (e + 1) * P)
             proj[(i, t)] = bank(PROJ_BANK[i][t] if j0 == 0 else SUM_BANK[0])
             nc.tensor.matmul_mx(
-                out=proj[(i, t)][:, j0 : j0 + n], lhsT=w_codes[i][:, cols].bitcast(FP8X4), lhsT_scale=w_scales[i][:, cols],
+                out=proj[(i, t)][:, j0 : j0 + n], lhsT=w_codes[(i, u)][:, cols].bitcast(FP8X4), lhsT_scale=w_scales[(i, u)][:, cols],
                 rhs=xg_words[:, j0 : j0 + n].bitcast(FP8X4), rhs_scale=xg_scales[:, j0 : j0 + n], start=True, stop=True,
             )
 
@@ -145,19 +148,23 @@ def tile_picked_beamf_none_po_kernel(
 
         def cross_term(i, t, mic, dst):
             cross[(i, t, mic)] = dst
-            nc.scalar.activation(cross[(i, t, mic)], proj[(i, t)][:], COPY, scale=w_cross[i][mic][:, t : t + 1])
+            nc.scalar.activation(cross[(i, t, mic)], proj[(i, t)][:], COPY, scale=wi[mic][:, t : t + 1])
 
         def combine(z, t, mic):
             mixed[(z, t, mic)] = held([P, S], F32, "mixed%d%d%d" % (z, t, mic))
             nc.vector.scalar_tensor_tensor(
-                mixed[(z, t, mic)][:], proj[(z, t)][:], wr[mic][:, t : t + 1], cross[(1 - z, t, mic)], MULT, ADD
+                mixed[(z, t, mic)][:], proj[(z, t)][:], wr[mic][:, t : t + 1], cross[(1 - z, t, mic)], MULT, (SUBTRACT, ADD)[z]
             )
 
+        direct = {}
+
+        def direct_term(z, t, mic):
+            direct[(z, t, mic)] = slot("direct%d%d%d" % (z, t, mic))
+            nc.scalar.activation(direct[(z, t, mic)], proj[(z, t)][:], COPY, scale=wr[mic][:, t : t + 1])
+
         def combine_aside(z, t, mic):
-            direct = slot("direct%d%d%d" % (z, t, mic))
-            nc.scalar.activation(direct, proj[(z, t)][:], COPY, scale=wr[mic][:, t : t + 1])
             mixed[(z, t, mic)] = held([P, S], F32, "mixed%d%d%d" % (z, t, mic))
-            nc.gpsimd.tensor_tensor(mixed[(z, t, mic)][:], direct, cross[(1 - z, t, mic)], ADD)
+            nc.gpsimd.tensor_tensor(mixed[(z, t, mic)][:], direct[(z, t, mic)], cross[(1 - z, t, mic)], ADD)
 
         def add_term(term, t, z, chunks):
             for c in chunks:
@@ -203,9 +210,9 @@ def tile_picked_beamf_none_po_kernel(
 
         first = {}
 
-        def fetch_first(c, chunks, z, name):
+        def fetch_first(c, chunks, z, dst):
             n = chunks * CH
-            first[(c, z)] = held([P, 2 * n], F32, name)
+            first[(c, z)] = dst
             for e in range(2):
                 offsets = lists[0][:, c * CH // 16 : (c * CH + n) // 16]
                 nc.vector.tensor_copy(first[(c, z)][:, e * n : (e + 1) * n], mixed[(z, 2 + e, 0)][:].indirect(offsets))
@@ -223,7 +230,7 @@ def tile_picked_beamf_none_po_kernel(
                 z_high[(c + d, z)] = total[:].rearrange("p (e j) -> p j e", e=2)[:, d * CH : (d + 1) * CH, :]
 
         def high_lanes(c, chunks, z, first_name, sum_name):
-            fetch_first(c, chunks, z, first_name)
+            fetch_first(c, chunks, z, held([P, 2 * chunks * CH], F32, first_name)[:])
             add_second(c, chunks, z, sum_name)
 
         def round_high(c, z, move):
@@ -294,17 +301,19 @@ def tile_picked_beamf_none_po_kernel(
 
         for u in range(2):
             grouped[(0, u)] = held([P, 2 * H], BF16, "grouped%d" % u)
-        regroup(0, 0, nc.vector.tensor_copy)
+        regroup(0, 0, nc.vector.tensor_copy, slice(0, P // 2))
+        regroup(0, 0, nc.scalar.copy, slice(P // 2, P))
         regroup(0, 1, nc.scalar.copy)
-        quantise_w(0, 0, 2)
-        quantise_w(0, 2, LANES)
+        quantise_w(0, 0, "wc00")
         for h in range(2):
             nc.vector.tensor_copy(
                 xg_words[:, h * HALF : (h + 1) * HALF], xw[:].bitcast(U32).indirect(offs_t[:, h * HALF // 16 : (h + 1) * HALF // 16])
             )
             project(0, 0, h * HALF, HALF)
             fill(0, 0, h * HALF, HALF)
-        for t in range(1, LANES):
+        project(0, 1)
+        quantise_w(0, 1, "xw")
+        for t in (2, 3):
             project(0, t)
         fill(0, 1)
         for i in range(2):
@@ -317,47 +326,55 @@ def tile_picked_beamf_none_po_kernel(
             grouped[(1, u)] = held([P, 2 * H], BF16, "grouped%d" % u)
             regroup(1, u, nc.scalar.copy)
         picked = [picked[0], picked[1]]
-        quantise_w(1, 0, 2)
+        quantise_w(1, 0, "wc10")
         for t in range(2):
             project(1, t)
             fill(1, t)
         after = [held([P, 2 * S], F32, "grouped0")]
         picked.append(after[0][:, 0:S])
         look_up(picked[2], 0, 1, 0)
-        quantise_w(1, 2, LANES)
+        quantise_w(1, 1, "wc11")
         for t in (2, 3):
             project(1, t)
-        after.append(held([P, 5 * S], F32, "grouped1"))
+        after.append(held([P, 7 * S], F32, "grouped1"))
         picked.append(slot("raw1"))
         look_up(picked[3], 0, 1, 1)
         for k in range(4, 8):
             picked.append(slot("pick%d" % k))
             look_up(picked[k], 1, k // 2 % 2, k % 2)
+        negate("ring0")
         for i in (1, 0):
             for n in range(4):
                 dst = slot("cross%d" % n) if i == 1 else after[1][:, (n + (n > 0)) * S : (n + (n > 0) + 1) * S]
                 cross_term(i, 2 + n % 2, n // 2, dst)
         for k in range(8):
+            if k == 7:
+                for t in (2, 3):
+                    combine(1, t, 0)
+                    direct_term(1, t, 1)
             names = [slot("term%d%d" % (k, z)) for z in range(2)]
             if k < 2:
                 names[1 - k] = after[k][:, S : 2 * S]
+            if k == 2:
+                names = [after[1][:, 5 * S : 6 * S], after[1][:, 6 * S : 7 * S]]
             weigh(picked[k], k // 4, k // 2 % 2, k % 2, (k < 7, k < 4), names)
         dealt_scales[0] = held([P, 2 * N], U8, "pick5")
         nc.gpsimd.tensor_copy(
             dealt_scales[0][:].rearrange("p (w t m) -> p w t m", w=2, t=LANES),
             w34_scales[:].rearrange("p (w m t) -> p w t m", w=2, t=LANES),
         )
-        windows = [(z, t, mic) for mic in range(2) for z in range(2) for t in (2, 3)]
-        for key in windows[:-ASIDE]:
-            combine(*key)
-        for key in windows[-ASIDE:]:
-            combine_aside(*key)
+        for mic in range(2):
+            for t in (2, 3):
+                combine(0, t, mic)
+        for t in (2, 3):
+            combine_aside(1, t, 1)
         for c in range(4):
             low_lanes(c)
         place_low(0)
         place_low(1)
+        early = held([P, 2 * S], F32, "cross2")
         for z in range(2):
-            fetch_first(0, 2, z, "first%d" % z)
+            fetch_first(0, 2, z, early[:, z * S : (z + 1) * S])
         for z in range(2):
             add_second(0, 2, z, "high%d" % z)
             for c in range(2):

@@ -101,9 +101,9 @@ def tile_picked_beamf_none_po_kernel(
 
         w34_dealt = {}
 
-        def deal_words(i, name):
+        def deal_words(i, name, engine):
             w34_dealt[i] = held([P, 2 * N], U8, name)
-            nc.gpsimd.tensor_copy(
+            engine.tensor_copy(
                 w34_dealt[i][:].rearrange("p (t m e) -> p t m e", t=LANES, e=2),
                 w34_words[i][:].rearrange("p (m t e) -> p t m e", t=LANES, e=2),
             )
@@ -316,8 +316,8 @@ def tile_picked_beamf_none_po_kernel(
         for t in (2, 3):
             project(0, t)
         fill(0, 1)
-        for i in range(2):
-            deal_words(i, "w%dd" % (3 + i))
+        deal_words(0, "w3d", nc.vector)
+        deal_words(1, "w3w", nc.gpsimd)
         picked = {}
         for k in range(2):
             picked[k] = slot("ring%d" % k)

@@ -25,10 +25,11 @@ CH = 128
 LAST = 3
 HALF = H // 2
 BANK = 512
-PROJ_BANK = ((0, 1, 4, 5), (6, 7, 6, 7))
-SUM_BANK = (2, 3, 0, 1)
-OUT_BANK = (4, 5, 6)
-LAST_OUT_BANK = (2, 3, 0, 7)
+PROJ_BANK = ((0, 1, 0, 1), (6, 7, 6, 7))
+SUM_BANK = (2, 3, 4, 5)
+BACK_BANK = (2, 3, 2, 3)
+OUT_BANK = (0, 1, 6)
+LAST_OUT_BANK = (2, 3, 4, 7)
 TERMS_IN_BANK = 16
 
 
@@ -77,9 +78,10 @@ def tile_picked_beamf_none_po_kernel(
         nc.sync.dma_start(m1_t[:], m1)
         nc.sync.dma_start(w34_words[0][:].bitcast(I32), w3_words[0].bitcast(I32))
         nc.sync.dma_start(w34_words[1][:].bitcast(I32), w4_words[0].bitcast(I32))
+        nc.sync.dma_start(wt["wr1"][:], wr1.rearrange("(p t) o -> p (t o)", t=LANES))
         nc.sync.dma_start(raw[1][:], w_rows[1])
         nc.sync.dma_start(m2_t[:], m2)
-        for name, src in (("wr1", wr1), ("wi1", wi1), ("wr2", wr2), ("wi2", wi2)):
+        for name, src in (("wi1", wi1), ("wr2", wr2), ("wi2", wi2)):
             nc.sync.dma_start(wt[name][:], src.rearrange("(p t) o -> p (t o)", t=LANES))
         make_identity(nc, ident[:])
         for i, src in enumerate((w3_scales, w4_scales)):
@@ -193,14 +195,19 @@ def tile_picked_beamf_none_po_kernel(
 
         z_in, z_high, out_bf, dealt_scales, back, result = {}, {}, {}, {}, {}, {}
 
+        low_words = {}
+
         def low_lanes(c):
             pairs = held([P, H], BF16, "zb%d" % c)
             nc.scalar.copy(
                 pairs[:].rearrange("j (z p e) -> j z p e", z=2, e=2),
                 sums[c][:].rearrange("j (z e p) -> j z p e", z=2, e=2),
             )
-            words = pairs[:].bitcast(F32)
-            back[c] = bank(SUM_BANK[c])
+            low_words[c] = pairs[:].bitcast(F32)
+
+        def turn_back(c):
+            words = low_words[c]
+            back[c] = bank(BACK_BANK[c])
             for z in range(2):
                 nc.tensor.transpose(back[c][:, z * P : (z + 1) * P], words[:, z * P : (z + 1) * P], ident[:])
 
@@ -336,7 +343,7 @@ def tile_picked_beamf_none_po_kernel(
         quantise_w(1, 1, "wc11")
         for t in (2, 3):
             project(1, t)
-        after.append(held([P, 7 * S], F32, "grouped1"))
+        after.append(held([P, 8 * S], F32, "grouped1"))
         picked.append(slot("raw1"))
         look_up(picked[3], 0, 1, 1)
         for k in range(4, 8):
@@ -353,8 +360,10 @@ def tile_picked_beamf_none_po_kernel(
                     combine(1, t, 0)
                     direct_term(1, t, 1)
             names = [slot("term%d%d" % (k, z)) for z in range(2)]
-            if k < 2:
-                names[1 - k] = after[k][:, S : 2 * S]
+            if k == 0:
+                names[1] = after[0][:, S : 2 * S]
+            if k == 1:
+                names = [after[1][:, S : 2 * S], after[1][:, 7 * S : 8 * S]]
             if k == 2:
                 names = [after[1][:, 5 * S : 6 * S], after[1][:, 6 * S : 7 * S]]
             weigh(picked[k], k // 4, k // 2 % 2, k % 2, (k < 7, k < 4), names)
@@ -368,10 +377,15 @@ def tile_picked_beamf_none_po_kernel(
                 combine(0, t, mic)
         for t in (2, 3):
             combine_aside(1, t, 1)
-        for c in range(4):
+        for c in range(LAST):
             low_lanes(c)
+        for c in range(2):
+            turn_back(c)
         place_low(0)
+        turn_back(2)
+        low_lanes(LAST)
         place_low(1)
+        turn_back(LAST)
         early = held([P, 2 * S], F32, "cross2")
         for z in range(2):
             fetch_first(0, 2, z, early[:, z * S : (z + 1) * S])

@@ -21,16 +21,22 @@ COPY = mybir.ActivationFunctionType.Copy
 
 P = 128
 LANES = 4
+HIGH = (2, 3)
+RE, IM = 0, 1
 CH = 128
 LAST = 3
-HALF = H // 2
+HALF = S // 2
 BANK = 512
+LOOK_UPS = 8
+TERMS_IN_BANK = 16
+GPSIMD_Z_TERMS = 7
+GPSIMD_Z2_TERMS = 4
+
 PROJ_BANK = ((0, 1, 0, 1), (6, 7, 6, 7))
 SUM_BANK = (2, 3, 4, 5)
 BACK_BANK = (2, 3, 2, 3)
 OUT_BANK = (0, 1, 6)
 LAST_OUT_BANK = (2, 3, 4, 7)
-TERMS_IN_BANK = 16
 
 
 def tile_picked_beamf_none_po_kernel(
@@ -45,6 +51,12 @@ def tile_picked_beamf_none_po_kernel(
         def held(shape, dtype, name):
             return keep.tile(shape, dtype, name=name, align_bytes=64)
 
+        def rows(name, count=1):
+            return held([P, count * S], F32, name)[:]
+
+        def part(ap, n, width=S):
+            return ap[:, n * width : (n + 1) * width]
+
         def bank(b):
             return psum.tile([P, BANK], F32, name="bank%d" % b)
 
@@ -55,73 +67,58 @@ def tile_picked_beamf_none_po_kernel(
         xs = held([P, T], U8, "xs")
         w34_words = [held([P, 2 * N], U8, "w3w"), held([P, 2 * N], U8, "w4w")]
         w34_scales = held([P, 2 * N], U8, "w34s")
-        raw = [held([P, LANES, H], F32, "raw%d" % i) for i in range(2)]
-        wt = {}
-        for name in ("wr1", "wi1", "wr2", "wi2"):
-            wt[name] = held([P, LANES], F32, name)
+        raw = [held([P, LANES, H], F32, "raw%d" % i) for i in (RE, IM)]
+        wr = [held([P, LANES], F32, "wr%d" % mic) for mic in range(2)]
+        wi = [held([P, LANES], F32, "wi%d" % mic) for mic in range(2)]
 
         nc.gpsimd.memset(xs[:].bitcast(I32), 0)
         nc.vector.memset(w34_scales[:].bitcast(I32), 0)
         window = {}
-        for i in range(2):
+        for i in (RE, IM):
             for t in range(2):
                 window[(i, t)] = held([P, 2 * S], F32, "window%d%d" % (i, t))
                 nc.vector.memset(window[(i, t)][:, S : 2 * S], 0.0)
         ident = held([P, P], F32, "ident")
 
-        w_rows = [w.rearrange("(p j) c -> p j c", j=LANES) for w in (w1, w2)]
-        nc.sync.dma_start(raw[0][:], w_rows[0])
+        def load_weight(dst, src):
+            nc.sync.dma_start(dst[:], src.rearrange("(p t) o -> p (t o)", t=LANES))
+
+        def load_scale_rows(dst, src):
+            for q in range(4):
+                nc.sync.dma_start(dst[q:P:32].bitcast(I32), src[0, q:16:4, :].bitcast(I32))
+
+        w_rows = [w.rearrange("(p q) c -> p q c", q=LANES) for w in (w1, w2)]
+        nc.sync.dma_start(raw[RE][:], w_rows[RE])
         nc.sync.dma_start(offs_t[:], offs)
-        for q in range(4):
-            nc.sync.dma_start(xs[q:P:32, :].bitcast(I32), x_scales[0, q:16:4, :].bitcast(I32))
+        load_scale_rows(xs[:, :], x_scales)
         nc.sync.dma_start(xw[:], x_words[0].rearrange("p c r -> p (c r)").bitcast(I32))
         nc.sync.dma_start(m1_t[:], m1)
         nc.sync.dma_start(w34_words[0][:].bitcast(I32), w3_words[0].bitcast(I32))
         nc.sync.dma_start(w34_words[1][:].bitcast(I32), w4_words[0].bitcast(I32))
-        nc.sync.dma_start(wt["wr1"][:], wr1.rearrange("(p t) o -> p (t o)", t=LANES))
-        nc.sync.dma_start(raw[1][:], w_rows[1])
+        load_weight(wr[0], wr1)
+        nc.sync.dma_start(raw[IM][:], w_rows[IM])
         nc.sync.dma_start(m2_t[:], m2)
-        for name, src in (("wi1", wi1), ("wr2", wr2), ("wi2", wi2)):
-            nc.sync.dma_start(wt[name][:], src.rearrange("(p t) o -> p (t o)", t=LANES))
+        load_weight(wi[0], wi1)
+        load_weight(wr[1], wr2)
+        load_weight(wi[1], wi2)
         make_identity(nc, ident[:])
-        for i, src in enumerate((w3_scales, w4_scales)):
-            for q in range(4):
-                nc.sync.dma_start(
-                    w34_scales[q:P:32, i * N : (i + 1) * N].bitcast(I32),
-                    src[0, q:16:4, :].bitcast(I32),
-                )
+        load_scale_rows(w34_scales[:, 0:N], w3_scales)
+        load_scale_rows(w34_scales[:, N : 2 * N], w4_scales)
         lists = (m1_t, m2_t)
-        wr = (wt["wr1"], wt["wr2"])
-        wi = (wt["wi1"], wt["wi2"])
-        w_cross = (wi, {})
 
-        def negate(name):
-            negated = held([P, 2 * LANES], F32, name)
-            for mic in range(2):
-                w_cross[1][mic] = negated[:, LANES * mic : LANES * (mic + 1)]
-                nc.scalar.activation(w_cross[1][mic], wi[mic][:], COPY, scale=-1.0)
-
-        w34_dealt = {}
-
-        def deal_words(i, name, engine):
-            w34_dealt[i] = held([P, 2 * N], U8, name)
-            engine.tensor_copy(
-                w34_dealt[i][:].rearrange("p (t m e) -> p t m e", t=LANES, e=2),
-                w34_words[i][:].rearrange("p (m t e) -> p t m e", t=LANES, e=2),
-            )
+        def offsets(mic, c, chunks):
+            return lists[mic][:, c * CH // 16 : (c + chunks) * CH // 16]
 
         xg_words = held([P, S], U32, "xgw")
         xg_scales = held([P, S], U8, "xgs")
         nc.vector.tensor_copy(xg_scales[:], xs[:].indirect(offs_t[:]))
 
-        grouped = {}
-        w_codes, w_scales = {}, {}
-        proj = {}
+        grouped, w_codes, w_scales, proj, w34_dealt = {}, {}, {}, {}, {}
 
-        def regroup(i, u, move, rows=slice(0, P)):
+        def regroup(i, u, move, cols=slice(0, P)):
             move(
-                grouped[(i, u)][:].rearrange("p (t m j) -> p m j t", t=2, j=LANES)[:, rows],
-                raw[i][:].rearrange("p j (m t) -> p m j t", t=LANES)[:, rows, :, 2 * u : 2 * u + 2],
+                grouped[(i, u)][:].rearrange("p (t c q) -> p c q t", t=2, q=LANES)[:, cols],
+                raw[i][:].rearrange("p q (c t) -> p c q t", t=LANES)[:, cols, :, 2 * u : 2 * u + 2],
             )
 
         def quantise_w(i, u, name):
@@ -129,76 +126,151 @@ def tile_picked_beamf_none_po_kernel(
             w_scales[(i, u)] = held([P, 2 * P], U8, "wsc%d%d" % (i, u))
             nc.vector.quantize_mx(out=w_codes[(i, u)][:].bitcast(FP8X4), scales=w_scales[(i, u)][:], in_=grouped[(i, u)][:])
 
-        def project(i, t, j0=0, n=S):
+        def project(i, t, frames=slice(0, S), into=None):
             u, e = divmod(t, 2)
-            cols = slice(e * P, (e + 1) * P)
-            proj[(i, t)] = bank(PROJ_BANK[i][t] if j0 == 0 else SUM_BANK[0])
+            proj[(i, t)] = bank(PROJ_BANK[i][t] if into is None else into)
             nc.tensor.matmul_mx(
-                out=proj[(i, t)][:, j0 : j0 + n], lhsT=w_codes[(i, u)][:, cols].bitcast(FP8X4), lhsT_scale=w_scales[(i, u)][:, cols],
-                rhs=xg_words[:, j0 : j0 + n].bitcast(FP8X4), rhs_scale=xg_scales[:, j0 : j0 + n], start=True, stop=True,
+                out=proj[(i, t)][:, frames],
+                lhsT=part(w_codes[(i, u)], e, P).bitcast(FP8X4), lhsT_scale=part(w_scales[(i, u)], e, P),
+                rhs=xg_words[:, frames].bitcast(FP8X4), rhs_scale=xg_scales[:, frames], start=True, stop=True,
             )
 
-        def fill(i, t, j0=0, n=S):
-            nc.scalar.copy(window[(i, t)][:, j0 : j0 + n], proj[(i, t)][:, j0 : j0 + n])
+        def fill(i, t, frames=slice(0, S)):
+            nc.scalar.copy(window[(i, t)][:, frames], proj[(i, t)][:, frames])
 
-        out_codes = held([P, S], U32, "oc")
-        out_scales = held([P, S], U8, "osc")
-        out_rows = out_0.rearrange("(p t) j -> p t j", t=LANES)
-        out_words = out_1[0].rearrange("p c r -> p (c r)").bitcast(I32)
+        def deal_words(z, name, engine):
+            w34_dealt[z] = held([P, 2 * N], U8, name)
+            engine.tensor_copy(
+                w34_dealt[z][:].rearrange("p (t c e) -> p t c e", t=LANES, e=2),
+                w34_words[z][:].rearrange("p (c t e) -> p t c e", t=LANES, e=2),
+            )
 
-        cross, mixed, sums, count = {}, {}, {}, {}
+        for u in range(2):
+            grouped[(RE, u)] = held([P, 2 * H], BF16, "grouped%d" % u)
+        regroup(RE, 0, nc.vector.tensor_copy, slice(0, P // 2))
+        regroup(RE, 0, nc.scalar.copy, slice(P // 2, P))
+        regroup(RE, 1, nc.scalar.copy)
+        quantise_w(RE, 0, "wc00")
+        for h in range(2):
+            frames = slice(h * HALF, (h + 1) * HALF)
+            nc.vector.tensor_copy(xg_words[:, frames], xw[:].bitcast(U32).indirect(part(offs_t, h, HALF // 16)))
+            project(RE, 0, frames, None if h == 0 else SUM_BANK[0])
+            fill(RE, 0, frames)
+        project(RE, 1)
+        quantise_w(RE, 1, "xw")
+        for t in HIGH:
+            project(RE, t)
+        fill(RE, 1)
+        deal_words(0, "w3d", nc.vector)
+        deal_words(1, "w3w", nc.gpsimd)
+
+        picked = {}
+
+        def look_up(k, dst):
+            picked[k] = dst
+            nc.vector.tensor_copy(dst, window[(k // 4, k // 2 % 2)][:].indirect(lists[k % 2][:]))
+
+        for k in range(2):
+            look_up(k, rows("picked%d" % k))
+        for u in range(2):
+            grouped[(IM, u)] = held([P, 2 * H], BF16, "grouped%d" % u)
+            regroup(IM, u, nc.scalar.copy)
+        quantise_w(IM, 0, "wc10")
+        for t in range(2):
+            project(IM, t)
+            fill(IM, t)
+        behind_low = rows("grouped0", 2)
+        look_up(2, part(behind_low, 0))
+        quantise_w(IM, 1, "wc11")
+        for t in HIGH:
+            project(IM, t)
+        behind_high = rows("grouped1", 8)
+        look_up(3, rows("raw1"))
+        for k in range(4, LOOK_UPS):
+            look_up(k, rows("picked%d" % k))
+
+        minus_wi = held([P, 2 * LANES], F32, "picked0")
+        for mic in range(2):
+            nc.scalar.activation(part(minus_wi, mic, LANES), wi[mic][:], COPY, scale=-1.0)
+
+        cross, direct, mixed, sums, added = {}, {}, {}, {}, {}
 
         def cross_term(i, t, mic, dst):
             cross[(i, t, mic)] = dst
-            nc.scalar.activation(cross[(i, t, mic)], proj[(i, t)][:], COPY, scale=wi[mic][:, t : t + 1])
+            nc.scalar.activation(dst, proj[(i, t)][:], COPY, scale=wi[mic][:, t : t + 1])
 
         def combine(z, t, mic):
             mixed[(z, t, mic)] = held([P, S], F32, "mixed%d%d%d" % (z, t, mic))
             nc.vector.scalar_tensor_tensor(
-                mixed[(z, t, mic)][:], proj[(z, t)][:], wr[mic][:, t : t + 1], cross[(1 - z, t, mic)], MULT, (SUBTRACT, ADD)[z]
+                mixed[(z, t, mic)][:], proj[(z, t)][:], wr[mic][:, t : t + 1], cross[(1 - z, t, mic)],
+                MULT, (SUBTRACT, ADD)[z],
             )
 
-        direct = {}
+        def direct_term(t):
+            direct[t] = rows("direct%d" % t)
+            nc.scalar.activation(direct[t], proj[(IM, t)][:], COPY, scale=wr[1][:, t : t + 1])
 
-        def direct_term(z, t, mic):
-            direct[(z, t, mic)] = slot("direct%d%d%d" % (z, t, mic))
-            nc.scalar.activation(direct[(z, t, mic)], proj[(z, t)][:], COPY, scale=wr[mic][:, t : t + 1])
+        def combine_aside(t):
+            mixed[(1, t, 1)] = held([P, S], F32, "mixed1%d1" % t)
+            nc.gpsimd.tensor_tensor(mixed[(1, t, 1)][:], direct[t], cross[(RE, t, 1)], ADD)
 
-        def combine_aside(z, t, mic):
-            mixed[(z, t, mic)] = held([P, S], F32, "mixed%d%d%d" % (z, t, mic))
-            nc.gpsimd.tensor_tensor(mixed[(z, t, mic)][:], direct[(z, t, mic)], cross[(1 - z, t, mic)], ADD)
-
-        def add_term(term, t, z, chunks):
-            for c in chunks:
+        def add_term(term, t, z):
+            for c in range(LAST + 1):
                 if c not in sums:
                     sums[c] = bank(SUM_BANK[c])
-                    count[c] = 0
+                    added[c] = 0
                 nc.tensor.matmul(
-                    sums[c][:, (2 * z + t) * P : (2 * z + t + 1) * P],
-                    lhsT=term[:, c * CH : (c + 1) * CH], rhs=ident[:], is_transpose=True,
-                    start=(count[c] == 0), stop=(count[c] == TERMS_IN_BANK - 1),
+                    part(sums[c], 2 * z + t, P), lhsT=part(term, c, CH), rhs=ident[:], is_transpose=True,
+                    start=(added[c] == 0), stop=(added[c] == TERMS_IN_BANK - 1),
                 )
-                count[c] = count[c] + 1
+                added[c] += 1
 
-        def look_up(dst, i, t, mic):
-            nc.vector.tensor_copy(dst, window[(i, t)][:].indirect(lists[mic][:]))
-
-        def weigh(src, i, t, mic, on_gpsimd, names):
+        def weigh(k, terms):
+            i, t, mic = k // 4, k // 2 % 2, k % 2
             for z in range(2):
-                w = wr[mic] if z == i else w_cross[i][mic]
-                term = names[z]
-                if on_gpsimd[z]:
-                    nc.gpsimd.tensor_scalar(term, src, w[:, t : t + 1], 0.0, MULT, ADD)
+                if z == i:
+                    w = wr[mic][:, t : t + 1]
+                elif i == RE:
+                    w = wi[mic][:, t : t + 1]
                 else:
-                    nc.scalar.activation(term, src, COPY, scale=w[:, t : t + 1])
-                add_term(term, t, z, range(4))
+                    w = part(minus_wi, mic, LANES)[:, t : t + 1]
+                if k < (GPSIMD_Z_TERMS, GPSIMD_Z2_TERMS)[z]:
+                    nc.gpsimd.tensor_scalar(terms[z], picked[k], w, 0.0, MULT, ADD)
+                else:
+                    nc.scalar.activation(terms[z], picked[k], COPY, scale=w)
+                add_term(terms[z], t, z)
 
-        z_in, z_high, out_bf, dealt_scales, back, result = {}, {}, {}, {}, {}, {}
+        for mic in range(2):
+            for t in HIGH:
+                cross_term(IM, t, mic, rows("cross%d%d" % (t, mic)))
+        for mic in range(2):
+            for t in HIGH:
+                cross_term(RE, t, mic, part(behind_high, 2 * mic + t - 2))
+        weigh(0, (rows("term00"), part(behind_low, 1)))
+        weigh(1, (part(behind_high, 4), part(behind_high, 5)))
+        weigh(2, (part(behind_high, 6), part(behind_high, 7)))
+        for k in range(3, LOOK_UPS):
+            if k == LOOK_UPS - 1:
+                for t in HIGH:
+                    combine(1, t, 0)
+                    direct_term(t)
+            weigh(k, (rows("term%d0" % k), rows("term%d1" % k)))
 
-        low_words = {}
+        dealt_scales = held([P, 2 * N], U8, "picked5")
+        nc.gpsimd.tensor_copy(
+            dealt_scales[:].rearrange("p (z t c) -> p z t c", z=2, t=LANES),
+            w34_scales[:].rearrange("p (z c t) -> p z t c", z=2, t=LANES),
+        )
+        for mic in range(2):
+            for t in HIGH:
+                combine(0, t, mic)
+        for t in HIGH:
+            combine_aside(t)
 
-        def low_lanes(c):
-            pairs = held([P, H], BF16, "zb%d" % c)
+        low_words, back, z_in, first, z_high = {}, {}, {}, {}, {}
+
+        def round_low(c):
+            pairs = held([P, H], BF16, "z%d" % c)
             nc.scalar.copy(
                 pairs[:].rearrange("j (z p e) -> j z p e", z=2, e=2),
                 sums[c][:].rearrange("j (z e p) -> j z p e", z=2, e=2),
@@ -206,213 +278,132 @@ def tile_picked_beamf_none_po_kernel(
             low_words[c] = pairs[:].bitcast(F32)
 
         def turn_back(c):
-            words = low_words[c]
             back[c] = bank(BACK_BANK[c])
             for z in range(2):
-                nc.tensor.transpose(back[c][:, z * P : (z + 1) * P], words[:, z * P : (z + 1) * P], ident[:])
+                nc.tensor.transpose(part(back[c], z, P), part(low_words[c], z, P), ident[:])
 
         def place_low(c):
-            z_in[c] = held([P, 2 * H], BF16, "zb%d" % c)
+            z_in[c] = held([P, 2 * H], BF16, "z%d" % c)
             nc.scalar.copy(z_in[c][:].bitcast(F32).rearrange("p (n u) -> p n u", u=2)[:, :, 0], back[c][:, 0 : 2 * P])
 
-        first = {}
-
         def fetch_first(c, chunks, z, dst):
-            n = chunks * CH
             first[(c, z)] = dst
-            for e in range(2):
-                offsets = lists[0][:, c * CH // 16 : (c * CH + n) // 16]
-                nc.vector.tensor_copy(first[(c, z)][:, e * n : (e + 1) * n], mixed[(z, 2 + e, 0)][:].indirect(offsets))
+            for e, t in enumerate(HIGH):
+                nc.vector.tensor_copy(part(dst, e, chunks * CH), mixed[(z, t, 0)][:].indirect(offsets(0, c, chunks)))
 
         def add_second(c, chunks, z, name):
             n = chunks * CH
             total = held([P, 2 * n], F32, name)
-            for e in range(2):
-                offsets = lists[1][:, c * CH // 16 : (c * CH + n) // 16]
+            for e, t in enumerate(HIGH):
                 nc.vector.tensor_tensor(
-                    total[:, e * n : (e + 1) * n], mixed[(z, 2 + e, 1)][:].indirect(offsets),
-                    first[(c, z)][:, e * n : (e + 1) * n], ADD,
+                    part(total, e, n), mixed[(z, t, 1)][:].indirect(offsets(1, c, chunks)), part(first[(c, z)], e, n), ADD
                 )
             for d in range(chunks):
                 z_high[(c + d, z)] = total[:].rearrange("p (e j) -> p j e", e=2)[:, d * CH : (d + 1) * CH, :]
 
-        def high_lanes(c, chunks, z, first_name, sum_name):
-            fetch_first(c, chunks, z, held([P, 2 * chunks * CH], F32, first_name)[:])
-            add_second(c, chunks, z, sum_name)
+        def high_lanes(c, z, behind):
+            fetch_first(c, 1, z, held([P, 2 * CH], F32, behind)[:])
+            add_second(c, 1, z, "high%d%d" % (c, z))
 
         def round_high(c, z, move):
-            move(
-                z_in[c][:, z * H : (z + 1) * H].rearrange("p (j t) -> p j t", t=LANES)[:, :, 2:4],
-                z_high[(c, z)],
-            )
+            move(part(z_in[c], z, H).rearrange("p (j t) -> p j t", t=LANES)[:, :, 2:4], z_high[(c, z)])
 
-        def out_pass(res, t, z, z_codes, z_scales):
+        out_codes = held([P, S], U32, "oc")
+        out_scales = held([P, S], U8, "osc")
+        out_rows = out_0.rearrange("(p t) j -> p t j", t=LANES)
+        out_words = out_1[0].rearrange("p c r -> p (c r)").bitcast(I32)
+        z_codes, z_scales, result, out_bf, last = {}, {}, {}, {}, {}
+
+        def out_pass(res, c, t, z):
             nc.tensor.matmul_mx(
                 out=res,
-                lhsT=w34_dealt[z][:, 2 * P * t : 2 * P * (t + 1)].bitcast(FP4X4),
-                lhsT_scale=dealt_scales[0][:, z * N + t * P : z * N + (t + 1) * P],
-                rhs=z_codes[:, z * CH : (z + 1) * CH].bitcast(FP8X4), rhs_scale=z_scales[:, z * CH : (z + 1) * CH],
+                lhsT=part(w34_dealt[z], t, 2 * P).bitcast(FP4X4), lhsT_scale=part(dealt_scales, LANES * z + t, P),
+                rhs=part(z_codes[c], z, CH).bitcast(FP8X4), rhs_scale=part(z_scales[c], z, CH),
                 start=(z == 0), stop=(z == 1),
             )
 
+        def store_out(c, out_f32):
+            nc.sync.dma_start(out_rows[:, :, c * CH : (c + 1) * CH], out_f32[:].rearrange("p (t j) -> p t j", t=LANES))
+
+        def interleave(move, c, src):
+            move(out_bf[c][:].rearrange("p (j t) -> p j t", t=LANES), src[:].rearrange("p (t j) -> p j t", t=LANES))
+
         def multiply(c):
-            z_codes = held([P, 2 * CH], U32, "zc%d" % c)
-            z_scales = held([P, 2 * CH], U8, "zs%d" % c)
-            nc.vector.quantize_mx(out=z_codes[:].bitcast(FP8X4), scales=z_scales[:], in_=z_in[c][:])
-            res = bank(OUT_BANK[c])
+            z_codes[c] = held([P, 2 * CH], U32, "zc%d" % c)
+            z_scales[c] = held([P, 2 * CH], U8, "zs%d" % c)
+            nc.vector.quantize_mx(out=z_codes[c][:].bitcast(FP8X4), scales=z_scales[c][:], in_=z_in[c][:])
+            result[c] = bank(OUT_BANK[c])
             for t in range(LANES):
                 for z in range(2):
-                    out_pass(res[:, t * CH : (t + 1) * CH], t, z, z_codes, z_scales)
+                    out_pass(part(result[c], t, CH), c, t, z)
             out_bf[c] = held([P, LANES * CH], BF16, "ob%d" % c)
             out_f32 = held([P, LANES * CH], F32, "of%d" % c)
-            nc.scalar.copy(out_f32[:], res[:])
-            nc.sync.dma_start(out_rows[:, :, c * CH : (c + 1) * CH], out_f32[:].rearrange("p (t j) -> p t j", t=LANES))
-            result[c] = res
-
-        def round_out(c):
-            nc.scalar.copy(out_bf[c][:].rearrange("p (j t) -> p j t", t=LANES), result[c][:].rearrange("p (t j) -> p j t", t=LANES))
+            nc.scalar.copy(out_f32[:], result[c][:])
+            store_out(c, out_f32)
 
         def hand_on(c):
-            cols = slice(c * CH, (c + 1) * CH)
-            nc.vector.quantize_mx(out=out_codes[:, cols].bitcast(FP8X4), scales=out_scales[:, cols], in_=out_bf[c][:])
+            nc.vector.quantize_mx(out=part(out_codes, c, CH).bitcast(FP8X4), scales=part(out_scales, c, CH), in_=out_bf[c][:])
             if c > 0:
-                done = slice((c - 1) * CH, (c + 1) * CH) if c == 1 else cols
+                done = slice(0 if c == 1 else c * CH, (c + 1) * CH)
                 nc.sync.dma_start(out_words[:, done], out_codes[:, done].bitcast(I32))
-
-        last = {}
 
         def last_passes(z):
             if z == 0:
-                last["codes"] = held([P, 2 * CH], U32, "zc3")
-                last["scales"] = held([P, 2 * CH], U8, "zs3")
-            cols = slice(z * CH, (z + 1) * CH)
+                z_codes[LAST] = held([P, 2 * CH], U32, "zc3")
+                z_scales[LAST] = held([P, 2 * CH], U8, "zs3")
             nc.vector.quantize_mx(
-                out=last["codes"][:, cols].bitcast(FP8X4), scales=last["scales"][:, cols], in_=z_in[LAST][:, z * H : (z + 1) * H]
+                out=part(z_codes[LAST], z, CH).bitcast(FP8X4), scales=part(z_scales[LAST], z, CH), in_=part(z_in[LAST], z, H)
             )
             for t in range(LANES):
                 if z == 0:
                     last[t] = bank(LAST_OUT_BANK[t])
-                out_pass(last[t][:, 0:CH], t, z, last["codes"], last["scales"])
+                out_pass(last[t][:, 0:CH], LAST, t, z)
 
         def last_out():
             out_f32 = held([P, LANES * CH], F32, "of3")
             for t in range(LANES):
                 move = nc.scalar.copy if t % 2 == 0 else nc.vector.tensor_copy
-                move(out_f32[:, t * CH : (t + 1) * CH], last[t][:, 0:CH])
-            nc.sync.dma_start(out_rows[:, :, LAST * CH : (LAST + 1) * CH], out_f32[:].rearrange("p (t j) -> p t j", t=LANES))
+                move(part(out_f32, t, CH), last[t][:, 0:CH])
+            store_out(LAST, out_f32)
             out_bf[LAST] = held([P, LANES * CH], BF16, "ob3")
-            nc.vector.tensor_copy(out_bf[LAST][:].rearrange("p (j t) -> p j t", t=LANES), out_f32[:].rearrange("p (t j) -> p j t", t=LANES))
+            interleave(nc.vector.tensor_copy, LAST, out_f32)
 
-        def slot(name):
-            return held([P, S], F32, name)[:]
-
-        for u in range(2):
-            grouped[(0, u)] = held([P, 2 * H], BF16, "grouped%d" % u)
-        regroup(0, 0, nc.vector.tensor_copy, slice(0, P // 2))
-        regroup(0, 0, nc.scalar.copy, slice(P // 2, P))
-        regroup(0, 1, nc.scalar.copy)
-        quantise_w(0, 0, "wc00")
-        for h in range(2):
-            nc.vector.tensor_copy(
-                xg_words[:, h * HALF : (h + 1) * HALF], xw[:].bitcast(U32).indirect(offs_t[:, h * HALF // 16 : (h + 1) * HALF // 16])
-            )
-            project(0, 0, h * HALF, HALF)
-            fill(0, 0, h * HALF, HALF)
-        project(0, 1)
-        quantise_w(0, 1, "xw")
-        for t in (2, 3):
-            project(0, t)
-        fill(0, 1)
-        deal_words(0, "w3d", nc.vector)
-        deal_words(1, "w3w", nc.gpsimd)
-        picked = {}
-        for k in range(2):
-            picked[k] = slot("ring%d" % k)
-            look_up(picked[k], 0, 0, k)
-        for u in range(2):
-            grouped[(1, u)] = held([P, 2 * H], BF16, "grouped%d" % u)
-            regroup(1, u, nc.scalar.copy)
-        picked = [picked[0], picked[1]]
-        quantise_w(1, 0, "wc10")
-        for t in range(2):
-            project(1, t)
-            fill(1, t)
-        after = [held([P, 2 * S], F32, "grouped0")]
-        picked.append(after[0][:, 0:S])
-        look_up(picked[2], 0, 1, 0)
-        quantise_w(1, 1, "wc11")
-        for t in (2, 3):
-            project(1, t)
-        after.append(held([P, 8 * S], F32, "grouped1"))
-        picked.append(slot("raw1"))
-        look_up(picked[3], 0, 1, 1)
-        for k in range(4, 8):
-            picked.append(slot("pick%d" % k))
-            look_up(picked[k], 1, k // 2 % 2, k % 2)
-        negate("ring0")
-        for i in (1, 0):
-            for n in range(4):
-                dst = slot("cross%d" % n) if i == 1 else after[1][:, (n + (n > 0)) * S : (n + (n > 0) + 1) * S]
-                cross_term(i, 2 + n % 2, n // 2, dst)
-        for k in range(8):
-            if k == 7:
-                for t in (2, 3):
-                    combine(1, t, 0)
-                    direct_term(1, t, 1)
-            names = [slot("term%d%d" % (k, z)) for z in range(2)]
-            if k == 0:
-                names[1] = after[0][:, S : 2 * S]
-            if k == 1:
-                names = [after[1][:, S : 2 * S], after[1][:, 7 * S : 8 * S]]
-            if k == 2:
-                names = [after[1][:, 5 * S : 6 * S], after[1][:, 6 * S : 7 * S]]
-            weigh(picked[k], k // 4, k // 2 % 2, k % 2, (k < 7, k < 4), names)
-        dealt_scales[0] = held([P, 2 * N], U8, "pick5")
-        nc.gpsimd.tensor_copy(
-            dealt_scales[0][:].rearrange("p (w t m) -> p w t m", w=2, t=LANES),
-            w34_scales[:].rearrange("p (w m t) -> p w t m", w=2, t=LANES),
-        )
-        for mic in range(2):
-            for t in (2, 3):
-                combine(0, t, mic)
-        for t in (2, 3):
-            combine_aside(1, t, 1)
         for c in range(LAST):
-            low_lanes(c)
+            round_low(c)
         for c in range(2):
             turn_back(c)
         place_low(0)
         turn_back(2)
-        low_lanes(LAST)
+        round_low(LAST)
         place_low(1)
         turn_back(LAST)
-        early = held([P, 2 * S], F32, "cross2")
+        early = rows("cross21", 2)
         for z in range(2):
-            fetch_first(0, 2, z, early[:, z * S : (z + 1) * S])
+            fetch_first(0, 2, z, part(early, z))
         for z in range(2):
             add_second(0, 2, z, "high%d" % z)
             for c in range(2):
                 round_high(c, z, nc.scalar.copy)
         place_low(2)
         place_low(LAST)
-        high_lanes(2, 1, 0, "direct131", "high20")
+        high_lanes(2, 0, "direct3")
         multiply(0)
         multiply(1)
         round_high(2, 0, nc.scalar.copy)
-        high_lanes(2, 1, 1, "high1", "high21")
+        high_lanes(2, 1, "high1")
         round_high(2, 1, nc.scalar.copy)
-        high_lanes(LAST, 1, 0, "zc0", "high30")
+        high_lanes(LAST, 0, "zc0")
         multiply(2)
         round_high(LAST, 0, nc.scalar.copy)
-        round_out(0)
-        round_out(1)
+        for c in range(2):
+            interleave(nc.scalar.copy, c, result[c])
         hand_on(0)
-        high_lanes(LAST, 1, 1, "high21", "high31")
+        high_lanes(LAST, 1, "high21")
         last_passes(0)
         round_high(LAST, 1, nc.vector.tensor_copy)
         last_passes(1)
         hand_on(1)
-        round_out(2)
+        interleave(nc.scalar.copy, 2, result[2])
         hand_on(2)
         last_out()
         hand_on(LAST)

@@ -35,8 +35,8 @@ GPSIMD_Z2_TERMS = 4
 PROJ_BANK = ((0, 1, 0, 1), (6, 7, 6, 7))
 SUM_BANK = (2, 3, 4, 5)
 BACK_BANK = (2, 3, 2, 3)
-OUT_BANK = (0, 1, 6)
-LAST_OUT_BANK = (2, 3, 4, 7)
+OUT_BANK = (0, 3, 6)
+LAST_OUT_BANK = (2, 1, 4, 7)
 
 
 def tile_picked_beamf_none_po_kernel(

@@ -21,22 +21,21 @@ COPY = mybir.ActivationFunctionType.Copy
 
 P = 128
 LANES = 4
+LOW = (0, 1)
 HIGH = (2, 3)
 RE, IM = 0, 1
 CH = 128
 LAST = 3
 HALF = S // 2
 BANK = 512
-LOOK_UPS = 8
 TERMS_IN_BANK = 16
-GPSIMD_Z_TERMS = 7
-GPSIMD_Z2_TERMS = 4
+GPSIMD_TERMS = 12
 
-PROJ_BANK = ((0, 1, 0, 1), (6, 7, 6, 7))
+PROJ_BANK = ((0, 1, 0, 6), (6, 7, 7, 1))
 SUM_BANK = (2, 3, 4, 5)
-BACK_BANK = (2, 3, 2, 3)
-OUT_BANK = (0, 3, 6)
-LAST_OUT_BANK = (2, 1, 4, 7)
+BACK_BANK = (0, 1, 6, 7)
+OUT_BANK = (2, 3, 4)
+LAST_OUT_BANK = (0, 1, 6, 5)
 
 
 def tile_picked_beamf_none_po_kernel(
@@ -75,7 +74,7 @@ def tile_picked_beamf_none_po_kernel(
         nc.vector.memset(w34_scales[:].bitcast(I32), 0)
         window = {}
         for i in (RE, IM):
-            for t in range(2):
+            for t in LOW:
                 window[(i, t)] = held([P, 2 * S], F32, "window%d%d" % (i, t))
                 nc.vector.memset(window[(i, t)][:, S : 2 * S], 0.0)
         ident = held([P, P], F32, "ident")
@@ -95,10 +94,10 @@ def tile_picked_beamf_none_po_kernel(
         nc.sync.dma_start(m1_t[:], m1)
         nc.sync.dma_start(w34_words[0][:].bitcast(I32), w3_words[0].bitcast(I32))
         nc.sync.dma_start(w34_words[1][:].bitcast(I32), w4_words[0].bitcast(I32))
-        load_weight(wr[0], wr1)
         nc.sync.dma_start(raw[IM][:], w_rows[IM])
         nc.sync.dma_start(m2_t[:], m2)
         load_weight(wi[0], wi1)
+        load_weight(wr[0], wr1)
         load_weight(wr[1], wr2)
         load_weight(wi[1], wi2)
         make_identity(nc, ident[:])
@@ -158,61 +157,54 @@ def tile_picked_beamf_none_po_kernel(
             fill(RE, 0, frames)
         project(RE, 1)
         quantise_w(RE, 1, "xw")
-        for t in HIGH:
-            project(RE, t)
+        project(RE, 2)
         fill(RE, 1)
         deal_words(0, "w3d", nc.vector)
         deal_words(1, "w3w", nc.gpsimd)
 
-        picked = {}
+        picked, cross, mixed, sums, added = {}, {}, {}, {}, {}
 
-        def look_up(k, dst):
-            picked[k] = dst
-            nc.vector.tensor_copy(dst, window[(k // 4, k // 2 % 2)][:].indirect(lists[k % 2][:]))
+        def fetch(engine, dst, src):
+            if engine is nc.scalar:
+                nc.scalar.activation(dst, src, COPY)
+            else:
+                nc.vector.tensor_copy(dst, src)
 
-        for k in range(2):
-            look_up(k, rows("picked%d" % k))
+        def look_up(engine, i, t, mic):
+            picked[(i, t, mic)] = rows("picked%d%d%d" % (i, t, mic))
+            fetch(engine, picked[(i, t, mic)], window[(i, t)][:].indirect(lists[mic][:]))
+
+        def cross_term(i, t, mic, name=None):
+            cross[(i, t, mic)] = rows(name or "cross%d%d%d" % (i, t, mic))
+            nc.scalar.activation(cross[(i, t, mic)], proj[(i, t)][:], COPY, scale=wi[mic][:, t : t + 1])
+
+        look_up(nc.vector, RE, 0, 0)
+        look_up(nc.scalar, RE, 1, 0)
+        look_up(nc.scalar, RE, 0, 1)
+        cross_term(RE, 2, 0)
         for u in range(2):
             grouped[(IM, u)] = held([P, 2 * H], BF16, "grouped%d" % u)
-            regroup(IM, u, nc.scalar.copy)
-        quantise_w(IM, 0, "wc10")
-        for t in range(2):
+            regroup(IM, u, nc.vector.tensor_copy)
+        for u in range(2):
+            quantise_w(IM, u, "wc1%d" % u)
+        for t in LOW:
             project(IM, t)
             fill(IM, t)
-        behind_low = rows("grouped0", 2)
-        look_up(2, part(behind_low, 0))
-        quantise_w(IM, 1, "wc11")
-        for t in HIGH:
-            project(IM, t)
-        behind_high = rows("grouped1", 8)
-        look_up(3, rows("raw1"))
-        for k in range(4, LOOK_UPS):
-            look_up(k, rows("picked%d" % k))
-
-        minus_wi = held([P, 2 * LANES], F32, "picked0")
+        project(IM, 3)
+        project(RE, 3)
+        project(IM, 2)
+        look_up(nc.vector, RE, 1, 1)
+        for t in LOW:
+            for mic in range(2):
+                look_up(nc.vector, IM, t, mic)
+        cross_term(RE, 2, 1, "wc10")
+        minus_wi = held([P, 2 * LANES], F32, "minus_wi")
         for mic in range(2):
             nc.scalar.activation(part(minus_wi, mic, LANES), wi[mic][:], COPY, scale=-1.0)
-
-        cross, direct, mixed, sums, added = {}, {}, {}, {}, {}
-
-        def cross_term(i, t, mic, dst):
-            cross[(i, t, mic)] = dst
-            nc.scalar.activation(dst, proj[(i, t)][:], COPY, scale=wi[mic][:, t : t + 1])
-
-        def combine(z, t, mic):
-            mixed[(z, t, mic)] = held([P, S], F32, "mixed%d%d%d" % (z, t, mic))
-            nc.vector.scalar_tensor_tensor(
-                mixed[(z, t, mic)][:], proj[(z, t)][:], wr[mic][:, t : t + 1], cross[(1 - z, t, mic)],
-                MULT, (SUBTRACT, ADD)[z],
-            )
-
-        def direct_term(t):
-            direct[t] = rows("direct%d" % t)
-            nc.scalar.activation(direct[t], proj[(IM, t)][:], COPY, scale=wr[1][:, t : t + 1])
-
-        def combine_aside(t):
-            mixed[(1, t, 1)] = held([P, S], F32, "mixed1%d1" % t)
-            nc.gpsimd.tensor_tensor(mixed[(1, t, 1)][:], direct[t], cross[(RE, t, 1)], ADD)
+        for mic in range(2):
+            cross_term(IM, 3, mic)
+            cross_term(RE, 3, mic)
+            cross_term(IM, 2, mic)
 
         def add_term(term, t, z):
             for c in range(LAST + 1):
@@ -225,94 +217,90 @@ def tile_picked_beamf_none_po_kernel(
                 )
                 added[c] += 1
 
-        def weigh(k, terms):
-            i, t, mic = k // 4, k // 2 % 2, k % 2
-            for z in range(2):
-                if z == i:
-                    w = wr[mic][:, t : t + 1]
-                elif i == RE:
-                    w = wi[mic][:, t : t + 1]
-                else:
-                    w = part(minus_wi, mic, LANES)[:, t : t + 1]
-                if k < (GPSIMD_Z_TERMS, GPSIMD_Z2_TERMS)[z]:
-                    nc.gpsimd.tensor_scalar(terms[z], picked[k], w, 0.0, MULT, ADD)
-                else:
-                    nc.scalar.activation(terms[z], picked[k], COPY, scale=w)
-                add_term(terms[z], t, z)
+        def weight_of(i, t, mic, z):
+            if z == i:
+                return wr[mic][:, t : t + 1]
+            if i == RE:
+                return wi[mic][:, t : t + 1]
+            return part(minus_wi, mic, LANES)[:, t : t + 1]
 
-        for mic in range(2):
-            for t in HIGH:
-                cross_term(IM, t, mic, rows("cross%d%d" % (t, mic)))
-        for mic in range(2):
-            for t in HIGH:
-                cross_term(RE, t, mic, part(behind_high, 2 * mic + t - 2))
-        weigh(0, (rows("term00"), part(behind_low, 1)))
-        weigh(1, (part(behind_high, 4), part(behind_high, 5)))
-        weigh(2, (part(behind_high, 6), part(behind_high, 7)))
-        for k in range(3, LOOK_UPS):
-            if k == LOOK_UPS - 1:
-                for t in HIGH:
-                    combine(1, t, 0)
-                    direct_term(t)
-            weigh(k, (rows("term%d0" % k), rows("term%d1" % k)))
+        look_ups = ((RE, 0, 0), (RE, 1, 0), (RE, 0, 1), (RE, 1, 1), (IM, 0, 0), (IM, 0, 1), (IM, 1, 0), (IM, 1, 1))
+        early_terms = rows("grouped1", 6)
+        for n in range(TERMS_IN_BANK):
+            (i, t, mic), z = look_ups[n // 2], n % 2
+            term = part(early_terms, n) if n < 6 else rows("term%d" % n)
+            if n < GPSIMD_TERMS:
+                nc.gpsimd.tensor_scalar(term, picked[(i, t, mic)], weight_of(i, t, mic, z), 0.0, MULT, ADD)
+            else:
+                nc.scalar.activation(term, picked[(i, t, mic)], COPY, scale=weight_of(i, t, mic, z))
+            add_term(term, t, z)
 
-        dealt_scales = held([P, 2 * N], U8, "picked5")
+        dealt_scales = held([P, 2 * N], U8, "picked101")
         nc.gpsimd.tensor_copy(
             dealt_scales[:].rearrange("p (z t c) -> p z t c", z=2, t=LANES),
             w34_scales[:].rearrange("p (z c t) -> p z t c", z=2, t=LANES),
         )
+
+        def combine(z, t, mic):
+            if mic == 0:
+                mixed[(z, t, mic)] = window[(z, t - 2)]
+            else:
+                mixed[(z, t, mic)] = held([P, S], F32, "mixed%d%d" % (z, t))
+            nc.vector.scalar_tensor_tensor(
+                mixed[(z, t, mic)][:, 0:S], proj[(z, t)][:], wr[mic][:, t : t + 1], cross[(1 - z, t, mic)],
+                MULT, (SUBTRACT, ADD)[z],
+            )
+
         for mic in range(2):
+            for z in range(2):
+                for t in HIGH:
+                    combine(z, t, mic)
+        first = {}
+        for z in range(2):
             for t in HIGH:
-                combine(0, t, mic)
-        for t in HIGH:
-            combine_aside(t)
+                first[(z, t)] = rows("first%d%d" % (z, t))
+                fetch(nc.scalar, first[(z, t)], mixed[(z, t, 0)][:].indirect(lists[0][:]))
 
-        low_words, back, z_in, first, z_high = {}, {}, {}, {}, {}
+        pairs, back, z_in, high = {}, {}, {}, {}
 
-        def round_low(c):
-            pairs = held([P, H], BF16, "z%d" % c)
+        def round_low(c, name):
+            pairs[c] = held([P, H], BF16, name)
             nc.scalar.copy(
-                pairs[:].rearrange("j (z p e) -> j z p e", z=2, e=2),
+                pairs[c][:].rearrange("j (z p e) -> j z p e", z=2, e=2),
                 sums[c][:].rearrange("j (z e p) -> j z p e", z=2, e=2),
             )
-            low_words[c] = pairs[:].bitcast(F32)
-
-        def turn_back(c):
             back[c] = bank(BACK_BANK[c])
             for z in range(2):
-                nc.tensor.transpose(part(back[c], z, P), part(low_words[c], z, P), ident[:])
+                nc.tensor.transpose(part(back[c], z, P), part(pairs[c][:].bitcast(F32), z, P), ident[:])
 
         def place_low(c):
             z_in[c] = held([P, 2 * H], BF16, "z%d" % c)
-            nc.scalar.copy(z_in[c][:].bitcast(F32).rearrange("p (n u) -> p n u", u=2)[:, :, 0], back[c][:, 0 : 2 * P])
+            nc.scalar.copy(
+                z_in[c][:].bitcast(F32).rearrange("p (n u) -> p n u", u=2),
+                back[c][:, 0 : 2 * P].unsqueeze(2).to_broadcast([P, 2 * P, 2]),
+            )
 
-        def fetch_first(c, chunks, z, dst):
-            first[(c, z)] = dst
-            for e, t in enumerate(HIGH):
-                nc.vector.tensor_copy(part(dst, e, chunks * CH), mixed[(z, t, 0)][:].indirect(offsets(0, c, chunks)))
-
-        def add_second(c, chunks, z, name):
+        def add_second(c, chunks, zs, name):
             n = chunks * CH
-            total = held([P, 2 * n], F32, name)
-            for e, t in enumerate(HIGH):
-                nc.vector.tensor_tensor(
-                    part(total, e, n), mixed[(z, t, 1)][:].indirect(offsets(1, c, chunks)), part(first[(c, z)], e, n), ADD
-                )
+            total = held([P, len(zs) * 2 * n], F32, name)
+            for a, z in enumerate(zs):
+                for e, t in enumerate(HIGH):
+                    nc.vector.tensor_tensor(
+                        part(total, 2 * a + e, n), mixed[(z, t, 1)][:].indirect(offsets(1, c, chunks)),
+                        first[(z, t)][:, c * CH : c * CH + n], ADD,
+                    )
             for d in range(chunks):
-                z_high[(c + d, z)] = total[:].rearrange("p (e j) -> p j e", e=2)[:, d * CH : (d + 1) * CH, :]
+                high[(c + d, zs)] = total[:].rearrange("p (z e j) -> p z j e", z=len(zs), e=2)[:, :, d * CH : (d + 1) * CH, :]
 
-        def high_lanes(c, z, behind):
-            fetch_first(c, 1, z, held([P, 2 * CH], F32, behind)[:])
-            add_second(c, 1, z, "high%d%d" % (c, z))
-
-        def round_high(c, z, move):
-            move(part(z_in[c], z, H).rearrange("p (j t) -> p j t", t=LANES)[:, :, 2:4], z_high[(c, z)])
+        def round_high(c, zs):
+            dst = z_in[c][:].rearrange("p (z j t) -> p z j t", z=2, t=LANES)[:, zs[0] : zs[-1] + 1, :, 2:4]
+            nc.vector.tensor_copy(dst, high[(c, zs)])
 
         out_codes = held([P, S], U32, "oc")
         out_scales = held([P, S], U8, "osc")
         out_rows = out_0.rearrange("(p t) j -> p t j", t=LANES)
         out_words = out_1[0].rearrange("p c r -> p (c r)").bitcast(I32)
-        z_codes, z_scales, result, out_bf, last = {}, {}, {}, {}, {}
+        z_codes, z_scales, result, out_f32, out_bf, last = {}, {}, {}, {}, {}, {}
 
         def out_pass(res, c, t, z):
             nc.tensor.matmul_mx(
@@ -322,11 +310,11 @@ def tile_picked_beamf_none_po_kernel(
                 start=(z == 0), stop=(z == 1),
             )
 
-        def store_out(c, out_f32):
-            nc.sync.dma_start(out_rows[:, :, c * CH : (c + 1) * CH], out_f32[:].rearrange("p (t j) -> p t j", t=LANES))
+        def store_out(c):
+            nc.sync.dma_start(out_rows[:, :, c * CH : (c + 1) * CH], out_f32[c][:].rearrange("p (t j) -> p t j", t=LANES))
 
         def interleave(move, c, src):
-            move(out_bf[c][:].rearrange("p (j t) -> p j t", t=LANES), src[:].rearrange("p (t j) -> p j t", t=LANES))
+            move(out_bf[c].rearrange("p (j t) -> p j t", t=LANES), src[:].rearrange("p (t j) -> p j t", t=LANES))
 
         def multiply(c):
             z_codes[c] = held([P, 2 * CH], U32, "zc%d" % c)
@@ -336,16 +324,16 @@ def tile_picked_beamf_none_po_kernel(
             for t in range(LANES):
                 for z in range(2):
                     out_pass(part(result[c], t, CH), c, t, z)
-            out_bf[c] = held([P, LANES * CH], BF16, "ob%d" % c)
-            out_f32 = held([P, LANES * CH], F32, "of%d" % c)
-            nc.scalar.copy(out_f32[:], result[c][:])
-            store_out(c, out_f32)
 
-        def hand_on(c):
-            nc.vector.quantize_mx(out=part(out_codes, c, CH).bitcast(FP8X4), scales=part(out_scales, c, CH), in_=out_bf[c][:])
-            if c > 0:
-                done = slice(0 if c == 1 else c * CH, (c + 1) * CH)
-                nc.sync.dma_start(out_words[:, done], out_codes[:, done].bitcast(I32))
+        def copy_out(c):
+            out_f32[c] = held([P, LANES * CH], F32, "of%d" % c)
+            nc.scalar.copy(out_f32[c][:], result[c][:])
+            store_out(c)
+
+        def hand_on(c, chunks, src):
+            done = slice(c * CH, (c + chunks) * CH)
+            nc.vector.quantize_mx(out=out_codes[:, done].bitcast(FP8X4), scales=out_scales[:, done], in_=src)
+            nc.sync.dma_start(out_words[:, done], out_codes[:, done].bitcast(I32))
 
         def last_passes(z):
             if z == 0:
@@ -359,54 +347,47 @@ def tile_picked_beamf_none_po_kernel(
                     last[t] = bank(LAST_OUT_BANK[t])
                 out_pass(last[t][:, 0:CH], LAST, t, z)
 
-        def last_out():
-            out_f32 = held([P, LANES * CH], F32, "of3")
-            for t in range(LANES):
-                move = nc.scalar.copy if t % 2 == 0 else nc.vector.tensor_copy
-                move(part(out_f32, t, CH), last[t][:, 0:CH])
-            store_out(LAST, out_f32)
-            out_bf[LAST] = held([P, LANES * CH], BF16, "ob3")
-            interleave(nc.vector.tensor_copy, LAST, out_f32)
-
-        for c in range(LAST):
-            round_low(c)
-        for c in range(2):
-            turn_back(c)
+        BOTH = (0, 1)
+        round_low(0, "window10")
+        round_low(1, "window11")
         place_low(0)
-        turn_back(2)
-        round_low(LAST)
         place_low(1)
-        turn_back(LAST)
-        early = rows("cross21", 2)
-        for z in range(2):
-            fetch_first(0, 2, z, part(early, z))
-        for z in range(2):
-            add_second(0, 2, z, "high%d" % z)
-            for c in range(2):
-                round_high(c, z, nc.scalar.copy)
+        round_low(2, "window10")
+        round_low(3, "window11")
         place_low(2)
-        place_low(LAST)
-        high_lanes(2, 0, "direct3")
+        place_low(3)
+        add_second(0, 2, BOTH, "high01")
+        add_second(2, 1, BOTH, "high2")
+        round_high(0, BOTH)
+        round_high(1, BOTH)
         multiply(0)
         multiply(1)
-        round_high(2, 0, nc.scalar.copy)
-        high_lanes(2, 1, "high1")
-        round_high(2, 1, nc.scalar.copy)
-        high_lanes(LAST, 0, "zc0")
+        add_second(LAST, 1, (0,), "z0")
+        round_high(2, BOTH)
+        add_second(LAST, 1, (1,), "z1")
         multiply(2)
-        round_high(LAST, 0, nc.scalar.copy)
-        for c in range(2):
-            interleave(nc.scalar.copy, c, result[c])
-        hand_on(0)
-        high_lanes(LAST, 1, "high21")
+        round_high(LAST, (0,))
+        round_high(LAST, (1,))
         last_passes(0)
-        round_high(LAST, 1, nc.vector.tensor_copy)
         last_passes(1)
-        hand_on(1)
-        interleave(nc.scalar.copy, 2, result[2])
-        hand_on(2)
-        last_out()
-        hand_on(LAST)
+        early_bf = held([P, 2 * LANES * CH], BF16, "ob01")
+        late_bf = held([P, 2 * LANES * CH], BF16, "ob23")
+        for c in range(LAST + 1):
+            out_bf[c] = part((early_bf, late_bf)[c // 2], c % 2, LANES * CH)
+        for c in range(2):
+            copy_out(c)
+            interleave(nc.scalar.copy, c, result[c])
+        copy_out(2)
+        hand_on(0, 2, early_bf[:])
+        interleave(nc.vector.tensor_copy, 2, out_f32[2])
+        out_f32[LAST] = held([P, LANES * CH], F32, "of3")
+        for t in range(LANES):
+            move = nc.scalar.copy if t % 2 == 0 else nc.vector.tensor_copy
+            move(part(out_f32[LAST], t, CH), last[t][:, 0:CH])
+        store_out(LAST)
+        hand_on(2, 1, out_bf[2])
+        interleave(nc.vector.tensor_copy, LAST, out_f32[LAST])
+        hand_on(LAST, 1, out_bf[LAST])
 
         for q in range(4):
             queue = nc.sync if q % 2 == 0 else nc.scalar

@@ -29,13 +29,11 @@ LAST = 3
 HALF = S // 2
 BANK = 512
 TERMS_IN_BANK = 16
-GPSIMD_TERMS = 12
 
 PROJ_BANK = ((0, 1, 0, 6), (6, 7, 7, 1))
 SUM_BANK = (2, 3, 4, 5)
 BACK_BANK = (0, 1, 6, 7)
-OUT_BANK = (2, 3, 4)
-LAST_OUT_BANK = (0, 1, 6, 5)
+OUT_BANK = ((2,), (3,), (4,), (0, 1, 6, 5))
 
 
 def tile_picked_beamf_none_po_kernel(
@@ -76,34 +74,49 @@ def tile_picked_beamf_none_po_kernel(
         for i in (RE, IM):
             for t in LOW:
                 window[(i, t)] = held([P, 2 * S], F32, "window%d%d" % (i, t))
-                nc.vector.memset(window[(i, t)][:, S : 2 * S], 0.0)
+                (nc.vector, nc.gpsimd)[i].memset(window[(i, t)][:, S : 2 * S], 0.0)
         ident = held([P, P], F32, "ident")
 
         def load_weight(dst, src):
             nc.sync.dma_start(dst[:], src.rearrange("(p t) o -> p (t o)", t=LANES))
 
-        def load_scale_rows(dst, src):
+        def load_scale_rows(dst, src, name):
+            staged_w = held([P, 4, N // 4], I32, name)
+            nc.sync.dma_start(staged_w[0:4], src[0].bitcast(I32).rearrange("(q r) c -> r q c", q=4))
             for q in range(4):
-                nc.sync.dma_start(dst[q:P:32].bitcast(I32), src[0, q:16:4, :].bitcast(I32))
+                nc.vector.tensor_copy(dst.bitcast(I32)[32 * q : 32 * q + 4], staged_w[0:4, q])
 
         w_rows = [w.rearrange("(p q) c -> p q c", q=LANES) for w in (w1, w2)]
-        nc.sync.dma_start(raw[RE][:], w_rows[RE])
         nc.sync.dma_start(offs_t[:], offs)
-        load_scale_rows(xs[:, :], x_scales)
+        staged = held([P, 2, T // 4], I32, "staged")
+        for h in range(2):
+            nc.sync.dma_start(
+                staged[64 * h : 64 * h + 4], x_scales[0, 8 * h : 8 * h + 8, :].bitcast(I32).rearrange("(q r) c -> r q c", q=2)
+            )
+        for h in range(2):
+            for q in range(2):
+                to = 64 * h + 32 * q
+                nc.vector.tensor_copy(xs[:].bitcast(I32)[to : to + 4], staged[64 * h : 64 * h + 4, q])
+        load_scale_rows(w34_scales[:, 0:N], w3_scales, "staged3")
+        load_scale_rows(w34_scales[:, N : 2 * N], w4_scales, "staged4")
+        nc.sync.dma_start(raw[RE][:], w_rows[RE])
         nc.sync.dma_start(xw[:], x_words[0].rearrange("p c r -> p (c r)").bitcast(I32))
-        nc.sync.dma_start(m1_t[:], m1)
         nc.sync.dma_start(w34_words[0][:].bitcast(I32), w3_words[0].bitcast(I32))
+        nc.sync.dma_start(m1_t[:], m1)
         nc.sync.dma_start(w34_words[1][:].bitcast(I32), w4_words[0].bitcast(I32))
         nc.sync.dma_start(raw[IM][:], w_rows[IM])
         nc.sync.dma_start(m2_t[:], m2)
         load_weight(wi[0], wi1)
+        load_weight(wi[1], wi2)
         load_weight(wr[0], wr1)
         load_weight(wr[1], wr2)
-        load_weight(wi[1], wi2)
         make_identity(nc, ident[:])
-        load_scale_rows(w34_scales[:, 0:N], w3_scales)
-        load_scale_rows(w34_scales[:, N : 2 * N], w4_scales)
         lists = (m1_t, m2_t)
+        dealt_scales = held([P, 2 * N], U8, "w34sd")
+        nc.gpsimd.tensor_copy(
+            dealt_scales[:].rearrange("p (z t c) -> p z t c", z=2, t=LANES),
+            w34_scales[:].rearrange("p (z c t) -> p z t c", z=2, t=LANES),
+        )
 
         def offsets(mic, c, chunks):
             return lists[mic][:, c * CH // 16 : (c + chunks) * CH // 16]
@@ -134,8 +147,8 @@ def tile_picked_beamf_none_po_kernel(
                 rhs=xg_words[:, frames].bitcast(FP8X4), rhs_scale=xg_scales[:, frames], start=True, stop=True,
             )
 
-        def fill(i, t, frames=slice(0, S)):
-            nc.scalar.copy(window[(i, t)][:, frames], proj[(i, t)][:, frames])
+        def fill(i, t, frames=slice(0, S), move=nc.scalar.copy):
+            move(window[(i, t)][:, frames], proj[(i, t)][:, frames])
 
         def deal_words(z, name, engine):
             w34_dealt[z] = held([P, 2 * N], U8, name)
@@ -146,23 +159,24 @@ def tile_picked_beamf_none_po_kernel(
 
         for u in range(2):
             grouped[(RE, u)] = held([P, 2 * H], BF16, "grouped%d" % u)
-        regroup(RE, 0, nc.vector.tensor_copy, slice(0, P // 2))
-        regroup(RE, 0, nc.scalar.copy, slice(P // 2, P))
+        regroup(RE, 0, nc.vector.tensor_copy)
         regroup(RE, 1, nc.scalar.copy)
-        quantise_w(RE, 0, "wc00")
+        for u in range(2):
+            quantise_w(RE, u, "wc0%d" % u)
         for h in range(2):
             frames = slice(h * HALF, (h + 1) * HALF)
             nc.vector.tensor_copy(xg_words[:, frames], xw[:].bitcast(U32).indirect(part(offs_t, h, HALF // 16)))
-            project(RE, 0, frames, None if h == 0 else SUM_BANK[0])
-            fill(RE, 0, frames)
-        project(RE, 1)
-        quantise_w(RE, 1, "xw")
+            for t in LOW:
+                project(RE, t, frames, None if h == 0 else SUM_BANK[t])
+                fill(RE, t, frames, nc.vector.tensor_copy if (h, t) == (1, 0) else nc.scalar.copy)
         project(RE, 2)
-        fill(RE, 1)
-        deal_words(0, "w3d", nc.vector)
-        deal_words(1, "w3w", nc.gpsimd)
+        for z in range(2):
+            deal_words(z, "w34d%d" % z, nc.gpsimd)
 
         picked, cross, mixed, sums, added = {}, {}, {}, {}, {}
+        for t in LOW:
+            for mic in range(2):
+                picked[(t, mic)] = rows("picked%d%d" % (t, mic), 2)
 
         def fetch(engine, dst, src):
             if engine is nc.scalar:
@@ -171,17 +185,20 @@ def tile_picked_beamf_none_po_kernel(
                 nc.vector.tensor_copy(dst, src)
 
         def look_up(engine, i, t, mic):
-            picked[(i, t, mic)] = rows("picked%d%d%d" % (i, t, mic))
-            fetch(engine, picked[(i, t, mic)], window[(i, t)][:].indirect(lists[mic][:]))
+            fetch(engine, part(picked[(t, mic)], i), window[(i, t)][:].indirect(lists[mic][:]))
 
-        def cross_term(i, t, mic, name=None):
-            cross[(i, t, mic)] = rows(name or "cross%d%d%d" % (i, t, mic))
+        def cross_term(i, t, mic):
+            cross[(i, t, mic)] = rows("cross%d%d%d" % (i, t, mic))
             nc.scalar.activation(cross[(i, t, mic)], proj[(i, t)][:], COPY, scale=wi[mic][:, t : t + 1])
 
+        minus_wi = held([P, 2 * LANES], F32, "minus_wi")
+        for mic in range(2):
+            nc.gpsimd.tensor_scalar(part(minus_wi, mic, LANES), wi[mic][:], -1.0, 0.0, MULT, ADD)
         look_up(nc.vector, RE, 0, 0)
         look_up(nc.scalar, RE, 1, 0)
         look_up(nc.scalar, RE, 0, 1)
-        cross_term(RE, 2, 0)
+        for mic in range(2):
+            cross_term(RE, 2, mic)
         for u in range(2):
             grouped[(IM, u)] = held([P, 2 * H], BF16, "grouped%d" % u)
             regroup(IM, u, nc.vector.tensor_copy)
@@ -194,13 +211,8 @@ def tile_picked_beamf_none_po_kernel(
         project(RE, 3)
         project(IM, 2)
         look_up(nc.vector, RE, 1, 1)
-        for t in LOW:
-            for mic in range(2):
-                look_up(nc.vector, IM, t, mic)
-        cross_term(RE, 2, 1, "wc10")
-        minus_wi = held([P, 2 * LANES], F32, "minus_wi")
-        for mic in range(2):
-            nc.scalar.activation(part(minus_wi, mic, LANES), wi[mic][:], COPY, scale=-1.0)
+        for t, mic in ((0, 0), (0, 1), (1, 0)):
+            look_up(nc.vector, IM, t, mic)
         for mic in range(2):
             cross_term(IM, 3, mic)
             cross_term(RE, 3, mic)
@@ -217,37 +229,35 @@ def tile_picked_beamf_none_po_kernel(
                 )
                 added[c] += 1
 
-        def weight_of(i, t, mic, z):
-            if z == i:
-                return wr[mic][:, t : t + 1]
-            if i == RE:
-                return wi[mic][:, t : t + 1]
-            return part(minus_wi, mic, LANES)[:, t : t + 1]
+        def scale_aside(dst, src, w):
+            nc.gpsimd.tensor_scalar(dst, src, w, 0.0, MULT, ADD)
 
-        look_ups = ((RE, 0, 0), (RE, 1, 0), (RE, 0, 1), (RE, 1, 1), (IM, 0, 0), (IM, 0, 1), (IM, 1, 0), (IM, 1, 1))
-        early_terms = rows("grouped1", 6)
-        for n in range(TERMS_IN_BANK):
-            (i, t, mic), z = look_ups[n // 2], n % 2
-            term = part(early_terms, n) if n < 6 else rows("term%d" % n)
-            if n < GPSIMD_TERMS:
-                nc.gpsimd.tensor_scalar(term, picked[(i, t, mic)], weight_of(i, t, mic, z), 0.0, MULT, ADD)
-            else:
-                nc.scalar.activation(term, picked[(i, t, mic)], COPY, scale=weight_of(i, t, mic, z))
-            add_term(term, t, z)
-
-        dealt_scales = held([P, 2 * N], U8, "picked101")
-        nc.gpsimd.tensor_copy(
-            dealt_scales[:].rearrange("p (z t c) -> p z t c", z=2, t=LANES),
-            w34_scales[:].rearrange("p (z c t) -> p z t c", z=2, t=LANES),
-        )
+        pairs_of = [(t, mic) for mic in range(2) for t in LOW]
+        early_terms = rows("grouped1", 4)
+        for n, (t, mic) in enumerate(pairs_of):
+            scale_aside(part(early_terms, n), part(picked[(t, mic)], RE), wi[mic][:, t : t + 1])
+            add_term(part(early_terms, n), t, 1)
+        for t, mic in ((0, 0), (0, 1), (1, 0)):
+            direct = rows("direct%d%d" % (t, mic), 2)
+            scale_aside(direct, picked[(t, mic)], wr[mic][:, t : t + 1])
+            for z in range(2):
+                add_term(part(direct, z), t, z)
+            term = rows("minus%d%d" % (t, mic))
+            scale_aside(term, part(picked[(t, mic)], IM), part(minus_wi, mic, LANES)[:, t : t + 1])
+            add_term(term, t, 0)
+        for z in range(2):
+            term = rows("scaled%d" % z)
+            w = (part(minus_wi, 1, LANES), wr[1])[z][:, 1:2]
+            nc.scalar.activation(term, window[(IM, 1)][:].indirect(lists[1][:]), COPY, scale=w)
+            add_term(term, 1, z)
+        term = rows("direct11")
+        scale_aside(term, part(picked[(1, 1)], RE), wr[1][:, 1:2])
+        add_term(term, 1, 0)
 
         def combine(z, t, mic):
-            if mic == 0:
-                mixed[(z, t, mic)] = window[(z, t - 2)]
-            else:
-                mixed[(z, t, mic)] = held([P, S], F32, "mixed%d%d" % (z, t))
+            mixed[(z, t, mic)] = held([P, S], F32, "mixed%d%d%d" % (z, t, mic))
             nc.vector.scalar_tensor_tensor(
-                mixed[(z, t, mic)][:, 0:S], proj[(z, t)][:], wr[mic][:, t : t + 1], cross[(1 - z, t, mic)],
+                mixed[(z, t, mic)][:], proj[(z, t)][:], wr[mic][:, t : t + 1], cross[(1 - z, t, mic)],
                 MULT, (SUBTRACT, ADD)[z],
             )
 
@@ -255,139 +265,148 @@ def tile_picked_beamf_none_po_kernel(
             for z in range(2):
                 for t in HIGH:
                     combine(z, t, mic)
-        first = {}
-        for z in range(2):
-            for t in HIGH:
-                first[(z, t)] = rows("first%d%d" % (z, t))
-                fetch(nc.scalar, first[(z, t)], mixed[(z, t, 0)][:].indirect(lists[0][:]))
 
-        pairs, back, z_in, high = {}, {}, {}, {}
+        first, pairs, back, z_in, high = {}, {}, {}, {}, {}
+        SPANS = ((0, 1), (1, 1), (2, 1), (3, 1))
 
-        def round_low(c, name):
+        def fetch_first(engine, h, z, t, dst):
+            first[(h, z, t)] = dst
+            fetch(engine, dst, mixed[(z, t, 0)][:].indirect(offsets(0, 2 * h, 2)))
+
+        def add_second(c0, chunks, name):
+            n = chunks * CH
+            h, lo = divmod(c0 * CH, HALF)
+            total = held([P, 4 * n], F32, name)
+            for z in range(2):
+                for e, t in enumerate(HIGH):
+                    nc.vector.tensor_tensor(
+                        part(total, 2 * z + e, n), mixed[(z, t, 1)][:].indirect(offsets(1, c0, chunks)),
+                        first[(h, z, t)][:, lo : lo + n], ADD,
+                    )
+            for d in range(chunks):
+                high[c0 + d] = total[:].rearrange("p (z e j) -> p z j e", z=2, e=2)[:, :, d * CH : (d + 1) * CH]
+
+        def round_low(span, d, name):
+            c0, chunks = SPANS[span]
+            c = c0 + d
             pairs[c] = held([P, H], BF16, name)
             nc.scalar.copy(
                 pairs[c][:].rearrange("j (z p e) -> j z p e", z=2, e=2),
                 sums[c][:].rearrange("j (z e p) -> j z p e", z=2, e=2),
             )
-            back[c] = bank(BACK_BANK[c])
+            if d == 0:
+                back[span] = bank(BACK_BANK[span])
             for z in range(2):
-                nc.tensor.transpose(part(back[c], z, P), part(pairs[c][:].bitcast(F32), z, P), ident[:])
+                nc.tensor.transpose(part(back[span], z * chunks + d, P), part(pairs[c][:].bitcast(F32), z, P), ident[:])
 
-        def place_low(c):
-            z_in[c] = held([P, 2 * H], BF16, "z%d" % c)
+        def place_low(span):
+            n = 2 * SPANS[span][1] * CH
+            z_in[span] = held([P, LANES * n], BF16, "z%d" % span)
             nc.scalar.copy(
-                z_in[c][:].bitcast(F32).rearrange("p (n u) -> p n u", u=2),
-                back[c][:, 0 : 2 * P].unsqueeze(2).to_broadcast([P, 2 * P, 2]),
+                z_in[span][:].bitcast(F32).rearrange("p (n u) -> p n u", u=2),
+                back[span][:, 0:n].unsqueeze(2).to_broadcast([P, n, 2]),
             )
 
-        def add_second(c, chunks, zs, name):
-            n = chunks * CH
-            total = held([P, len(zs) * 2 * n], F32, name)
-            for a, z in enumerate(zs):
-                for e, t in enumerate(HIGH):
-                    nc.vector.tensor_tensor(
-                        part(total, 2 * a + e, n), mixed[(z, t, 1)][:].indirect(offsets(1, c, chunks)),
-                        first[(z, t)][:, c * CH : c * CH + n], ADD,
-                    )
-            for d in range(chunks):
-                high[(c + d, zs)] = total[:].rearrange("p (z e j) -> p z j e", z=len(zs), e=2)[:, :, d * CH : (d + 1) * CH, :]
-
-        def round_high(c, zs):
-            dst = z_in[c][:].rearrange("p (z j t) -> p z j t", z=2, t=LANES)[:, zs[0] : zs[-1] + 1, :, 2:4]
-            nc.vector.tensor_copy(dst, high[(c, zs)])
+        def round_high(span, z, count=1):
+            dst = z_in[span][:].rearrange("p (z j t) -> p z j t", z=2, t=LANES)[:, z : z + count, :, 2:4]
+            nc.vector.tensor_copy(dst, high[span][:, z : z + count])
 
         out_codes = held([P, S], U32, "oc")
         out_scales = held([P, S], U8, "osc")
         out_rows = out_0.rearrange("(p t) j -> p t j", t=LANES)
         out_words = out_1[0].rearrange("p c r -> p (c r)").bitcast(I32)
-        z_codes, z_scales, result, out_f32, out_bf, last = {}, {}, {}, {}, {}, {}
+        z_codes, z_scales, result, out_f32, out_bf = {}, {}, {}, {}, {}
 
-        def out_pass(res, c, t, z):
+        def quantise_z(span, zs=(0, 1)):
+            n = SPANS[span][1] * CH
+            if zs[0] == 0:
+                z_codes[span] = held([P, 2 * n], U32, "zc%d" % span)
+                z_scales[span] = held([P, 2 * n], U8, "zs%d" % span)
+            cols = slice(zs[0] * n, (zs[-1] + 1) * n)
+            nc.vector.quantize_mx(
+                out=z_codes[span][:, cols].bitcast(FP8X4), scales=z_scales[span][:, cols],
+                in_=z_in[span][:, LANES * cols.start : LANES * cols.stop],
+            )
+
+        def out_pass(res, span, t, z):
+            n = SPANS[span][1] * CH
             nc.tensor.matmul_mx(
                 out=res,
                 lhsT=part(w34_dealt[z], t, 2 * P).bitcast(FP4X4), lhsT_scale=part(dealt_scales, LANES * z + t, P),
-                rhs=part(z_codes[c], z, CH).bitcast(FP8X4), rhs_scale=part(z_scales[c], z, CH),
+                rhs=part(z_codes[span], z, n).bitcast(FP8X4), rhs_scale=part(z_scales[span], z, n),
                 start=(z == 0), stop=(z == 1),
             )
 
-        def store_out(c):
-            nc.sync.dma_start(out_rows[:, :, c * CH : (c + 1) * CH], out_f32[c][:].rearrange("p (t j) -> p t j", t=LANES))
-
-        def interleave(move, c, src):
-            move(out_bf[c].rearrange("p (j t) -> p j t", t=LANES), src[:].rearrange("p (t j) -> p j t", t=LANES))
-
-        def multiply(c):
-            z_codes[c] = held([P, 2 * CH], U32, "zc%d" % c)
-            z_scales[c] = held([P, 2 * CH], U8, "zs%d" % c)
-            nc.vector.quantize_mx(out=z_codes[c][:].bitcast(FP8X4), scales=z_scales[c][:], in_=z_in[c][:])
-            result[c] = bank(OUT_BANK[c])
+        def multiply(span):
+            n = SPANS[span][1] * CH
+            banks = OUT_BANK[span]
+            per = LANES // len(banks)
+            result[span] = [bank(b) for b in banks]
             for t in range(LANES):
                 for z in range(2):
-                    out_pass(part(result[c], t, CH), c, t, z)
+                    out_pass(part(result[span][t // per], t % per, n), span, t, z)
 
-        def copy_out(c):
-            out_f32[c] = held([P, LANES * CH], F32, "of%d" % c)
-            nc.scalar.copy(out_f32[c][:], result[c][:])
-            store_out(c)
+        def copy_out(span, moves):
+            c0, chunks = SPANS[span]
+            n = chunks * CH
+            out_f32[span] = held([P, LANES * n], F32, "of%d" % span)
+            width = LANES * n // len(result[span])
+            for b, res in enumerate(result[span]):
+                moves[b](part(out_f32[span], b, width), res[:, 0:width])
+            nc.sync.dma_start(out_rows[:, :, c0 * CH : c0 * CH + n], out_f32[span][:].rearrange("p (t j) -> p t j", t=LANES))
 
-        def hand_on(c, chunks, src):
-            done = slice(c * CH, (c + chunks) * CH)
-            nc.vector.quantize_mx(out=out_codes[:, done].bitcast(FP8X4), scales=out_scales[:, done], in_=src)
+        def interleave(move, dst, src):
+            move(dst.rearrange("p (j t) -> p j t", t=LANES), src[:].rearrange("p (t j) -> p j t", t=LANES))
+
+        def hand_on(h, src):
+            done = slice(h * HALF, (h + 1) * HALF)
+            nc.vector.quantize_mx(out=out_codes[:, done].bitcast(FP8X4), scales=out_scales[:, done], in_=src[:])
             nc.sync.dma_start(out_words[:, done], out_codes[:, done].bitcast(I32))
 
-        def last_passes(z):
-            if z == 0:
-                z_codes[LAST] = held([P, 2 * CH], U32, "zc3")
-                z_scales[LAST] = held([P, 2 * CH], U8, "zs3")
-            nc.vector.quantize_mx(
-                out=part(z_codes[LAST], z, CH).bitcast(FP8X4), scales=part(z_scales[LAST], z, CH), in_=part(z_in[LAST], z, H)
-            )
-            for t in range(LANES):
-                if z == 0:
-                    last[t] = bank(LAST_OUT_BANK[t])
-                out_pass(last[t][:, 0:CH], LAST, t, z)
-
-        BOTH = (0, 1)
-        round_low(0, "window10")
-        round_low(1, "window11")
+        first_tile = held([P, 8 * HALF], F32, "first")
+        for h in range(2):
+            for z in range(2):
+                for e, t in enumerate(HIGH):
+                    engine = nc.vector if (h, z, t) == (1, 1, 2) else nc.scalar
+                    fetch_first(engine, h, z, t, part(first_tile, 4 * h + 2 * z + e, HALF))
+        add_second(0, 2, "high0")
+        add_second(2, 1, "high2")
+        round_low(0, 0, "pairs0")
+        round_low(1, 0, "pairs1")
         place_low(0)
         place_low(1)
-        round_low(2, "window10")
-        round_low(3, "window11")
+        round_low(2, 0, "pairs0")
+        round_low(3, 0, "pairs1")
         place_low(2)
         place_low(3)
-        add_second(0, 2, BOTH, "high01")
-        add_second(2, 1, BOTH, "high2")
-        round_high(0, BOTH)
-        round_high(1, BOTH)
-        multiply(0)
-        multiply(1)
-        add_second(LAST, 1, (0,), "z0")
-        round_high(2, BOTH)
-        add_second(LAST, 1, (1,), "z1")
-        multiply(2)
-        round_high(LAST, (0,))
-        round_high(LAST, (1,))
-        last_passes(0)
-        last_passes(1)
-        early_bf = held([P, 2 * LANES * CH], BF16, "ob01")
-        late_bf = held([P, 2 * LANES * CH], BF16, "ob23")
-        for c in range(LAST + 1):
-            out_bf[c] = part((early_bf, late_bf)[c // 2], c % 2, LANES * CH)
         for c in range(2):
-            copy_out(c)
-            interleave(nc.scalar.copy, c, result[c])
-        copy_out(2)
-        hand_on(0, 2, early_bf[:])
-        interleave(nc.vector.tensor_copy, 2, out_f32[2])
-        out_f32[LAST] = held([P, LANES * CH], F32, "of3")
-        for t in range(LANES):
-            move = nc.scalar.copy if t % 2 == 0 else nc.vector.tensor_copy
-            move(part(out_f32[LAST], t, CH), last[t][:, 0:CH])
-        store_out(LAST)
-        hand_on(2, 1, out_bf[2])
-        interleave(nc.vector.tensor_copy, LAST, out_f32[LAST])
-        hand_on(LAST, 1, out_bf[LAST])
+            round_high(c, 0, 2)
+        for c in range(2):
+            quantise_z(c)
+            multiply(c)
+        add_second(LAST, 1, "z0")
+        round_high(2, 0, 2)
+        for z in range(2):
+            round_high(LAST, z)
+        quantise_z(2)
+        multiply(2)
+        result[LAST] = [bank(b) for b in OUT_BANK[LAST]]
+        for z in range(2):
+            quantise_z(LAST, (z,))
+            for t in range(LANES):
+                out_pass(result[LAST][t][:, 0:CH], LAST, t, z)
+        early_bf = held([P, LANES * HALF], BF16, "ob0")
+        late_bf = held([P, LANES * HALF], BF16, "ob1")
+        for c in range(2):
+            copy_out(c, (nc.scalar.copy,))
+        interleave(nc.scalar.copy, part(early_bf, 0, LANES * CH), result[0][0])
+        interleave(nc.vector.tensor_copy, part(early_bf, 1, LANES * CH), out_f32[1])
+        copy_out(2, (nc.scalar.copy,))
+        hand_on(0, early_bf)
+        interleave(nc.vector.tensor_copy, part(late_bf, 0, LANES * CH), out_f32[2])
+        copy_out(LAST, (nc.scalar.copy, nc.vector.tensor_copy, nc.scalar.copy, nc.vector.tensor_copy))
+        interleave(nc.vector.tensor_copy, part(late_bf, 1, LANES * CH), out_f32[LAST])
+        hand_on(1, late_bf)
 
         for q in range(4):
             queue = nc.sync if q % 2 == 0 else nc.scalar

@@ -74,36 +74,24 @@ def tile_picked_beamf_none_po_kernel(
         for i in (RE, IM):
             for t in LOW:
                 window[(i, t)] = held([P, 2 * S], F32, "window%d%d" % (i, t))
-                (nc.vector, nc.gpsimd)[i].memset(window[(i, t)][:, S : 2 * S], 0.0)
+                nc.vector.memset(window[(i, t)][:, S : 2 * S], 0.0)
         ident = held([P, P], F32, "ident")
 
         def load_weight(dst, src):
             nc.sync.dma_start(dst[:], src.rearrange("(p t) o -> p (t o)", t=LANES))
 
-        def load_scale_rows(dst, src, name):
-            staged_w = held([P, 4, N // 4], I32, name)
-            nc.sync.dma_start(staged_w[0:4], src[0].bitcast(I32).rearrange("(q r) c -> r q c", q=4))
+        def load_scale_rows(dst, src):
             for q in range(4):
-                nc.vector.tensor_copy(dst.bitcast(I32)[32 * q : 32 * q + 4], staged_w[0:4, q])
+                nc.sync.dma_start(dst[q:P:32].bitcast(I32), src[0, q:16:4, :].bitcast(I32))
 
         w_rows = [w.rearrange("(p q) c -> p q c", q=LANES) for w in (w1, w2)]
-        nc.sync.dma_start(offs_t[:], offs)
-        staged = held([P, 2, T // 4], I32, "staged")
-        for h in range(2):
-            nc.sync.dma_start(
-                staged[64 * h : 64 * h + 4], x_scales[0, 8 * h : 8 * h + 8, :].bitcast(I32).rearrange("(q r) c -> r q c", q=2)
-            )
-        for h in range(2):
-            for q in range(2):
-                to = 64 * h + 32 * q
-                nc.vector.tensor_copy(xs[:].bitcast(I32)[to : to + 4], staged[64 * h : 64 * h + 4, q])
-        load_scale_rows(w34_scales[:, 0:N], w3_scales, "staged3")
-        load_scale_rows(w34_scales[:, N : 2 * N], w4_scales, "staged4")
         nc.sync.dma_start(raw[RE][:], w_rows[RE])
+        nc.sync.dma_start(offs_t[:], offs)
+        load_scale_rows(xs[:, :], x_scales)
         nc.sync.dma_start(xw[:], x_words[0].rearrange("p c r -> p (c r)").bitcast(I32))
         nc.sync.dma_start(w34_words[0][:].bitcast(I32), w3_words[0].bitcast(I32))
-        nc.sync.dma_start(m1_t[:], m1)
         nc.sync.dma_start(w34_words[1][:].bitcast(I32), w4_words[0].bitcast(I32))
+        nc.sync.dma_start(m1_t[:], m1)
         nc.sync.dma_start(raw[IM][:], w_rows[IM])
         nc.sync.dma_start(m2_t[:], m2)
         load_weight(wi[0], wi1)
@@ -111,12 +99,9 @@ def tile_picked_beamf_none_po_kernel(
         load_weight(wr[0], wr1)
         load_weight(wr[1], wr2)
         make_identity(nc, ident[:])
+        load_scale_rows(w34_scales[:, 0:N], w3_scales)
+        load_scale_rows(w34_scales[:, N : 2 * N], w4_scales)
         lists = (m1_t, m2_t)
-        dealt_scales = held([P, 2 * N], U8, "w34sd")
-        nc.gpsimd.tensor_copy(
-            dealt_scales[:].rearrange("p (z t c) -> p z t c", z=2, t=LANES),
-            w34_scales[:].rearrange("p (z c t) -> p z t c", z=2, t=LANES),
-        )
 
         def offsets(mic, c, chunks):
             return lists[mic][:, c * CH // 16 : (c + chunks) * CH // 16]
@@ -150,28 +135,30 @@ def tile_picked_beamf_none_po_kernel(
         def fill(i, t, frames=slice(0, S), move=nc.scalar.copy):
             move(window[(i, t)][:, frames], proj[(i, t)][:, frames])
 
-        def deal_words(z, name, engine):
-            w34_dealt[z] = held([P, 2 * N], U8, name)
-            engine.tensor_copy(
-                w34_dealt[z][:].rearrange("p (t c e) -> p t c e", t=LANES, e=2),
-                w34_words[z][:].rearrange("p (c t e) -> p t c e", t=LANES, e=2),
+        def deal_words(z):
+            w34_dealt[z] = held([P, 2 * N], U8, "w34d%d" % z)
+            nc.scalar.copy(
+                w34_dealt[z][:].bitcast(U16).rearrange("p (t c) -> p t c", t=LANES),
+                w34_words[z][:].bitcast(U16).rearrange("p (c t) -> p t c", t=LANES),
             )
 
         for u in range(2):
             grouped[(RE, u)] = held([P, 2 * H], BF16, "grouped%d" % u)
-        regroup(RE, 0, nc.vector.tensor_copy)
+        regroup(RE, 0, nc.vector.tensor_copy, slice(0, P // 2))
+        regroup(RE, 0, nc.scalar.copy, slice(P // 2, P))
         regroup(RE, 1, nc.scalar.copy)
-        for u in range(2):
-            quantise_w(RE, u, "wc0%d" % u)
+        quantise_w(RE, 0, "wc00")
+        for z in range(2):
+            deal_words(z)
         for h in range(2):
             frames = slice(h * HALF, (h + 1) * HALF)
             nc.vector.tensor_copy(xg_words[:, frames], xw[:].bitcast(U32).indirect(part(offs_t, h, HALF // 16)))
+            if h == 1:
+                quantise_w(RE, 1, "xw")
             for t in LOW:
                 project(RE, t, frames, None if h == 0 else SUM_BANK[t])
                 fill(RE, t, frames, nc.vector.tensor_copy if (h, t) == (1, 0) else nc.scalar.copy)
         project(RE, 2)
-        for z in range(2):
-            deal_words(z, "w34d%d" % z, nc.gpsimd)
 
         picked, cross, mixed, sums, added = {}, {}, {}, {}, {}
         for t in LOW:
@@ -266,6 +253,11 @@ def tile_picked_beamf_none_po_kernel(
                 for t in HIGH:
                     combine(z, t, mic)
 
+        dealt_scales = held([P, 2 * N], U8, "cross131")
+        nc.vector.tensor_copy(
+            dealt_scales[:].rearrange("p (z t c) -> p z t c", z=2, t=LANES),
+            w34_scales[:].rearrange("p (z c t) -> p z t c", z=2, t=LANES),
+        )
         first, pairs, back, z_in, high = {}, {}, {}, {}, {}
         SPANS = ((0, 1), (1, 1), (2, 1), (3, 1))
 

@@ -33,7 +33,7 @@ TERMS_IN_BANK = 16
 PROJ_BANK = ((0, 1, 0, 6), (6, 7, 7, 1))
 SUM_BANK = (2, 3, 4, 5)
 BACK_BANK = (0, 1, 6, 7)
-OUT_BANK = ((2,), (3,), (4,), (0, 1, 6, 5))
+OUT_BANK = (2, 3, 4, 5)
 
 
 def tile_picked_beamf_none_po_kernel(
@@ -63,13 +63,15 @@ def tile_picked_beamf_none_po_kernel(
         xw = held([P, T], I32, "xw")
         xs = held([P, T], U8, "xs")
         w34_words = [held([P, 2 * N], U8, "w3w"), held([P, 2 * N], U8, "w4w")]
-        w34_scales = held([P, 2 * N], U8, "w34s")
+        w34_scales = held([P, N], U8, "w34s")
+        w4_dealt_scales = held([P, N], U8, "w4sd")
         raw = [held([P, LANES, H], F32, "raw%d" % i) for i in (RE, IM)]
         wr = [held([P, LANES], F32, "wr%d" % mic) for mic in range(2)]
         wi = [held([P, LANES], F32, "wi%d" % mic) for mic in range(2)]
 
         nc.gpsimd.memset(xs[:].bitcast(I32), 0)
         nc.vector.memset(w34_scales[:].bitcast(I32), 0)
+        nc.vector.memset(w4_dealt_scales[:].bitcast(I32), 0)
         window = {}
         for i in (RE, IM):
             for t in LOW:
@@ -80,9 +82,9 @@ def tile_picked_beamf_none_po_kernel(
         def load_weight(dst, src):
             nc.sync.dma_start(dst[:], src.rearrange("(p t) o -> p (t o)", t=LANES))
 
-        def load_scale_rows(dst, src):
+        def load_scale_rows(dst, src, base=0):
             for q in range(4):
-                nc.sync.dma_start(dst[q:P:32].bitcast(I32), src[0, q:16:4, :].bitcast(I32))
+                nc.sync.dma_start(dst[base + q : P : 32].bitcast(I32), src[0, q:16:4, :].bitcast(I32))
 
         w_rows = [w.rearrange("(p q) c -> p q c", q=LANES) for w in (w1, w2)]
         nc.sync.dma_start(raw[RE][:], w_rows[RE])
@@ -99,8 +101,8 @@ def tile_picked_beamf_none_po_kernel(
         load_weight(wr[0], wr1)
         load_weight(wr[1], wr2)
         make_identity(nc, ident[:])
-        load_scale_rows(w34_scales[:, 0:N], w3_scales)
-        load_scale_rows(w34_scales[:, N : 2 * N], w4_scales)
+        load_scale_rows(w34_scales[:, :], w3_scales)
+        load_scale_rows(w34_scales[:, :], w4_scales, 4)
         lists = (m1_t, m2_t)
 
         def offsets(mic, c, chunks):
@@ -180,7 +182,7 @@ def tile_picked_beamf_none_po_kernel(
 
         minus_wi = held([P, 2 * LANES], F32, "minus_wi")
         for mic in range(2):
-            nc.gpsimd.tensor_scalar(part(minus_wi, mic, LANES), wi[mic][:], -1.0, 0.0, MULT, ADD)
+            nc.scalar.activation(part(minus_wi, mic, LANES), wi[mic][:], COPY, scale=-1.0)
         look_up(nc.vector, RE, 0, 0)
         look_up(nc.scalar, RE, 1, 0)
         look_up(nc.scalar, RE, 0, 1)
@@ -232,19 +234,15 @@ def tile_picked_beamf_none_po_kernel(
             term = rows("minus%d%d" % (t, mic))
             scale_aside(term, part(picked[(t, mic)], IM), part(minus_wi, mic, LANES)[:, t : t + 1])
             add_term(term, t, 0)
-        for z in range(2):
-            term = rows("scaled%d" % z)
-            w = (part(minus_wi, 1, LANES), wr[1])[z][:, 1:2]
-            nc.scalar.activation(term, window[(IM, 1)][:].indirect(lists[1][:]), COPY, scale=w)
-            add_term(term, 1, z)
-        term = rows("direct11")
-        scale_aside(term, part(picked[(1, 1)], RE), wr[1][:, 1:2])
-        add_term(term, 1, 0)
+        look_up(nc.scalar, IM, 1, 1)
 
         def combine(z, t, mic):
-            mixed[(z, t, mic)] = held([P, S], F32, "mixed%d%d%d" % (z, t, mic))
+            if mic == 0:
+                mixed[(z, t, mic)] = window[(z, t - 2)]
+            else:
+                mixed[(z, t, mic)] = held([P, S], F32, "mixed%d%d" % (z, t))
             nc.vector.scalar_tensor_tensor(
-                mixed[(z, t, mic)][:], proj[(z, t)][:], wr[mic][:, t : t + 1], cross[(1 - z, t, mic)],
+                mixed[(z, t, mic)][:, 0:S], proj[(z, t)][:], wr[mic][:, t : t + 1], cross[(1 - z, t, mic)],
                 MULT, (SUBTRACT, ADD)[z],
             )
 
@@ -253,30 +251,34 @@ def tile_picked_beamf_none_po_kernel(
                 for t in HIGH:
                     combine(z, t, mic)
 
-        dealt_scales = held([P, 2 * N], U8, "cross131")
+        both_dealt = held([P, N], U8, "cross131")
         nc.vector.tensor_copy(
-            dealt_scales[:].rearrange("p (z t c) -> p z t c", z=2, t=LANES),
-            w34_scales[:].rearrange("p (z c t) -> p z t c", z=2, t=LANES),
+            both_dealt[:].rearrange("p (t c) -> p t c", t=LANES), w34_scales[:].rearrange("p (c t) -> p t c", t=LANES)
         )
-        first, pairs, back, z_in, high = {}, {}, {}, {}, {}
+        for q in range(4):
+            nc.sync.dma_start(w4_dealt_scales[q:P:32].bitcast(I32), both_dealt[4 + q : P : 32].bitcast(I32))
+        dealt_scales = (both_dealt, w4_dealt_scales)
+        late_terms = rows("picked10", 3)
+        nc.vector.tensor_scalar(late_terms[:, 0 : 2 * S], picked[(1, 1)], wr[1][:, 1:2], None, MULT)
+        nc.vector.tensor_scalar(part(late_terms, 2), part(picked[(1, 1)], IM), part(minus_wi, 1, LANES)[:, 1:2], None, MULT)
+        for n in range(3):
+            add_term(part(late_terms, n), 1, n % 2)
+        first, pairs, back, z_in, high, total = {}, {}, {}, {}, {}, {}
         SPANS = ((0, 1), (1, 1), (2, 1), (3, 1))
 
-        def fetch_first(engine, h, z, t, dst):
-            first[(h, z, t)] = dst
-            fetch(engine, dst, mixed[(z, t, 0)][:].indirect(offsets(0, 2 * h, 2)))
 
-        def add_second(c0, chunks, name):
+        def add_second(c0, chunks, name, which=range(4)):
             n = chunks * CH
-            h, lo = divmod(c0 * CH, HALF)
-            total = held([P, 4 * n], F32, name)
-            for z in range(2):
-                for e, t in enumerate(HIGH):
-                    nc.vector.tensor_tensor(
-                        part(total, 2 * z + e, n), mixed[(z, t, 1)][:].indirect(offsets(1, c0, chunks)),
-                        first[(h, z, t)][:, lo : lo + n], ADD,
-                    )
+            if name:
+                total[c0] = held([P, 4 * n], F32, name)
+            for k in which:
+                z, t = k // 2, HIGH[k % 2]
+                nc.vector.tensor_tensor(
+                    part(total[c0], k, n), mixed[(z, t, 1)][:].indirect(offsets(1, c0, chunks)),
+                    first[(z, t)][:, c0 * CH : c0 * CH + n], ADD,
+                )
             for d in range(chunks):
-                high[c0 + d] = total[:].rearrange("p (z e j) -> p z j e", z=2, e=2)[:, :, d * CH : (d + 1) * CH]
+                high[c0 + d] = total[c0][:].rearrange("p (z e j) -> p z j e", z=2, e=2)[:, :, d * CH : (d + 1) * CH]
 
         def round_low(span, d, name):
             c0, chunks = SPANS[span]
@@ -320,32 +322,24 @@ def tile_picked_beamf_none_po_kernel(
                 in_=z_in[span][:, LANES * cols.start : LANES * cols.stop],
             )
 
-        def out_pass(res, span, t, z):
-            n = SPANS[span][1] * CH
+        def out_pass(c, t, z, start, stop):
             nc.tensor.matmul_mx(
-                out=res,
-                lhsT=part(w34_dealt[z], t, 2 * P).bitcast(FP4X4), lhsT_scale=part(dealt_scales, LANES * z + t, P),
-                rhs=part(z_codes[span], z, n).bitcast(FP8X4), rhs_scale=part(z_scales[span], z, n),
-                start=(z == 0), stop=(z == 1),
+                out=part(result[c], t, CH),
+                lhsT=part(w34_dealt[z], t, 2 * P).bitcast(FP4X4), lhsT_scale=part(dealt_scales[z], t, P),
+                rhs=part(z_codes[c], z, CH).bitcast(FP8X4), rhs_scale=part(z_scales[c], z, CH),
+                start=start, stop=stop,
             )
 
-        def multiply(span):
-            n = SPANS[span][1] * CH
-            banks = OUT_BANK[span]
-            per = LANES // len(banks)
-            result[span] = [bank(b) for b in banks]
+        def multiply(c):
+            result[c] = bank(OUT_BANK[c])
             for t in range(LANES):
                 for z in range(2):
-                    out_pass(part(result[span][t // per], t % per, n), span, t, z)
+                    out_pass(c, t, z, z == 0, z == 1)
 
-        def copy_out(span, moves):
-            c0, chunks = SPANS[span]
-            n = chunks * CH
-            out_f32[span] = held([P, LANES * n], F32, "of%d" % span)
-            width = LANES * n // len(result[span])
-            for b, res in enumerate(result[span]):
-                moves[b](part(out_f32[span], b, width), res[:, 0:width])
-            nc.sync.dma_start(out_rows[:, :, c0 * CH : c0 * CH + n], out_f32[span][:].rearrange("p (t j) -> p t j", t=LANES))
+        def copy_out(c, move):
+            out_f32[c] = held([P, LANES * CH], F32, "of%d" % c)
+            move(out_f32[c][:], result[c][:])
+            nc.sync.dma_start(out_rows[:, :, c * CH : (c + 1) * CH], out_f32[c][:].rearrange("p (t j) -> p t j", t=LANES))
 
         def interleave(move, dst, src):
             move(dst.rearrange("p (j t) -> p j t", t=LANES), src[:].rearrange("p (t j) -> p j t", t=LANES))
@@ -355,12 +349,10 @@ def tile_picked_beamf_none_po_kernel(
             nc.vector.quantize_mx(out=out_codes[:, done].bitcast(FP8X4), scales=out_scales[:, done], in_=src[:])
             nc.sync.dma_start(out_words[:, done], out_codes[:, done].bitcast(I32))
 
-        first_tile = held([P, 8 * HALF], F32, "first")
-        for h in range(2):
-            for z in range(2):
-                for e, t in enumerate(HIGH):
-                    engine = nc.vector if (h, z, t) == (1, 1, 2) else nc.scalar
-                    fetch_first(engine, h, z, t, part(first_tile, 4 * h + 2 * z + e, HALF))
+        for z in range(2):
+            for t in HIGH:
+                first[(z, t)] = rows("first%d%d" % (z, t))
+                fetch(nc.scalar, first[(z, t)], mixed[(z, t, 0)][:].indirect(lists[0][:]))
         add_second(0, 2, "high0")
         add_second(2, 1, "high2")
         round_low(0, 0, "pairs0")
@@ -376,27 +368,26 @@ def tile_picked_beamf_none_po_kernel(
         for c in range(2):
             quantise_z(c)
             multiply(c)
-        add_second(LAST, 1, "z0")
+        add_second(LAST, 1, "z0", (0,))
         round_high(2, 0, 2)
-        for z in range(2):
-            round_high(LAST, z)
+        add_second(LAST, 1, None, (1,))
         quantise_z(2)
         multiply(2)
-        result[LAST] = [bank(b) for b in OUT_BANK[LAST]]
+        add_second(LAST, 1, None, (2, 3))
+        for z in range(2):
+            round_high(LAST, z)
+        result[LAST] = bank(OUT_BANK[LAST])
         for z in range(2):
             quantise_z(LAST, (z,))
             for t in range(LANES):
-                out_pass(result[LAST][t][:, 0:CH], LAST, t, z)
+                out_pass(LAST, t, z, (z, t) == (0, 0), (z, t) == (1, LANES - 1))
         early_bf = held([P, LANES * HALF], BF16, "ob0")
         late_bf = held([P, LANES * HALF], BF16, "ob1")
-        for c in range(2):
-            copy_out(c, (nc.scalar.copy,))
-        interleave(nc.scalar.copy, part(early_bf, 0, LANES * CH), result[0][0])
-        interleave(nc.vector.tensor_copy, part(early_bf, 1, LANES * CH), out_f32[1])
-        copy_out(2, (nc.scalar.copy,))
+        for c in range(LAST):
+            copy_out(c, nc.scalar.copy)
+            interleave(nc.scalar.copy, part((early_bf, late_bf)[c // 2], c % 2, LANES * CH), result[c])
         hand_on(0, early_bf)
-        interleave(nc.vector.tensor_copy, part(late_bf, 0, LANES * CH), out_f32[2])
-        copy_out(LAST, (nc.scalar.copy, nc.vector.tensor_copy, nc.scalar.copy, nc.vector.tensor_copy))
+        copy_out(LAST, nc.vector.tensor_copy)
         interleave(nc.vector.tensor_copy, part(late_bf, 1, LANES * CH), out_f32[LAST])
         hand_on(1, late_bf)
 

@@ -33,7 +33,8 @@ TERMS_IN_BANK = 16
 PROJ_BANK = ((0, 1, 0, 6), (6, 7, 7, 1))
 SUM_BANK = (2, 3, 4, 5)
 BACK_BANK = (0, 1, 6, 7)
-OUT_BANK = (2, 3, 4, 5)
+OUT_BANK = (2, 3, 4)
+LAST_OUT_BANK = (5, 0)
 
 
 def tile_picked_beamf_none_po_kernel(
@@ -235,6 +236,9 @@ def tile_picked_beamf_none_po_kernel(
             scale_aside(term, part(picked[(t, mic)], IM), part(minus_wi, mic, LANES)[:, t : t + 1])
             add_term(term, t, 0)
         look_up(nc.scalar, IM, 1, 1)
+        term = rows("minus11")
+        nc.scalar.activation(term, part(picked[(1, 1)], IM), COPY, scale=part(minus_wi, 1, LANES)[:, 1:2])
+        add_term(term, 1, 0)
 
         def combine(z, t, mic):
             if mic == 0:
@@ -258,11 +262,10 @@ def tile_picked_beamf_none_po_kernel(
         for q in range(4):
             nc.sync.dma_start(w4_dealt_scales[q:P:32].bitcast(I32), both_dealt[4 + q : P : 32].bitcast(I32))
         dealt_scales = (both_dealt, w4_dealt_scales)
-        late_terms = rows("picked10", 3)
-        nc.vector.tensor_scalar(late_terms[:, 0 : 2 * S], picked[(1, 1)], wr[1][:, 1:2], None, MULT)
-        nc.vector.tensor_scalar(part(late_terms, 2), part(picked[(1, 1)], IM), part(minus_wi, 1, LANES)[:, 1:2], None, MULT)
-        for n in range(3):
-            add_term(part(late_terms, n), 1, n % 2)
+        late_terms = rows("picked10", 2)
+        nc.vector.tensor_scalar(late_terms, picked[(1, 1)], wr[1][:, 1:2], None, MULT)
+        for z in range(2):
+            add_term(part(late_terms, z), 1, z)
         first, pairs, back, z_in, high, total = {}, {}, {}, {}, {}, {}
         SPANS = ((0, 1), (1, 1), (2, 1), (3, 1))
 
@@ -322,9 +325,9 @@ def tile_picked_beamf_none_po_kernel(
                 in_=z_in[span][:, LANES * cols.start : LANES * cols.stop],
             )
 
-        def out_pass(c, t, z, start, stop):
+        def out_pass(res, c, t, z, start, stop):
             nc.tensor.matmul_mx(
-                out=part(result[c], t, CH),
+                out=res,
                 lhsT=part(w34_dealt[z], t, 2 * P).bitcast(FP4X4), lhsT_scale=part(dealt_scales[z], t, P),
                 rhs=part(z_codes[c], z, CH).bitcast(FP8X4), rhs_scale=part(z_scales[c], z, CH),
                 start=start, stop=stop,
@@ -334,19 +337,25 @@ def tile_picked_beamf_none_po_kernel(
             result[c] = bank(OUT_BANK[c])
             for t in range(LANES):
                 for z in range(2):
-                    out_pass(c, t, z, z == 0, z == 1)
+                    out_pass(part(result[c], t, CH), c, t, z, z == 0, z == 1)
 
         def copy_out(c, move):
             out_f32[c] = held([P, LANES * CH], F32, "of%d" % c)
             move(out_f32[c][:], result[c][:])
+            store_out(c)
+
+        def store_out(c):
             nc.sync.dma_start(out_rows[:, :, c * CH : (c + 1) * CH], out_f32[c][:].rearrange("p (t j) -> p t j", t=LANES))
 
         def interleave(move, dst, src):
             move(dst.rearrange("p (j t) -> p j t", t=LANES), src[:].rearrange("p (t j) -> p j t", t=LANES))
 
-        def hand_on(h, src):
+        def hand_on(h, src, calls=1):
+            n = HALF // calls
+            for d in range(calls):
+                cols = slice(h * HALF + d * n, h * HALF + (d + 1) * n)
+                nc.vector.quantize_mx(out=out_codes[:, cols].bitcast(FP8X4), scales=out_scales[:, cols], in_=part(src, d, LANES * n))
             done = slice(h * HALF, (h + 1) * HALF)
-            nc.vector.quantize_mx(out=out_codes[:, done].bitcast(FP8X4), scales=out_scales[:, done], in_=src[:])
             nc.sync.dma_start(out_words[:, done], out_codes[:, done].bitcast(I32))
 
         for z in range(2):
@@ -376,20 +385,25 @@ def tile_picked_beamf_none_po_kernel(
         add_second(LAST, 1, None, (2, 3))
         for z in range(2):
             round_high(LAST, z)
-        result[LAST] = bank(OUT_BANK[LAST])
+        last = [bank(b) for b in LAST_OUT_BANK]
         for z in range(2):
             quantise_z(LAST, (z,))
             for t in range(LANES):
-                out_pass(LAST, t, z, (z, t) == (0, 0), (z, t) == (1, LANES - 1))
+                out_pass(part(last[t // 2], t % 2, CH), LAST, t, z, (z, t % 2) == (0, 0), (z, t % 2) == (1, 1))
         early_bf = held([P, LANES * HALF], BF16, "ob0")
         late_bf = held([P, LANES * HALF], BF16, "ob1")
-        for c in range(LAST):
+        for c in range(2):
             copy_out(c, nc.scalar.copy)
-            interleave(nc.scalar.copy, part((early_bf, late_bf)[c // 2], c % 2, LANES * CH), result[c])
+            interleave(nc.scalar.copy, part(early_bf, c, LANES * CH), result[c])
+        copy_out(2, nc.scalar.copy)
         hand_on(0, early_bf)
-        copy_out(LAST, nc.vector.tensor_copy)
+        out_f32[LAST] = held([P, LANES * CH], F32, "of3")
+        for u, move in enumerate((nc.vector.tensor_copy, nc.scalar.copy)):
+            move(part(out_f32[LAST], u, 2 * CH), last[u][:, 0 : 2 * CH])
+        store_out(LAST)
+        interleave(nc.vector.tensor_copy, part(late_bf, 0, LANES * CH), out_f32[2])
         interleave(nc.vector.tensor_copy, part(late_bf, 1, LANES * CH), out_f32[LAST])
-        hand_on(1, late_bf)
+        hand_on(1, late_bf, 2)
 
         for q in range(4):
             queue = nc.sync if q % 2 == 0 else nc.scalar

@@ -95,8 +95,8 @@ def tile_picked_beamf_none_po_kernel(
         nc.sync.dma_start(w34_words[0][:].bitcast(I32), w3_words[0].bitcast(I32))
         nc.sync.dma_start(w34_words[1][:].bitcast(I32), w4_words[0].bitcast(I32))
         nc.sync.dma_start(m1_t[:], m1)
-        nc.sync.dma_start(raw[IM][:], w_rows[IM])
         nc.sync.dma_start(m2_t[:], m2)
+        nc.sync.dma_start(raw[IM][:], w_rows[IM])
         load_weight(wi[0], wi1)
         load_weight(wi[1], wi2)
         load_weight(wr[0], wr1)
@@ -146,13 +146,12 @@ def tile_picked_beamf_none_po_kernel(
             )
 
         for u in range(2):
-            grouped[(RE, u)] = held([P, 2 * H], BF16, "grouped%d" % u)
+            grouped[(RE, u)] = held([P, 2 * H], BF16, ("grouped0", "w4d")[u])
         regroup(RE, 0, nc.vector.tensor_copy, slice(0, P // 2))
         regroup(RE, 0, nc.scalar.copy, slice(P // 2, P))
         regroup(RE, 1, nc.scalar.copy)
         quantise_w(RE, 0, "wc00")
-        for z in range(2):
-            deal_words(z)
+        deal_words(0)
         for h in range(2):
             frames = slice(h * HALF, (h + 1) * HALF)
             nc.vector.tensor_copy(xg_words[:, frames], xw[:].bitcast(U32).indirect(part(offs_t, h, HALF // 16)))
@@ -162,11 +161,17 @@ def tile_picked_beamf_none_po_kernel(
                 project(RE, t, frames, None if h == 0 else SUM_BANK[t])
                 fill(RE, t, frames, nc.vector.tensor_copy if (h, t) == (1, 0) else nc.scalar.copy)
         project(RE, 2)
+        w34_dealt[1] = held([P, 2 * N], U8, "w4d")
+        nc.gpsimd.tensor_copy(
+            w34_dealt[1][:].rearrange("p (t c e) -> p t c e", t=LANES, e=2),
+            w34_words[1][:].rearrange("p (c t e) -> p t c e", t=LANES, e=2),
+        )
 
         picked, cross, mixed, sums, added = {}, {}, {}, {}, {}
         for t in LOW:
             for mic in range(2):
-                picked[(t, mic)] = rows("picked%d%d" % (t, mic), 2)
+                if (t, mic) != (1, 1):
+                    picked[(t, mic)] = rows("picked%d%d" % (t, mic), 2)
 
         def fetch(engine, dst, src):
             if engine is nc.scalar:
@@ -200,6 +205,7 @@ def tile_picked_beamf_none_po_kernel(
         project(IM, 3)
         project(RE, 3)
         project(IM, 2)
+        picked[(1, 1)] = rows("raw1", 2)
         look_up(nc.vector, RE, 1, 1)
         for t, mic in ((0, 0), (0, 1), (1, 0)):
             look_up(nc.vector, IM, t, mic)

@@ -30,7 +30,7 @@ HALF = S // 2
 BANK = 512
 TERMS_IN_BANK = 16
 
-PROJ_BANK = ((0, 1, 0, 6), (6, 7, 7, 1))
+PROJ_BANK = ((0, 1, 0, 1), (6, 7, 7, 6))
 SUM_BANK = (2, 3, 4, 5)
 BACK_BANK = (0, 1, 6, 7)
 OUT_BANK = (2, 3, 4)
@@ -158,9 +158,10 @@ def tile_picked_beamf_none_po_kernel(
             if h == 1:
                 quantise_w(RE, 1, "xw")
             for t in LOW:
-                project(RE, t, frames, None if h == 0 else SUM_BANK[t])
+                project(RE, t, frames, SUM_BANK[t] if h == 0 else None)
                 fill(RE, t, frames, nc.vector.tensor_copy if (h, t) == (1, 0) else nc.scalar.copy)
-        project(RE, 2)
+        for t in HIGH:
+            project(RE, t)
         w34_dealt[1] = held([P, 2 * N], U8, "w4d")
         nc.gpsimd.tensor_copy(
             w34_dealt[1][:].rearrange("p (t c e) -> p t c e", t=LANES, e=2),
@@ -182,8 +183,8 @@ def tile_picked_beamf_none_po_kernel(
         def look_up(engine, i, t, mic):
             fetch(engine, part(picked[(t, mic)], i), window[(i, t)][:].indirect(lists[mic][:]))
 
-        def cross_term(i, t, mic):
-            cross[(i, t, mic)] = rows("cross%d%d%d" % (i, t, mic))
+        def cross_term(i, t, mic, dst=None):
+            cross[(i, t, mic)] = rows("cross%d%d%d" % (i, t, mic)) if dst is None else dst
             nc.scalar.activation(cross[(i, t, mic)], proj[(i, t)][:], COPY, scale=wi[mic][:, t : t + 1])
 
         minus_wi = held([P, 2 * LANES], F32, "minus_wi")
@@ -203,15 +204,15 @@ def tile_picked_beamf_none_po_kernel(
             project(IM, t)
             fill(IM, t)
         project(IM, 3)
-        project(RE, 3)
         project(IM, 2)
         picked[(1, 1)] = rows("raw1", 2)
         look_up(nc.vector, RE, 1, 1)
         for t, mic in ((0, 0), (0, 1), (1, 0)):
             look_up(nc.vector, IM, t, mic)
+        behind_im = rows("wc10", 2)
         for mic in range(2):
+            cross_term(RE, 3, mic, part(behind_im, mic))
             cross_term(IM, 3, mic)
-            cross_term(RE, 3, mic)
             cross_term(IM, 2, mic)
 
         def add_term(term, t, z):
@@ -242,9 +243,6 @@ def tile_picked_beamf_none_po_kernel(
             scale_aside(term, part(picked[(t, mic)], IM), part(minus_wi, mic, LANES)[:, t : t + 1])
             add_term(term, t, 0)
         look_up(nc.scalar, IM, 1, 1)
-        term = rows("minus11")
-        nc.scalar.activation(term, part(picked[(1, 1)], IM), COPY, scale=part(minus_wi, 1, LANES)[:, 1:2])
-        add_term(term, 1, 0)
 
         def combine(z, t, mic):
             if mic == 0:
@@ -268,10 +266,11 @@ def tile_picked_beamf_none_po_kernel(
         for q in range(4):
             nc.sync.dma_start(w4_dealt_scales[q:P:32].bitcast(I32), both_dealt[4 + q : P : 32].bitcast(I32))
         dealt_scales = (both_dealt, w4_dealt_scales)
-        late_terms = rows("picked10", 2)
-        nc.vector.tensor_scalar(late_terms, picked[(1, 1)], wr[1][:, 1:2], None, MULT)
-        for z in range(2):
-            add_term(part(late_terms, z), 1, z)
+        late_terms = rows("picked10", 3)
+        nc.vector.tensor_scalar(late_terms[:, 0 : 2 * S], picked[(1, 1)], wr[1][:, 1:2], None, MULT)
+        nc.vector.tensor_scalar(part(late_terms, 2), part(picked[(1, 1)], IM), part(minus_wi, 1, LANES)[:, 1:2], None, MULT)
+        for n in range(3):
+            add_term(part(late_terms, n), 1, n % 2)
         first, pairs, back, z_in, high, total = {}, {}, {}, {}, {}, {}
         SPANS = ((0, 1), (1, 1), (2, 1), (3, 1))
 
@@ -373,8 +372,8 @@ def tile_picked_beamf_none_po_kernel(
         round_low(0, 0, "pairs0")
         round_low(1, 0, "pairs1")
         place_low(0)
-        place_low(1)
         round_low(2, 0, "pairs0")
+        place_low(1)
         round_low(3, 0, "pairs1")
         place_low(2)
         place_low(3)

@@ -33,8 +33,7 @@ TERMS_IN_BANK = 16
 PROJ_BANK = ((0, 1, 0, 1), (6, 7, 7, 6))
 SUM_BANK = (2, 3, 4, 5)
 BACK_BANK = (0, 1, 6, 7)
-OUT_BANK = (2, 3, 4)
-LAST_OUT_BANK = (5, 0)
+OUT_BANK = (2, 3, 4, 5)
 
 
 def tile_picked_beamf_none_po_kernel(
@@ -47,7 +46,7 @@ def tile_picked_beamf_none_po_kernel(
         psum = ctx.enter_context(tc.psum_pool(name="psum", bufs=1))
 
         def held(shape, dtype, name):
-            return keep.tile(shape, dtype, name=name, align_bytes=64)
+            return keep.tile(shape, dtype, name=name, align_bytes=256)
 
         def rows(name, count=1):
             return held([P, count * S], F32, name)[:]
@@ -330,9 +329,9 @@ def tile_picked_beamf_none_po_kernel(
                 in_=z_in[span][:, LANES * cols.start : LANES * cols.stop],
             )
 
-        def out_pass(res, c, t, z, start, stop):
+        def out_pass(c, t, z, start, stop):
             nc.tensor.matmul_mx(
-                out=res,
+                out=part(result[c], t, CH),
                 lhsT=part(w34_dealt[z], t, 2 * P).bitcast(FP4X4), lhsT_scale=part(dealt_scales[z], t, P),
                 rhs=part(z_codes[c], z, CH).bitcast(FP8X4), rhs_scale=part(z_scales[c], z, CH),
                 start=start, stop=stop,
@@ -342,25 +341,19 @@ def tile_picked_beamf_none_po_kernel(
             result[c] = bank(OUT_BANK[c])
             for t in range(LANES):
                 for z in range(2):
-                    out_pass(part(result[c], t, CH), c, t, z, z == 0, z == 1)
+                    out_pass(c, t, z, z == 0, z == 1)
 
         def copy_out(c, move):
             out_f32[c] = held([P, LANES * CH], F32, "of%d" % c)
             move(out_f32[c][:], result[c][:])
-            store_out(c)
-
-        def store_out(c):
             nc.sync.dma_start(out_rows[:, :, c * CH : (c + 1) * CH], out_f32[c][:].rearrange("p (t j) -> p t j", t=LANES))
 
         def interleave(move, dst, src):
             move(dst.rearrange("p (j t) -> p j t", t=LANES), src[:].rearrange("p (t j) -> p j t", t=LANES))
 
-        def hand_on(h, src, calls=1):
-            n = HALF // calls
-            for d in range(calls):
-                cols = slice(h * HALF + d * n, h * HALF + (d + 1) * n)
-                nc.vector.quantize_mx(out=out_codes[:, cols].bitcast(FP8X4), scales=out_scales[:, cols], in_=part(src, d, LANES * n))
+        def hand_on(h, src):
             done = slice(h * HALF, (h + 1) * HALF)
+            nc.vector.quantize_mx(out=out_codes[:, done].bitcast(FP8X4), scales=out_scales[:, done], in_=src[:])
             nc.sync.dma_start(out_words[:, done], out_codes[:, done].bitcast(I32))
 
         for z in range(2):
@@ -372,8 +365,8 @@ def tile_picked_beamf_none_po_kernel(
         round_low(0, 0, "pairs0")
         round_low(1, 0, "pairs1")
         place_low(0)
-        round_low(2, 0, "pairs0")
         place_low(1)
+        round_low(2, 0, "pairs0")
         round_low(3, 0, "pairs1")
         place_low(2)
         place_low(3)
@@ -390,25 +383,20 @@ def tile_picked_beamf_none_po_kernel(
         add_second(LAST, 1, None, (2, 3))
         for z in range(2):
             round_high(LAST, z)
-        last = [bank(b) for b in LAST_OUT_BANK]
+        result[LAST] = bank(OUT_BANK[LAST])
         for z in range(2):
             quantise_z(LAST, (z,))
             for t in range(LANES):
-                out_pass(part(last[t // 2], t % 2, CH), LAST, t, z, (z, t % 2) == (0, 0), (z, t % 2) == (1, 1))
+                out_pass(LAST, t, z, (z, t) == (0, 0), (z, t) == (1, LANES - 1))
         early_bf = held([P, LANES * HALF], BF16, "ob0")
         late_bf = held([P, LANES * HALF], BF16, "ob1")
-        for c in range(2):
+        for c in range(LAST):
             copy_out(c, nc.scalar.copy)
-            interleave(nc.scalar.copy, part(early_bf, c, LANES * CH), result[c])
-        copy_out(2, nc.scalar.copy)
+            interleave(nc.scalar.copy, part((early_bf, late_bf)[c // 2], c % 2, LANES * CH), result[c])
         hand_on(0, early_bf)
-        out_f32[LAST] = held([P, LANES * CH], F32, "of3")
-        for u, move in enumerate((nc.vector.tensor_copy, nc.scalar.copy)):
-            move(part(out_f32[LAST], u, 2 * CH), last[u][:, 0 : 2 * CH])
-        store_out(LAST)
-        interleave(nc.vector.tensor_copy, part(late_bf, 0, LANES * CH), out_f32[2])
+        copy_out(LAST, nc.vector.tensor_copy)
         interleave(nc.vector.tensor_copy, part(late_bf, 1, LANES * CH), out_f32[LAST])
-        hand_on(1, late_bf, 2)
+        hand_on(1, late_bf)
 
         for q in range(4):
             queue = nc.sync if q % 2 == 0 else nc.scalar

@@ -30,7 +30,7 @@ HALF = S // 2
 BANK = 512
 TERMS_IN_BANK = 16
 
-PROJ_BANK = ((0, 1, 0, 1), (6, 7, 7, 6))
+PROJ_BANK = ((0, 1, 0, 1), (3, 2, 7, 6))
 SUM_BANK = (2, 3, 4, 5)
 BACK_BANK = (0, 1, 6, 7)
 OUT_BANK = (2, 3, 4, 5)
@@ -168,10 +168,17 @@ def tile_picked_beamf_none_po_kernel(
         )
 
         picked, cross, mixed, sums, added = {}, {}, {}, {}, {}
-        for t in LOW:
-            for mic in range(2):
-                if (t, mic) != (1, 1):
-                    picked[(t, mic)] = rows("picked%d%d" % (t, mic), 2)
+        both = {}
+
+        def hold_pair(t, mic, name):
+            both[(t, mic)] = rows(name, 2)
+            for i in (RE, IM):
+                picked[(i, t, mic)] = part(both[(t, mic)], i)
+
+        hold_pair(0, 0, "picked00")
+        for t, mic in ((0, 1), (1, 0)):
+            for i in (RE, IM):
+                picked[(i, t, mic)] = rows("picked%d%d%d" % (i, t, mic))
 
         def fetch(engine, dst, src):
             if engine is nc.scalar:
@@ -180,11 +187,39 @@ def tile_picked_beamf_none_po_kernel(
                 nc.vector.tensor_copy(dst, src)
 
         def look_up(engine, i, t, mic):
-            fetch(engine, part(picked[(t, mic)], i), window[(i, t)][:].indirect(lists[mic][:]))
+            fetch(engine, picked[(i, t, mic)], window[(i, t)][:].indirect(lists[mic][:]))
 
         def cross_term(i, t, mic, dst=None):
             cross[(i, t, mic)] = rows("cross%d%d%d" % (i, t, mic)) if dst is None else dst
             nc.scalar.activation(cross[(i, t, mic)], proj[(i, t)][:], COPY, scale=wi[mic][:, t : t + 1])
+
+        def add_term(term, t, z):
+            for c in range(LAST + 1):
+                if c not in sums:
+                    sums[c] = bank(SUM_BANK[c])
+                    added[c] = 0
+                nc.tensor.matmul(
+                    part(sums[c], 2 * z + t, P), lhsT=part(term, c, CH), rhs=ident[:], is_transpose=True,
+                    start=(added[c] == 0), stop=(added[c] == TERMS_IN_BANK - 1),
+                )
+                added[c] += 1
+
+        def weigh(engine, i, t, mic, zs, dst):
+            src = both[(t, mic)] if i is None else picked[(i, t, mic)]
+            if i is None or zs[0] == i:
+                w = wr[mic][:, t : t + 1]
+            elif i == RE:
+                w = wi[mic][:, t : t + 1]
+            else:
+                w = part(minus_wi, mic, LANES)[:, t : t + 1]
+            if engine is nc.gpsimd:
+                nc.gpsimd.tensor_scalar(dst, src, w, 0.0, MULT, ADD)
+            elif engine is nc.vector:
+                nc.vector.tensor_scalar(dst, src, w, None, MULT)
+            else:
+                nc.scalar.activation(dst, src, COPY, scale=w)
+            for n, z in enumerate(zs):
+                add_term(part(dst, n), t, z)
 
         minus_wi = held([P, 2 * LANES], F32, "minus_wi")
         for mic in range(2):
@@ -204,7 +239,10 @@ def tile_picked_beamf_none_po_kernel(
             fill(IM, t)
         project(IM, 3)
         project(IM, 2)
-        picked[(1, 1)] = rows("raw1", 2)
+        weigh(nc.vector, RE, 0, 0, (1,), rows("early0"))
+        for z in (1, 0):
+            weigh(nc.vector, RE, 1, 0, (z,), rows("early1%d" % z))
+        hold_pair(1, 1, "raw1")
         look_up(nc.vector, RE, 1, 1)
         for t, mic in ((0, 0), (0, 1), (1, 0)):
             look_up(nc.vector, IM, t, mic)
@@ -214,34 +252,18 @@ def tile_picked_beamf_none_po_kernel(
             cross_term(IM, 3, mic)
             cross_term(IM, 2, mic)
 
-        def add_term(term, t, z):
-            for c in range(LAST + 1):
-                if c not in sums:
-                    sums[c] = bank(SUM_BANK[c])
-                    added[c] = 0
-                nc.tensor.matmul(
-                    part(sums[c], 2 * z + t, P), lhsT=part(term, c, CH), rhs=ident[:], is_transpose=True,
-                    start=(added[c] == 0), stop=(added[c] == TERMS_IN_BANK - 1),
-                )
-                added[c] += 1
-
-        def scale_aside(dst, src, w):
-            nc.gpsimd.tensor_scalar(dst, src, w, 0.0, MULT, ADD)
-
-        pairs_of = [(t, mic) for mic in range(2) for t in LOW]
-        early_terms = rows("grouped1", 4)
-        for n, (t, mic) in enumerate(pairs_of):
-            scale_aside(part(early_terms, n), part(picked[(t, mic)], RE), wi[mic][:, t : t + 1])
-            add_term(part(early_terms, n), t, 1)
-        for t, mic in ((0, 0), (0, 1), (1, 0)):
-            direct = rows("direct%d%d" % (t, mic), 2)
-            scale_aside(direct, picked[(t, mic)], wr[mic][:, t : t + 1])
+        aside = rows("picked010", 3)
+        weigh(nc.gpsimd, RE, 0, 1, (1,), part(aside, 0))
+        weigh(nc.gpsimd, RE, 0, 1, (0,), part(aside, 1))
+        weigh(nc.gpsimd, RE, 1, 1, (1,), part(aside, 2))
+        weigh(nc.gpsimd, None, 0, 0, (0, 1), rows("direct00", 2))
+        weigh(nc.gpsimd, IM, 0, 0, (0,), rows("minus00"))
+        for t, mic in ((0, 1), (1, 0)):
             for z in range(2):
-                add_term(part(direct, z), t, z)
-            term = rows("minus%d%d" % (t, mic))
-            scale_aside(term, part(picked[(t, mic)], IM), part(minus_wi, mic, LANES)[:, t : t + 1])
-            add_term(term, t, 0)
+                weigh(nc.gpsimd, IM, t, mic, (z,), rows("term%d%d%d" % (t, mic, z)))
         look_up(nc.scalar, IM, 1, 1)
+        weigh(nc.scalar, IM, 1, 1, (0,), rows("minus11"))
+        weigh(nc.gpsimd, None, 1, 1, (0, 1), rows("direct11", 2))
 
         def combine(z, t, mic):
             if mic == 0:
@@ -265,11 +287,6 @@ def tile_picked_beamf_none_po_kernel(
         for q in range(4):
             nc.sync.dma_start(w4_dealt_scales[q:P:32].bitcast(I32), both_dealt[4 + q : P : 32].bitcast(I32))
         dealt_scales = (both_dealt, w4_dealt_scales)
-        late_terms = rows("picked10", 3)
-        nc.vector.tensor_scalar(late_terms[:, 0 : 2 * S], picked[(1, 1)], wr[1][:, 1:2], None, MULT)
-        nc.vector.tensor_scalar(part(late_terms, 2), part(picked[(1, 1)], IM), part(minus_wi, 1, LANES)[:, 1:2], None, MULT)
-        for n in range(3):
-            add_term(part(late_terms, n), 1, n % 2)
         first, pairs, back, z_in, high, total = {}, {}, {}, {}, {}, {}
         SPANS = ((0, 1), (1, 1), (2, 1), (3, 1))
 
@@ -388,11 +405,14 @@ def tile_picked_beamf_none_po_kernel(
             quantise_z(LAST, (z,))
             for t in range(LANES):
                 out_pass(LAST, t, z, (z, t) == (0, 0), (z, t) == (1, LANES - 1))
-        early_bf = held([P, LANES * HALF], BF16, "ob0")
+        early_bf = held([P, LANES * HALF], BF16, "zc1")
         late_bf = held([P, LANES * HALF], BF16, "ob1")
-        for c in range(LAST):
+        for c in range(2):
             copy_out(c, nc.scalar.copy)
-            interleave(nc.scalar.copy, part((early_bf, late_bf)[c // 2], c % 2, LANES * CH), result[c])
+        for c in range(2):
+            interleave(nc.scalar.copy, part(early_bf, c, LANES * CH), result[c])
+        copy_out(2, nc.scalar.copy)
+        interleave(nc.scalar.copy, part(late_bf, 0, LANES * CH), result[2])
         hand_on(0, early_bf)
         copy_out(LAST, nc.vector.tensor_copy)
         interleave(nc.vector.tensor_copy, part(late_bf, 1, LANES * CH), out_f32[LAST])

@@ -29,11 +29,11 @@ LAST = 3
 HALF = S // 2
 BANK = 512
 TERMS_IN_BANK = 16
+W4_ROWS = 4
 
 PROJ_BANK = ((0, 1, 0, 1), (3, 2, 7, 6))
 SUM_BANK = (2, 3, 4, 5)
 BACK_BANK = (0, 1, 6, 7)
-OUT_BANK = (2, 3, 4, 5)
 
 
 def tile_picked_beamf_none_po_kernel(
@@ -102,7 +102,7 @@ def tile_picked_beamf_none_po_kernel(
         load_weight(wr[1], wr2)
         make_identity(nc, ident[:])
         load_scale_rows(w34_scales[:, :], w3_scales)
-        load_scale_rows(w34_scales[:, :], w4_scales, 4)
+        load_scale_rows(w34_scales[:, :], w4_scales, W4_ROWS)
         lists = (m1_t, m2_t)
 
         def offsets(mic, c, chunks):
@@ -137,20 +137,17 @@ def tile_picked_beamf_none_po_kernel(
         def fill(i, t, frames=slice(0, S), move=nc.scalar.copy):
             move(window[(i, t)][:, frames], proj[(i, t)][:, frames])
 
-        def deal_words(z):
-            w34_dealt[z] = held([P, 2 * N], U8, "w34d%d" % z)
-            nc.scalar.copy(
-                w34_dealt[z][:].bitcast(U16).rearrange("p (t c) -> p t c", t=LANES),
-                w34_words[z][:].bitcast(U16).rearrange("p (c t) -> p t c", t=LANES),
-            )
-
         for u in range(2):
             grouped[(RE, u)] = held([P, 2 * H], BF16, ("grouped0", "w4d")[u])
         regroup(RE, 0, nc.vector.tensor_copy, slice(0, P // 2))
         regroup(RE, 0, nc.scalar.copy, slice(P // 2, P))
         regroup(RE, 1, nc.scalar.copy)
         quantise_w(RE, 0, "wc00")
-        deal_words(0)
+        w34_dealt[0] = held([P, 2 * N], U8, "w3d")
+        nc.scalar.copy(
+            w34_dealt[0][:].bitcast(U16).rearrange("p (t c) -> p t c", t=LANES),
+            w34_words[0][:].bitcast(U16).rearrange("p (c t) -> p t c", t=LANES),
+        )
         for h in range(2):
             frames = slice(h * HALF, (h + 1) * HALF)
             nc.vector.tensor_copy(xg_words[:, frames], xw[:].bitcast(U32).indirect(part(offs_t, h, HALF // 16)))
@@ -167,8 +164,7 @@ def tile_picked_beamf_none_po_kernel(
             w34_words[1][:].rearrange("p (c t e) -> p t c e", t=LANES, e=2),
         )
 
-        picked, cross, mixed, sums, added = {}, {}, {}, {}, {}
-        both = {}
+        picked, both, cross, mixed, sums, added = {}, {}, {}, {}, {}, {}
 
         def hold_pair(t, mic, name):
             both[(t, mic)] = rows(name, 2)
@@ -193,16 +189,17 @@ def tile_picked_beamf_none_po_kernel(
             cross[(i, t, mic)] = rows("cross%d%d%d" % (i, t, mic)) if dst is None else dst
             nc.scalar.activation(cross[(i, t, mic)], proj[(i, t)][:], COPY, scale=wi[mic][:, t : t + 1])
 
-        def add_term(term, t, z):
+        def add_terms(terms, t, zs):
             for c in range(LAST + 1):
                 if c not in sums:
                     sums[c] = bank(SUM_BANK[c])
                     added[c] = 0
-                nc.tensor.matmul(
-                    part(sums[c], 2 * z + t, P), lhsT=part(term, c, CH), rhs=ident[:], is_transpose=True,
-                    start=(added[c] == 0), stop=(added[c] == TERMS_IN_BANK - 1),
-                )
-                added[c] += 1
+                for n, z in enumerate(zs):
+                    nc.tensor.matmul(
+                        part(sums[c], 2 * z + t, P), lhsT=part(part(terms, n), c, CH), rhs=ident[:], is_transpose=True,
+                        start=(added[c] == 0), stop=(added[c] == TERMS_IN_BANK - 1),
+                    )
+                    added[c] += 1
 
         def weigh(engine, i, t, mic, zs, dst):
             src = both[(t, mic)] if i is None else picked[(i, t, mic)]
@@ -218,8 +215,7 @@ def tile_picked_beamf_none_po_kernel(
                 nc.vector.tensor_scalar(dst, src, w, None, MULT)
             else:
                 nc.scalar.activation(dst, src, COPY, scale=w)
-            for n, z in enumerate(zs):
-                add_term(part(dst, n), t, z)
+            add_terms(dst, t, zs)
 
         minus_wi = held([P, 2 * LANES], F32, "minus_wi")
         for mic in range(2):
@@ -267,7 +263,7 @@ def tile_picked_beamf_none_po_kernel(
 
         def combine(z, t, mic):
             if mic == 0:
-                mixed[(z, t, mic)] = window[(z, t - 2)]
+                mixed[(z, t, mic)] = window[(z, t - len(LOW))]
             else:
                 mixed[(z, t, mic)] = held([P, S], F32, "mixed%d%d" % (z, t))
             nc.vector.scalar_tensor_tensor(
@@ -285,49 +281,45 @@ def tile_picked_beamf_none_po_kernel(
             both_dealt[:].rearrange("p (t c) -> p t c", t=LANES), w34_scales[:].rearrange("p (c t) -> p t c", t=LANES)
         )
         for q in range(4):
-            nc.sync.dma_start(w4_dealt_scales[q:P:32].bitcast(I32), both_dealt[4 + q : P : 32].bitcast(I32))
+            nc.sync.dma_start(w4_dealt_scales[q:P:32].bitcast(I32), both_dealt[W4_ROWS + q : P : 32].bitcast(I32))
         dealt_scales = (both_dealt, w4_dealt_scales)
-        first, pairs, back, z_in, high, total = {}, {}, {}, {}, {}, {}
-        SPANS = ((0, 1), (1, 1), (2, 1), (3, 1))
 
+        first, total, high, back, z_in = {}, {}, {}, {}, {}
 
-        def add_second(c0, chunks, name, which=range(4)):
+        def hold_total(c0, chunks, name):
+            total[c0] = held([P, 4 * chunks * CH], F32, name)
+            for d in range(chunks):
+                high[c0 + d] = total[c0][:].rearrange("p (z e j) -> p z j e", z=2, e=2)[:, :, d * CH : (d + 1) * CH]
+
+        def add_second(c0, chunks, which=range(4)):
             n = chunks * CH
-            if name:
-                total[c0] = held([P, 4 * n], F32, name)
             for k in which:
                 z, t = k // 2, HIGH[k % 2]
                 nc.vector.tensor_tensor(
                     part(total[c0], k, n), mixed[(z, t, 1)][:].indirect(offsets(1, c0, chunks)),
                     first[(z, t)][:, c0 * CH : c0 * CH + n], ADD,
                 )
-            for d in range(chunks):
-                high[c0 + d] = total[c0][:].rearrange("p (z e j) -> p z j e", z=2, e=2)[:, :, d * CH : (d + 1) * CH]
 
-        def round_low(span, d, name):
-            c0, chunks = SPANS[span]
-            c = c0 + d
-            pairs[c] = held([P, H], BF16, name)
+        def round_low(c):
+            pairs = held([P, H], BF16, "window1%d" % (c % 2))
             nc.scalar.copy(
-                pairs[c][:].rearrange("j (z p e) -> j z p e", z=2, e=2),
+                pairs[:].rearrange("j (z p e) -> j z p e", z=2, e=2),
                 sums[c][:].rearrange("j (z e p) -> j z p e", z=2, e=2),
             )
-            if d == 0:
-                back[span] = bank(BACK_BANK[span])
+            back[c] = bank(BACK_BANK[c])
             for z in range(2):
-                nc.tensor.transpose(part(back[span], z * chunks + d, P), part(pairs[c][:].bitcast(F32), z, P), ident[:])
+                nc.tensor.transpose(part(back[c], z, P), part(pairs[:].bitcast(F32), z, P), ident[:])
 
-        def place_low(span):
-            n = 2 * SPANS[span][1] * CH
-            z_in[span] = held([P, LANES * n], BF16, "z%d" % span)
+        def place_low(c):
+            z_in[c] = held([P, 2 * H], BF16, "z%d" % c)
             nc.scalar.copy(
-                z_in[span][:].bitcast(F32).rearrange("p (n u) -> p n u", u=2),
-                back[span][:, 0:n].unsqueeze(2).to_broadcast([P, n, 2]),
+                z_in[c][:].bitcast(F32).rearrange("p (n u) -> p n u", u=2),
+                back[c][:, 0 : 2 * P].unsqueeze(2).to_broadcast([P, 2 * P, 2]),
             )
 
-        def round_high(span, z, count=1):
-            dst = z_in[span][:].rearrange("p (z j t) -> p z j t", z=2, t=LANES)[:, z : z + count, :, 2:4]
-            nc.vector.tensor_copy(dst, high[span][:, z : z + count])
+        def round_high(c, zs=slice(0, 2)):
+            dst = z_in[c][:].rearrange("p (z j t) -> p z j t", z=2, t=LANES)[:, zs, :, 2:4]
+            nc.vector.tensor_copy(dst, high[c][:, zs])
 
         out_codes = held([P, S], U32, "oc")
         out_scales = held([P, S], U8, "osc")
@@ -335,15 +327,13 @@ def tile_picked_beamf_none_po_kernel(
         out_words = out_1[0].rearrange("p c r -> p (c r)").bitcast(I32)
         z_codes, z_scales, result, out_f32, out_bf = {}, {}, {}, {}, {}
 
-        def quantise_z(span, zs=(0, 1)):
-            n = SPANS[span][1] * CH
-            if zs[0] == 0:
-                z_codes[span] = held([P, 2 * n], U32, "zc%d" % span)
-                z_scales[span] = held([P, 2 * n], U8, "zs%d" % span)
-            cols = slice(zs[0] * n, (zs[-1] + 1) * n)
+        def quantise_z(c, zs=slice(0, 2)):
+            if zs.start == 0:
+                z_codes[c] = held([P, 2 * CH], U32, "zc%d" % c)
+                z_scales[c] = held([P, 2 * CH], U8, "zs%d" % c)
+            cols = slice(zs.start * CH, zs.stop * CH)
             nc.vector.quantize_mx(
-                out=z_codes[span][:, cols].bitcast(FP8X4), scales=z_scales[span][:, cols],
-                in_=z_in[span][:, LANES * cols.start : LANES * cols.stop],
+                out=z_codes[c][:, cols].bitcast(FP8X4), scales=z_scales[c][:, cols], in_=z_in[c][:, zs.start * H : zs.stop * H]
             )
 
         def out_pass(c, t, z, start, stop):
@@ -355,68 +345,80 @@ def tile_picked_beamf_none_po_kernel(
             )
 
         def multiply(c):
-            result[c] = bank(OUT_BANK[c])
+            result[c] = bank(SUM_BANK[c])
             for t in range(LANES):
                 for z in range(2):
                     out_pass(c, t, z, z == 0, z == 1)
 
-        def copy_out(c, move):
+        def copy_out(c):
             out_f32[c] = held([P, LANES * CH], F32, "of%d" % c)
-            move(out_f32[c][:], result[c][:])
+            nc.scalar.copy(out_f32[c][:], result[c][:])
             nc.sync.dma_start(out_rows[:, :, c * CH : (c + 1) * CH], out_f32[c][:].rearrange("p (t j) -> p t j", t=LANES))
 
-        def interleave(move, dst, src):
-            move(dst.rearrange("p (j t) -> p j t", t=LANES), src[:].rearrange("p (t j) -> p j t", t=LANES))
+        def interleave_from_psum(dst, c):
+            nc.scalar.copy(dst.rearrange("p (j t) -> p j t", t=LANES), result[c][:].rearrange("p (t j) -> p j t", t=LANES))
 
-        def hand_on(h, src):
-            done = slice(h * HALF, (h + 1) * HALF)
-            nc.vector.quantize_mx(out=out_codes[:, done].bitcast(FP8X4), scales=out_scales[:, done], in_=src[:])
-            nc.sync.dma_start(out_words[:, done], out_codes[:, done].bitcast(I32))
+        def interleave_from_sbuf(dst, c):
+            nc.vector.tensor_copy(
+                dst.rearrange("p (g n t) -> p g t n", n=4, t=LANES), out_f32[c][:].rearrange("p (t g n) -> p g t n", t=LANES, n=4)
+            )
+
+        def quantise_out(c0, chunks, src):
+            cols = slice(c0 * CH, (c0 + chunks) * CH)
+            nc.vector.quantize_mx(out=out_codes[:, cols].bitcast(FP8X4), scales=out_scales[:, cols], in_=src[:])
+
+        def store_words(h):
+            nc.sync.dma_start(part(out_words, h, HALF), part(out_codes, h, HALF).bitcast(I32))
 
         for z in range(2):
             for t in HIGH:
                 first[(z, t)] = rows("first%d%d" % (z, t))
                 fetch(nc.scalar, first[(z, t)], mixed[(z, t, 0)][:].indirect(lists[0][:]))
-        add_second(0, 2, "high0")
-        add_second(2, 1, "high2")
-        round_low(0, 0, "pairs0")
-        round_low(1, 0, "pairs1")
-        place_low(0)
-        place_low(1)
-        round_low(2, 0, "pairs0")
-        round_low(3, 0, "pairs1")
-        place_low(2)
-        place_low(3)
+        hold_total(0, 2, "high0")
+        add_second(0, 2)
+        hold_total(2, 1, "high2")
+        add_second(2, 1)
+        for c0 in (0, 2):
+            for c in (c0, c0 + 1):
+                round_low(c)
+            for c in (c0, c0 + 1):
+                place_low(c)
         for c in range(2):
-            round_high(c, 0, 2)
+            round_high(c)
         for c in range(2):
             quantise_z(c)
             multiply(c)
-        add_second(LAST, 1, "z0", (0,))
-        round_high(2, 0, 2)
-        add_second(LAST, 1, None, (1,))
+        hold_total(LAST, 1, "z0")
+        add_second(LAST, 1, (0,))
+        round_high(2)
+        add_second(LAST, 1, (1,))
         quantise_z(2)
         multiply(2)
-        add_second(LAST, 1, None, (2, 3))
+        add_second(LAST, 1, (2, 3))
         for z in range(2):
-            round_high(LAST, z)
-        result[LAST] = bank(OUT_BANK[LAST])
+            round_high(LAST, slice(z, z + 1))
+        result[LAST] = bank(SUM_BANK[LAST])
         for z in range(2):
-            quantise_z(LAST, (z,))
+            quantise_z(LAST, slice(z, z + 1))
             for t in range(LANES):
                 out_pass(LAST, t, z, (z, t) == (0, 0), (z, t) == (1, LANES - 1))
-        early_bf = held([P, LANES * HALF], BF16, "zc1")
-        late_bf = held([P, LANES * HALF], BF16, "ob1")
+
         for c in range(2):
-            copy_out(c, nc.scalar.copy)
+            copy_out(c)
+        out_bf[0] = held([P, LANES * CH], BF16, "zc1")
+        interleave_from_psum(out_bf[0][:], 0)
+        for c in (2, LAST):
+            copy_out(c)
+        out_bf[1] = held([P, LANES * CH], BF16, "z0")
+        interleave_from_sbuf(out_bf[1][:], 1)
         for c in range(2):
-            interleave(nc.scalar.copy, part(early_bf, c, LANES * CH), result[c])
-        copy_out(2, nc.scalar.copy)
-        interleave(nc.scalar.copy, part(late_bf, 0, LANES * CH), result[2])
-        hand_on(0, early_bf)
-        copy_out(LAST, nc.vector.tensor_copy)
-        interleave(nc.vector.tensor_copy, part(late_bf, 1, LANES * CH), out_f32[LAST])
-        hand_on(1, late_bf)
+            quantise_out(c, 1, out_bf[c])
+        store_words(0)
+        late_bf = held([P, LANES * HALF], BF16, "zc3")
+        interleave_from_psum(part(late_bf, 0, LANES * CH), 2)
+        interleave_from_sbuf(part(late_bf, 1, LANES * CH), LAST)
+        quantise_out(2, 2, late_bf)
+        store_words(1)
 
         for q in range(4):
             queue = nc.sync if q % 2 == 0 else nc.scalar

from contextlib import ExitStack

import concourse.mybir as mybir
from concourse.masks import make_identity

T, S, N, H = 2048, 512, 512, 512
FLOPS = 4 * 2 * 512 * 512 * 512

F32 = mybir.dt.float32
BF16 = mybir.dt.bfloat16
I32 = mybir.dt.int32
U32 = mybir.dt.uint32
U16 = mybir.dt.uint16
U8 = mybir.dt.uint8
FP8X4 = mybir.dt.float8_e4m3fn_x4
FP4X4 = mybir.dt.float4_e2m1fn_x4
MULT = mybir.AluOpType.mult
ADD = mybir.AluOpType.add
SUBTRACT = mybir.AluOpType.subtract
COPY = mybir.ActivationFunctionType.Copy

P = 128
LANES = 4
LOW = (0, 1)
HIGH = (2, 3)
RE, IM = 0, 1
CH = 128
LAST = 3
HALF = S // 2
BANK = 512
TERMS_IN_BANK = 16
W4_ROWS = 4

PROJ_BANK = ((0, 1, 0, 1), (3, 2, 7, 6))
SUM_BANK = (2, 3, 4, 5)
BACK_BANK = (0, 1, 6, 7)


def tile_picked_beamf_none_po_kernel(
    tc, x_words, x_scales, w1, w2, wr1, wi1, wr2, wi2, w3_words, w3_scales, w4_words, w4_scales,
    offs, m1, m2, out_0, out_1, out_2,
):
    nc = tc.nc
    with ExitStack() as ctx:
        keep = ctx.enter_context(tc.tile_pool(name="keep", bufs=1))
        psum = ctx.enter_context(tc.psum_pool(name="psum", bufs=1))

        def held(shape, dtype, name):
            return keep.tile(shape, dtype, name=name, align_bytes=256)

        def rows(name, count=1):
            return held([P, count * S], F32, name)[:]

        def part(ap, n, width=S):
            return ap[:, n * width : (n + 1) * width]

        def bank(b):
            return psum.tile([P, BANK], F32, name="bank%d" % b)

        offs_t = keep.tile([P, S // 16], U16, name="offs_t")
        m1_t = keep.tile([P, S // 16], U16, name="m1_t")
        m2_t = keep.tile([P, S // 16], U16, name="m2_t")
        xw = held([P, T], I32, "xw")
        xs = held([P, T], U8, "xs")
        w34_words = [held([P, 2 * N], U8, "w3w"), held([P, 2 * N], U8, "w4w")]
        w34_scales = held([P, N], U8, "w34s")
        w4_dealt_scales = held([P, N], U8, "w4sd")
        raw = [held([P, LANES, H], F32, "raw%d" % i) for i in (RE, IM)]
        wr = [held([P, LANES], F32, "wr%d" % mic) for mic in range(2)]
        wi = [held([P, LANES], F32, "wi%d" % mic) for mic in range(2)]

        nc.gpsimd.memset(xs[:].bitcast(I32), 0)
        nc.vector.memset(w34_scales[:].bitcast(I32), 0)
        nc.vector.memset(w4_dealt_scales[:].bitcast(I32), 0)
        window = {}
        for i in (RE, IM):
            for t in LOW:
                window[(i, t)] = held([P, 2 * S], F32, "window%d%d" % (i, t))
                nc.vector.memset(window[(i, t)][:, S : 2 * S], 0.0)
        ident = held([P, P], F32, "ident")

        def load_weight(dst, src):
            nc.sync.dma_start(dst[:], src.rearrange("(p t) o -> p (t o)", t=LANES))

        def load_scale_rows(dst, src, base=0):
            for q in range(4):
                nc.sync.dma_start(dst[base + q : P : 32].bitcast(I32), src[0, q:16:4, :].bitcast(I32))

        w_rows = [w.rearrange("(p q) c -> p q c", q=LANES) for w in (w1, w2)]
        nc.sync.dma_start(raw[RE][:], w_rows[RE])
        nc.sync.dma_start(offs_t[:], offs)
        load_scale_rows(xs[:, :], x_scales)
        nc.sync.dma_start(xw[:], x_words[0].rearrange("p c r -> p (c r)").bitcast(I32))
        nc.sync.dma_start(w34_words[0][:].bitcast(I32), w3_words[0].bitcast(I32))
        nc.sync.dma_start(w34_words[1][:].bitcast(I32), w4_words[0].bitcast(I32))
        nc.sync.dma_start(m1_t[:], m1)
        nc.sync.dma_start(m2_t[:], m2)
        nc.sync.dma_start(raw[IM][:], w_rows[IM])
        load_weight(wi[0], wi1)
        load_weight(wi[1], wi2)
        load_weight(wr[0], wr1)
        load_weight(wr[1], wr2)
        make_identity(nc, ident[:])
        load_scale_rows(w34_scales[:, :], w3_scales)
        load_scale_rows(w34_scales[:, :], w4_scales, W4_ROWS)
        lists = (m1_t, m2_t)

        def offsets(mic, c, chunks):
            return lists[mic][:, c * CH // 16 : (c + chunks) * CH // 16]

        xg_words = held([P, S], U32, "xgw")
        xg_scales = held([P, S], U8, "xgs")
        nc.vector.tensor_copy(xg_scales[:], xs[:].indirect(offs_t[:]))

        grouped, w_codes, w_scales, proj, w34_dealt = {}, {}, {}, {}, {}

        def regroup(i, u, move, cols=slice(0, P)):
            move(
                grouped[(i, u)][:].rearrange("p (t c q) -> p c q t", t=2, q=LANES)[:, cols],
                raw[i][:].rearrange("p q (c t) -> p c q t", t=LANES)[:, cols, :, 2 * u : 2 * u + 2],
            )

        def quantise_w(i, u, name):
            w_codes[(i, u)] = held([P, 2 * P], U32, name)
            w_scales[(i, u)] = held([P, 2 * P], U8, "wsc%d%d" % (i, u))
            nc.vector.quantize_mx(out=w_codes[(i, u)][:].bitcast(FP8X4), scales=w_scales[(i, u)][:], in_=grouped[(i, u)][:])

        def project(i, t, frames=slice(0, S), into=None):
            u, e = divmod(t, 2)
            proj[(i, t)] = bank(PROJ_BANK[i][t] if into is None else into)
            nc.tensor.matmul_mx(
                out=proj[(i, t)][:, frames],
                lhsT=part(w_codes[(i, u)], e, P).bitcast(FP8X4), lhsT_scale=part(w_scales[(i, u)], e, P),
                rhs=xg_words[:, frames].bitcast(FP8X4), rhs_scale=xg_scales[:, frames], start=True, stop=True,
            )

        def fill(i, t, frames=slice(0, S), move=nc.scalar.copy):
            move(window[(i, t)][:, frames], proj[(i, t)][:, frames])

        for u in range(2):
            grouped[(RE, u)] = held([P, 2 * H], BF16, ("grouped0", "w4d")[u])
        regroup(RE, 0, nc.vector.tensor_copy, slice(0, P // 2))
        regroup(RE, 0, nc.scalar.copy, slice(P // 2, P))
        regroup(RE, 1, nc.scalar.copy)
        quantise_w(RE, 0, "wc00")
        w34_dealt[0] = held([P, 2 * N], U8, "w3d")
        nc.scalar.copy(
            w34_dealt[0][:].bitcast(U16).rearrange("p (t c) -> p t c", t=LANES),
            w34_words[0][:].bitcast(U16).rearrange("p (c t) -> p t c", t=LANES),
        )
        for h in range(2):
            frames = slice(h * HALF, (h + 1) * HALF)
            nc.vector.tensor_copy(xg_words[:, frames], xw[:].bitcast(U32).indirect(part(offs_t, h, HALF // 16)))
            if h == 1:
                quantise_w(RE, 1, "xw")
            for t in LOW:
                project(RE, t, frames, SUM_BANK[t] if h == 0 else None)
                fill(RE, t, frames, nc.vector.tensor_copy if (h, t) == (1, 0) else nc.scalar.copy)
        for t in HIGH:
            project(RE, t)
        w34_dealt[1] = held([P, 2 * N], U8, "w4d")
        nc.gpsimd.tensor_copy(
            w34_dealt[1][:].rearrange("p (t c e) -> p t c e", t=LANES, e=2),
            w34_words[1][:].rearrange("p (c t e) -> p t c e", t=LANES, e=2),
        )

        picked, both, cross, mixed, sums, added = {}, {}, {}, {}, {}, {}

        def hold_pair(t, mic, name):
            both[(t, mic)] = rows(name, 2)
            for i in (RE, IM):
                picked[(i, t, mic)] = part(both[(t, mic)], i)

        hold_pair(0, 0, "picked00")
        for t, mic in ((0, 1), (1, 0)):
            for i in (RE, IM):
                picked[(i, t, mic)] = rows("picked%d%d%d" % (i, t, mic))

        def fetch(engine, dst, src):
            if engine is nc.scalar:
                nc.scalar.activation(dst, src, COPY)
            else:
                nc.vector.tensor_copy(dst, src)

        def look_up(engine, i, t, mic):
            fetch(engine, picked[(i, t, mic)], window[(i, t)][:].indirect(lists[mic][:]))

        def cross_term(i, t, mic, dst=None):
            cross[(i, t, mic)] = rows("cross%d%d%d" % (i, t, mic)) if dst is None else dst
            nc.scalar.activation(cross[(i, t, mic)], proj[(i, t)][:], COPY, scale=wi[mic][:, t : t + 1])

        def add_terms(terms, t, zs):
            for c in range(LAST + 1):
                if c not in sums:
                    sums[c] = bank(SUM_BANK[c])
                    added[c] = 0
                for n, z in enumerate(zs):
                    nc.tensor.matmul(
                        part(sums[c], 2 * z + t, P), lhsT=part(part(terms, n), c, CH), rhs=ident[:], is_transpose=True,
                        start=(added[c] == 0), stop=(added[c] == TERMS_IN_BANK - 1),
                    )
                    added[c] += 1

        def weigh(engine, i, t, mic, zs, dst):
            src = both[(t, mic)] if i is None else picked[(i, t, mic)]
            if i is None or zs[0] == i:
                w = wr[mic][:, t : t + 1]
            elif i == RE:
                w = wi[mic][:, t : t + 1]
            else:
                w = part(minus_wi, mic, LANES)[:, t : t + 1]
            if engine is nc.gpsimd:
                nc.gpsimd.tensor_scalar(dst, src, w, 0.0, MULT, ADD)
            elif engine is nc.vector:
                nc.vector.tensor_scalar(dst, src, w, None, MULT)
            else:
                nc.scalar.activation(dst, src, COPY, scale=w)
            add_terms(dst, t, zs)

        minus_wi = held([P, 2 * LANES], F32, "minus_wi")
        for mic in range(2):
            nc.scalar.activation(part(minus_wi, mic, LANES), wi[mic][:], COPY, scale=-1.0)
        look_up(nc.vector, RE, 0, 0)
        look_up(nc.scalar, RE, 1, 0)
        look_up(nc.scalar, RE, 0, 1)
        for mic in range(2):
            cross_term(RE, 2, mic)
        for u in range(2):
            grouped[(IM, u)] = held([P, 2 * H], BF16, "grouped%d" % u)
            regroup(IM, u, nc.vector.tensor_copy)
        for u in range(2):
            quantise_w(IM, u, "wc1%d" % u)
        for t in LOW:
            project(IM, t)
            fill(IM, t)
        project(IM, 3)
        project(IM, 2)
        weigh(nc.vector, RE, 0, 0, (1,), rows("early0"))
        for z in (1, 0):
            weigh(nc.vector, RE, 1, 0, (z,), rows("early1%d" % z))
        hold_pair(1, 1, "raw1")
        look_up(nc.vector, RE, 1, 1)
        for t, mic in ((0, 0), (0, 1), (1, 0)):
            look_up(nc.vector, IM, t, mic)
        behind_im = rows("wc10", 2)
        for mic in range(2):
            cross_term(RE, 3, mic, part(behind_im, mic))
            cross_term(IM, 3, mic)
            cross_term(IM, 2, mic)

        aside = rows("picked010", 3)
        weigh(nc.gpsimd, RE, 0, 1, (1,), part(aside, 0))
        weigh(nc.gpsimd, RE, 0, 1, (0,), part(aside, 1))
        weigh(nc.gpsimd, RE, 1, 1, (1,), part(aside, 2))
        weigh(nc.gpsimd, None, 0, 0, (0, 1), rows("direct00", 2))
        weigh(nc.gpsimd, IM, 0, 0, (0,), rows("minus00"))
        for t, mic in ((0, 1), (1, 0)):
            for z in range(2):
                weigh(nc.gpsimd, IM, t, mic, (z,), rows("term%d%d%d" % (t, mic, z)))
        look_up(nc.scalar, IM, 1, 1)
        weigh(nc.scalar, IM, 1, 1, (0,), rows("minus11"))
        weigh(nc.gpsimd, None, 1, 1, (0, 1), rows("direct11", 2))

        def combine(z, t, mic):
            if mic == 0:
                mixed[(z, t, mic)] = window[(z, t - len(LOW))]
            else:
                mixed[(z, t, mic)] = held([P, S], F32, "mixed%d%d" % (z, t))
            nc.vector.scalar_tensor_tensor(
                mixed[(z, t, mic)][:, 0:S], proj[(z, t)][:], wr[mic][:, t : t + 1], cross[(1 - z, t, mic)],
                MULT, (SUBTRACT, ADD)[z],
            )

        for mic in range(2):
            for z in range(2):
                for t in HIGH:
                    combine(z, t, mic)

        both_dealt = held([P, N], U8, "cross131")
        nc.vector.tensor_copy(
            both_dealt[:].rearrange("p (t c) -> p t c", t=LANES), w34_scales[:].rearrange("p (c t) -> p t c", t=LANES)
        )
        for q in range(4):
            nc.sync.dma_start(w4_dealt_scales[q:P:32].bitcast(I32), both_dealt[W4_ROWS + q : P : 32].bitcast(I32))
        dealt_scales = (both_dealt, w4_dealt_scales)

        first, total, high, back, z_in = {}, {}, {}, {}, {}

        def hold_total(c0, chunks, name):
            total[c0] = held([P, 4 * chunks * CH], F32, name)
            for d in range(chunks):
                high[c0 + d] = total[c0][:].rearrange("p (z e j) -> p z j e", z=2, e=2)[:, :, d * CH : (d + 1) * CH]

        def add_second(c0, chunks, which=range(4)):
            n = chunks * CH
            for k in which:
                z, t = k // 2, HIGH[k % 2]
                nc.vector.tensor_tensor(
                    part(total[c0], k, n), mixed[(z, t, 1)][:].indirect(offsets(1, c0, chunks)),
                    first[(z, t)][:, c0 * CH : c0 * CH + n], ADD,
                )

        def round_low(c):
            pairs = held([P, H], BF16, "window1%d" % (c % 2))
            nc.scalar.copy(
                pairs[:].rearrange("j (z p e) -> j z p e", z=2, e=2),
                sums[c][:].rearrange("j (z e p) -> j z p e", z=2, e=2),
            )
            back[c] = bank(BACK_BANK[c])
            for z in range(2):
                nc.tensor.transpose(part(back[c], z, P), part(pairs[:].bitcast(F32), z, P), ident[:])

        def place_low(c):
            z_in[c] = held([P, 2 * H], BF16, "z%d" % c)
            nc.scalar.copy(
                z_in[c][:].bitcast(F32).rearrange("p (n u) -> p n u", u=2),
                back[c][:, 0 : 2 * P].unsqueeze(2).to_broadcast([P, 2 * P, 2]),
            )

        def round_high(c, zs=slice(0, 2)):
            dst = z_in[c][:].rearrange("p (z j t) -> p z j t", z=2, t=LANES)[:, zs, :, 2:4]
            nc.vector.tensor_copy(dst, high[c][:, zs])

        out_codes = held([P, S], U32, "oc")
        out_scales = held([P, S], U8, "osc")
        out_rows = out_0.rearrange("(p t) j -> p t j", t=LANES)
        out_words = out_1[0].rearrange("p c r -> p (c r)").bitcast(I32)
        z_codes, z_scales, result, out_f32, out_bf = {}, {}, {}, {}, {}

        def quantise_z(c, zs=slice(0, 2)):
            if zs.start == 0:
                z_codes[c] = held([P, 2 * CH], U32, "zc%d" % c)
                z_scales[c] = held([P, 2 * CH], U8, "zs%d" % c)
            cols = slice(zs.start * CH, zs.stop * CH)
            nc.vector.quantize_mx(
                out=z_codes[c][:, cols].bitcast(FP8X4), scales=z_scales[c][:, cols], in_=z_in[c][:, zs.start * H : zs.stop * H]
            )

        def out_pass(c, t, z, start, stop):
            nc.tensor.matmul_mx(
                out=part(result[c], t, CH),
                lhsT=part(w34_dealt[z], t, 2 * P).bitcast(FP4X4), lhsT_scale=part(dealt_scales[z], t, P),
                rhs=part(z_codes[c], z, CH).bitcast(FP8X4), rhs_scale=part(z_scales[c], z, CH),
                start=start, stop=stop,
            )

        def multiply(c):
            result[c] = bank(SUM_BANK[c])
            for t in range(LANES):
                for z in range(2):
                    out_pass(c, t, z, z == 0, z == 1)

        def copy_out(c):
            out_f32[c] = held([P, LANES * CH], F32, "of%d" % c)
            nc.scalar.copy(out_f32[c][:], result[c][:])
            nc.sync.dma_start(out_rows[:, :, c * CH : (c + 1) * CH], out_f32[c][:].rearrange("p (t j) -> p t j", t=LANES))

        def interleave_from_psum(dst, c):
            nc.scalar.copy(dst.rearrange("p (j t) -> p j t", t=LANES), result[c][:].rearrange("p (t j) -> p j t", t=LANES))

        def interleave_from_sbuf(dst, c):
            nc.vector.tensor_copy(
                dst.rearrange("p (g n t) -> p g t n", n=4, t=LANES), out_f32[c][:].rearrange("p (t g n) -> p g t n", t=LANES, n=4)
            )

        def quantise_out(c0, chunks, src):
            cols = slice(c0 * CH, (c0 + chunks) * CH)
            nc.vector.quantize_mx(out=out_codes[:, cols].bitcast(FP8X4), scales=out_scales[:, cols], in_=src[:])

        def store_words(h):
            nc.sync.dma_start(part(out_words, h, HALF), part(out_codes, h, HALF).bitcast(I32))

        for z in range(2):
            for t in HIGH:
                first[(z, t)] = rows("first%d%d" % (z, t))
                fetch(nc.scalar, first[(z, t)], mixed[(z, t, 0)][:].indirect(lists[0][:]))
        hold_total(0, 2, "high0")
        add_second(0, 2)
        hold_total(2, 1, "high2")
        add_second(2, 1)
        for c0 in (0, 2):
            for c in (c0, c0 + 1):
                round_low(c)
            for c in (c0, c0 + 1):
                place_low(c)
        for c in range(2):
            round_high(c)
        for c in range(2):
            quantise_z(c)
            multiply(c)
        hold_total(LAST, 1, "z0")
        add_second(LAST, 1, (0,))
        round_high(2)
        add_second(LAST, 1, (1,))
        quantise_z(2)
        multiply(2)
        add_second(LAST, 1, (2, 3))
        for z in range(2):
            round_high(LAST, slice(z, z + 1))
        result[LAST] = bank(SUM_BANK[LAST])
        for z in range(2):
            quantise_z(LAST, slice(z, z + 1))
            for t in range(LANES):
                out_pass(LAST, t, z, (z, t) == (0, 0), (z, t) == (1, LANES - 1))

        for c in range(2):
            copy_out(c)
        out_bf[0] = held([P, LANES * CH], BF16, "zc1")
        interleave_from_psum(out_bf[0][:], 0)
        for c in (2, LAST):
            copy_out(c)
        out_bf[1] = held([P, LANES * CH], BF16, "z0")
        interleave_from_sbuf(out_bf[1][:], 1)
        for c in range(2):
            quantise_out(c, 1, out_bf[c])
        store_words(0)
        late_bf = held([P, LANES * HALF], BF16, "zc3")
        interleave_from_psum(part(late_bf, 0, LANES * CH), 2)
        interleave_from_sbuf(part(late_bf, 1, LANES * CH), LAST)
        quantise_out(2, 2, late_bf)
        store_words(1)

        for q in range(4):
            queue = nc.sync if q % 2 == 0 else nc.scalar
            queue.dma_start(out_2[0, 4 * q : 4 * q + 4, :].bitcast(I32), out_scales[32 * q : 32 * q + 4, :].bitcast(I32))
